import numpy as np
import ml_dtypes


def mxq(x, axis, fmt="e4m3"):
    dtype, down = {"e4m3": (ml_dtypes.float8_e4m3fn, 7), "e5m2": (ml_dtypes.float8_e5m2, 14)}[fmt]
    v = np.moveaxis(np.asarray(x, np.float32).astype(ml_dtypes.bfloat16).astype(np.float64), axis, -1)
    blocks = v.reshape(v.shape[:-1] + (-1, 32))
    amax = np.abs(blocks).max(-1, keepdims=True)
    byte = np.maximum(np.where(amax > 0, np.frexp(amax)[1] - 1 + 127, 0) - down, 1)
    scale = np.exp2(byte - 127.0)
    codes = (blocks / scale).astype(np.float32).astype(dtype).astype(np.float64)
    return np.moveaxis((codes * scale).reshape(v.shape), -1, axis)


WIDE = False


def mx_kscale(k):
    if not WIDE:
        return np.ones(k)
    levels = np.array([10, -10, 5, -5, 0])
    if k % 512:
        return np.exp2(np.random.permutation(np.resize(levels, k // 32))).repeat(32)
    a = np.empty((k // 512, 16))
    for p in range(k // 512):
        a[p, :8] = np.random.permutation(np.resize(levels, 8))
        for g in range(8):
            far = levels[np.abs(levels - a[p, g]) >= 10]
            a[p, g + 8] = far[np.random.randint(len(far))]
    return np.exp2(a.ravel()).repeat(32)


def f64(x):
    return np.asarray(x).astype(np.float64)


def striped(idx):
    return np.tile(idx.reshape(-1, 16).T, (8, 1)).astype(np.uint16)


def unstriped(offs):
    return offs[:16].T.reshape(-1).astype(np.int64)


E2M1 = np.array([0.0, 0.5, 1.0, 1.5, 2.0, 3.0, 4.0, 6.0, -0.0, -0.5, -1.0, -1.5, -2.0, -3.0, -4.0, -6.0])


def pack_weight(w, fmt):
    k, n = w.shape
    w = f64(np.asarray(w, np.float32).astype(ml_dtypes.bfloat16)).reshape(k // 32, 32, n)
    amax = np.abs(w).max(1)
    if fmt == "e4m3":
        byte = np.frexp(amax)[1] - 1 + 127 - 7
    else:
        mant, ex = np.frexp(amax / 6.0)
        byte = np.where(mant > 0.5, ex, ex - 1) + 127
    byte = np.clip(np.where(amax > 0, byte, 1), 1, 254)
    scaled = (w * np.exp2(127.0 - byte)[:, None, :]).reshape(k, n).astype(np.float32)
    by_word = np.ascontiguousarray(scaled.reshape(k // 512, 128, 4, n).transpose(0, 1, 3, 2))
    if fmt == "e4m3":
        words = by_word.astype(ml_dtypes.float8_e4m3fn).view(np.uint8)
    else:
        c = by_word.astype(ml_dtypes.float4_e2m1fn).view(np.uint8) & 0xF
        words = (c[..., 0::2] | (c[..., 1::2] << 4)).reshape(k // 512, 128, 2 * n)
    return np.ascontiguousarray(words), np.ascontiguousarray(byte.astype(np.uint8).reshape(k // 512, 16, n))


def unpack_weight(words, scales, fmt):
    g, _, n = scales.shape
    words = np.ascontiguousarray(words).reshape(g, 128, n, -1)
    if fmt == "e4m3":
        vals = words.view(ml_dtypes.float8_e4m3fn).astype(np.float64)
    else:
        nib = np.empty((g, 128, n, 4), np.uint8)
        nib[..., 0::2] = words & 0xF
        nib[..., 1::2] = words >> 4
        vals = E2M1[nib]
    vals = vals * np.repeat(np.exp2(scales.astype(np.float64) - 127.0), 8, axis=1)[..., None]
    return vals.transpose(0, 1, 3, 2).reshape(g * 512, n)


def gelu(v):
    return 0.5 * v * (1.0 + np.tanh(np.sqrt(2.0 / np.pi) * (v + 0.044715 * v**3)))


K, T, E, C, N = 2048, 1024, 12, 256, 128
TOP = 3


def by_expert(wq, xq):
    return np.concatenate([wq[e].T @ xq[:, e * C:(e + 1) * C] for e in range(E)], axis=1)


def setup_inputs():
    n = np.random.standard_normal
    s = mx_kscale(K)[:, None]
    deal = np.repeat(np.arange(E), C).reshape(TOP, T)[:, np.random.permutation(T)]
    deal = np.take_along_axis(deal, np.argsort(np.random.rand(TOP, T), axis=0), axis=0)
    for _ in range(8):
        s_, t_ = np.random.permutation(T).reshape(2, -1); r = np.random.randint(TOP, size=T // 2); x, y = deal[r, s_].copy(), deal[r, t_].copy()
        ok = ~((deal[:, s_] == y).any(0) | (deal[:, t_] == x).any(0)); deal[r[ok], s_[ok]] = y[ok]; deal[r[ok], t_[ok]] = x[ok]
    order = np.lexsort((np.random.rand(TOP * T), deal.reshape(-1)))
    slot_token = order % T; pos = np.empty(TOP * T, np.int64); pos[order] = np.arange(TOP * T); pos = pos.reshape(TOP, T)
    g = np.random.uniform(0.5, 1.5, (TOP, T)); g = g / g.sum(0)
    w = [pack_weight(m, "e2m1") for m in n((E, K, N)) / np.sqrt(K) / s[None]]
    return {
        "xT": (n((K, T)) * s).astype(np.float32),
        "w_words": np.stack([m[0] for m in w]),
        "w_scales": np.stack([m[1] for m in w]),
        "b": (0.3 * n((N, E))).astype(np.float32),
        "gate": np.stack([np.tile(r, (N, 1)) for r in g]).astype(np.float32),
        "offs": striped(slot_token),
        "pos1": striped(pos[0]),
        "pos2": striped(pos[1]),
        "pos3": striped(pos[2]),
    }


def reference(xT, w_words, w_scales, b, gate, offs, pos1, pos2, pos3):
    idx = unstriped(offs)
    w = np.stack([unpack_weight(w_words[e], w_scales[e], "e2m1") for e in range(E)])
    xq = mxq(f64(xT)[:, idx], 0, "e4m3")
    y = by_expert(w, xq)
    y = gelu(y + np.repeat(f64(b), C, axis=1))
    return sum(f64(gate[r]) * y[:, unstriped(p)] for r, p in enumerate((pos1, pos2, pos3)))

@@ -1,0 +1,216 @@
+from contextlib import ExitStack
+
+import concourse.mybir as mybir
+
+K, T, E, C, N = 2048, 1024, 12, 256, 128
+TOP = 3
+S = E * C
+P = 128
+PACK = 4
+K_PASS = P * PACK
+PASSES = K // K_PASS
+FLOPS = 2 * K * N * S
+
+F32 = mybir.dt.float32
+BF16 = mybir.dt.bfloat16
+I32 = mybir.dt.int32
+U32 = mybir.dt.uint32
+U16 = mybir.dt.uint16
+U8 = mybir.dt.uint8
+FP8X4 = mybir.dt.float8_e4m3fn_x4
+FP4X4 = mybir.dt.float4_e2m1fn_x4
+AF = mybir.ActivationFunctionType
+MULT = mybir.AluOpType.mult
+ADD = mybir.AluOpType.add
+
+GROUP = 128
+LIST = 16
+
+
+def tile_moe_tk_lin_gelu_kernel(tc, xT, w_words, w_scales, b, gate, offs, pos1, pos2, pos3, out):
+    nc = tc.nc
+    with ExitStack() as ctx:
+        keep = ctx.enter_context(tc.tile_pool(name="keep", bufs=1))
+        raws = ctx.enter_context(tc.tile_pool(name="raws", bufs=1))
+        stage = ctx.enter_context(tc.tile_pool(name="stage", bufs=7))
+        prods = ctx.enter_context(tc.tile_pool(name="prods", bufs=1))
+        psum = ctx.enter_context(tc.psum_pool(name="psum", bufs=8))
+
+        offs_t = keep.tile([P, S // LIST], U16, name="offs_t")
+        pos_t = [keep.tile([P, T // LIST], U16, name="pos%d_t" % r) for r in range(TOP)]
+        x_scales = keep.tile([P, T], U8, name="x_scales", align_bytes=64)
+        first_codes = keep.tile([P, T], U32, name="first_codes", align_bytes=64)
+        late_codes = keep.tile([P, 3 * T], I32, name="late_codes", align_bytes=64)
+        start = {1: T, 2: 0, 3: 2 * T}
+        slot_codes = [keep.tile([P, S], U32, name="slot_codes%d" % a, align_bytes=64) for a in range(PASSES)]
+        slot_scales = [keep.tile([P, S], U8, name="slot_scales%d" % a, align_bytes=64) for a in range(PASSES)]
+        w_codes = keep.tile([P, E * PASSES, 2 * N], U8, name="w_codes", align_bytes=64)
+        w_planes = keep.tile([P, E * PASSES, N], U8, name="w_planes", align_bytes=64)
+        b_t = keep.tile([P, E], F32, name="b_t")
+        gate_t = [keep.tile([P, T], F32, name="gate%d" % r) for r in range(TOP)]
+        y = keep.tile([P, S], F32, name="y")
+        warm = keep.tile([P, 1], F32, name="warm")
+        warm_out = keep.tile([P, 1], F32, name="warm_out")
+
+        nc.vector.memset(warm[:], 0.0)
+        nc.vector.memset(late_codes[:, 2 * T:], 0)
+        nc.scalar.activation(out=warm_out[:], in_=warm[:], func=AF.Gelu_apprx_tanh)
+        nc.gpsimd.memset(x_scales[:].bitcast(I32), 0)
+        nc.gpsimd.memset(w_planes[:].rearrange("p g n -> p (g n)").bitcast(I32), 0)
+        for a in range(1, PASSES):
+            nc.vector.memset(slot_scales[a][:].bitcast(I32), 0)
+
+        def load_x(a, c0, width):
+            raw = raws.tile([P, PACK, width], F32, name="raw%d_%d" % (a, c0))
+            rows = xT[a * K_PASS:(a + 1) * K_PASS, c0:c0 + width]
+            nc.sync.dma_start(raw[:], rows.rearrange("(p j) w -> p j w", j=PACK))
+            return raw
+
+        pieces = {}
+
+        def load_pass(a, widths):
+            c0 = 0
+            for width in widths:
+                pieces[(a, c0)] = (load_x(a, c0, width), width)
+                c0 += width
+
+        def load_w(e0, e1):
+            nc.sync.dma_start(
+                w_codes[:, e0 * PASSES:e1 * PASSES, :].bitcast(I32),
+                w_words[e0:e1].rearrange("e a p n -> p (e a) n").bitcast(I32),
+            )
+
+        load_pass(0, (256, 256, 256, 128, 128))
+        nc.sync.dma_start(offs_t[:], offs)
+        load_pass(1, (512, 512))
+        load_pass(2, (512, 512))
+        load_pass(3, (512, 256, 256))
+        for r in range(4):
+            nc.sync.dma_start(
+                w_planes[r:P:32, :, :].bitcast(I32),
+                w_scales.rearrange("e a (q r) n -> r q (e a) n", r=4)[r].bitcast(I32),
+            )
+        for e0 in range(0, E, 3):
+            load_w(e0, e0 + 3)
+        nc.sync.dma_start(b_t[:], b)
+
+        def quantize(a, key, lo, hi, on_vector):
+            raw = pieces[(a, key)][0]
+            width = hi - lo
+            grouped = stage.tile([P, width, PACK], BF16, name="grouped", align_bytes=64)
+            src = raw[:, :, lo - key:hi - key].rearrange("p j (c i) -> p c j i", i=4)
+            dst = grouped[:].rearrange("p (c i) j -> p c j i", i=4)
+            if on_vector:
+                nc.vector.tensor_copy(out=dst, in_=src)
+            else:
+                nc.scalar.copy(out=dst, in_=src)
+            return lambda: nc.vector.quantize_mx(
+                out=(first_codes[:, lo:hi] if a == 0 else late_codes[:, start[a] + lo:start[a] + hi]).bitcast(FP8X4),
+                scales=x_scales[4 * a:P, lo:hi],
+                in_=grouped[:].rearrange("p w j -> p (w j)"),
+            )
+
+        def gather_codes(a, s0, n):
+            nc.vector.tensor_copy(
+                out=slot_codes[a][:, s0:s0 + n],
+                in_=(first_codes[:] if a == 0 else late_codes[:, start[a]:].bitcast(U32)).indirect(offs_t[:, s0 // LIST:(s0 + n) // LIST]),
+            )
+
+        def gather_scales(s0, n):
+            nc.vector.tensor_copy(
+                out=slot_scales[0][:, s0:s0 + n],
+                in_=x_scales[:].indirect(offs_t[:, s0 // LIST:(s0 + n) // LIST]),
+            )
+
+        def gather_and_move_scales(s0, s1):
+            for lo in range(s0, s1, 768):
+                gather_scales(lo, 768)
+            for a in range(1, PASSES):
+                nc.sync.dma_start(
+                    slot_scales[a][0:112, s0:s1].bitcast(I32),
+                    slot_scales[0][4 * a:4 * a + 112, s0:s1].bitcast(I32),
+                )
+
+        waiting = None
+        for c0, width in ((0, 256), (256, 256), (512, 256), (768, 128), (896, 128)):
+            ready = quantize(0, c0, c0, c0 + width, True)
+            if waiting:
+                waiting()
+            waiting = ready
+        waiting()
+        for s0 in (0, 768, 1536):
+            gather_codes(0, s0, 768)
+        for c0 in (0, 512):
+            quantize(1, c0, c0, c0 + 512, False)()
+        gather_codes(0, 2304, 768)
+        for s0 in (0, 768, 1536):
+            gather_codes(1, s0, 768)
+        for c0 in (0, 512):
+            quantize(2, c0, c0, c0 + 512, False)()
+        gather_codes(1, 2304, 768)
+        for c0, width in ((0, 512), (512, 256), (768, 256)):
+            quantize(3, c0, c0, c0 + width, False)()
+        gather_and_move_scales(0, 1536)
+        gather_and_move_scales(1536, S)
+        for r, pos in enumerate((pos1, pos2, pos3)):
+            nc.sync.dma_start(pos_t[r][:], pos)
+            nc.sync.dma_start(gate_t[r][:], gate[r])
+
+        acc = {}
+
+        def multiply(g, a):
+            s0, e = g * GROUP, g * GROUP // C
+            if a == 0:
+                acc[g] = psum.tile([P, GROUP], F32, name="acc")
+            nc.tensor.matmul_mx(
+                out=acc[g][:],
+                lhsT=w_codes[:, e * PASSES + a, :].bitcast(FP4X4),
+                lhsT_scale=w_planes[:, e * PASSES + a, :],
+                rhs=slot_codes[a][:, s0:s0 + GROUP].bitcast(FP8X4),
+                rhs_scale=slot_scales[a][:, s0:s0 + GROUP],
+                start=(a == 0),
+                stop=(a == PASSES - 1),
+            )
+
+        def open_groups(s0, s1):
+            for a in range(PASSES - 1):
+                for g in range(s0 // GROUP, s1 // GROUP):
+                    multiply(g, a)
+
+        def close_groups(s0, s1):
+            for g in range(s0 // GROUP, s1 // GROUP):
+                multiply(g, PASSES - 1)
+                e = g * GROUP // C
+                nc.scalar.activation(
+                    out=y[:, g * GROUP:(g + 1) * GROUP], in_=acc[g][:],
+                    func=AF.Gelu_apprx_tanh, bias=b_t[:, e:e + 1],
+                )
+
+        for s0 in range(0, S, 768):
+            gather_codes(2, s0, 768)
+            open_groups(s0, s0 + 768)
+            sizes = (768,) if s0 + 768 < S else (384, 256, 128)
+            lo = s0
+            for n in sizes:
+                gather_codes(3, lo, n)
+                close_groups(lo, lo + n)
+                lo += n
+
+        prod = [prods.tile([P, T], F32, name="prod%d" % r) for r in range(TOP)]
+
+        def pick(r, t0, t1):
+            nc.vector.tensor_tensor(
+                prod[r][:, t0:t1], y[:].indirect(pos_t[r][:, t0 // LIST:t1 // LIST]), gate_t[r][:, t0:t1], MULT,
+            )
+
+        def add(r, t0, t1):
+            nc.vector.tensor_tensor(prod[0][:, t0:t1], prod[0][:, t0:t1], prod[r][:, t0:t1], ADD)
+
+        pick(0, 0, T)
+        pick(1, 0, T)
+        pick(2, 0, 576)
+        add(1, 0, T)
+        pick(2, 576, T)
+        for t0, t1 in ((0, 576), (576, 800), (800, T)):
+            add(2, t0, t1)
+            nc.sync.dma_start(out[:, t0:t1], prod[0][:, t0:t1])

@@ -1,6 +1,7 @@
 from contextlib import ExitStack
 
 import concourse.mybir as mybir
+from concourse.masks import make_identity
 
 K, T, E, C, N = 2048, 1024, 12, 256, 128
 TOP = 3
@@ -38,10 +39,9 @@ def tile_moe_tk_lin_gelu_kernel(tc, xT, w_words, w_scales, b, gate, offs, pos1, 
 
         offs_t = keep.tile([P, S // LIST], U16, name="offs_t")
         pos_t = [keep.tile([P, T // LIST], U16, name="pos%d_t" % r) for r in range(TOP)]
-        x_scales = keep.tile([P, T], U8, name="x_scales", align_bytes=64)
-        first_codes = keep.tile([P, T], U32, name="first_codes", align_bytes=64)
-        late_codes = keep.tile([P, 3 * T], I32, name="late_codes", align_bytes=64)
-        start = {1: T, 2: 0, 3: 2 * T}
+        x_scales = keep.tile([P, 2 * T], U8, name="x_scales", align_bytes=64)
+        codes = keep.tile([P, 5 * T], I32, name="codes", align_bytes=64)
+        start = {2: 0, 3: T, 1: 2 * T, 0: 3 * T}
         slot_codes = [keep.tile([P, S], U32, name="slot_codes%d" % a, align_bytes=64) for a in range(PASSES)]
         slot_scales = [keep.tile([P, S], U8, name="slot_scales%d" % a, align_bytes=64) for a in range(PASSES)]
         w_codes = keep.tile([P, E * PASSES, 2 * N], U8, name="w_codes", align_bytes=64)
@@ -52,13 +52,13 @@ def tile_moe_tk_lin_gelu_kernel(tc, xT, w_words, w_scales, b, gate, offs, pos1, 
         warm = keep.tile([P, 1], F32, name="warm")
         warm_out = keep.tile([P, 1], F32, name="warm_out")
 
+        ident = keep.tile([P, P], F32, name="ident")
+        make_identity(nc, ident[:])
         nc.vector.memset(warm[:], 0.0)
-        nc.vector.memset(late_codes[:, 2 * T:], 0)
         nc.scalar.activation(out=warm_out[:], in_=warm[:], func=AF.Gelu_apprx_tanh)
-        nc.gpsimd.memset(x_scales[:].bitcast(I32), 0)
-        nc.gpsimd.memset(w_planes[:].rearrange("p g n -> p (g n)").bitcast(I32), 0)
-        for a in range(1, PASSES):
-            nc.vector.memset(slot_scales[a][:].bitcast(I32), 0)
+        nc.vector.memset(x_scales[:].bitcast(I32), 0)
+        nc.vector.memset(codes[:, 4 * T:], 0)
+        nc.vector.memset(w_planes[:].rearrange("p g n -> p (g n)").bitcast(I32), 0)
 
         def load_x(a, c0, width):
             raw = raws.tile([P, PACK, width], F32, name="raw%d_%d" % (a, c0))
@@ -98,14 +98,15 @@ def tile_moe_tk_lin_gelu_kernel(tc, xT, w_words, w_scales, b, gate, offs, pos1, 
             raw = pieces[(a, key)][0]
             width = hi - lo
             grouped = stage.tile([P, width, PACK], BF16, name="grouped", align_bytes=64)
-            src = raw[:, :, lo - key:hi - key].rearrange("p j (c i) -> p c j i", i=4)
-            dst = grouped[:].rearrange("p (c i) j -> p c j i", i=4)
-            if on_vector:
-                nc.vector.tensor_copy(out=dst, in_=src)
-            else:
-                nc.scalar.copy(out=dst, in_=src)
+            cut = width // 2 if on_vector else 0
+            for c0, c1, copy in ((0, cut, nc.vector.tensor_copy), (cut, width, nc.scalar.copy)):
+                if c1 > c0:
+                    copy(
+                        out=grouped[:, c0:c1, :].rearrange("p (c i) j -> p c j i", i=4),
+                        in_=raw[:, :, lo - key + c0:lo - key + c1].rearrange("p j (c i) -> p c j i", i=4),
+                    )
             return lambda: nc.vector.quantize_mx(
-                out=(first_codes[:, lo:hi] if a == 0 else late_codes[:, start[a] + lo:start[a] + hi]).bitcast(FP8X4),
+                out=codes[:, start[a] + lo:start[a] + hi].bitcast(FP8X4),
                 scales=x_scales[4 * a:P, lo:hi],
                 in_=grouped[:].rearrange("p w j -> p (w j)"),
             )
@@ -113,7 +114,7 @@ def tile_moe_tk_lin_gelu_kernel(tc, xT, w_words, w_scales, b, gate, offs, pos1, 
         def gather_codes(a, s0, n):
             nc.vector.tensor_copy(
                 out=slot_codes[a][:, s0:s0 + n],
-                in_=(first_codes[:] if a == 0 else late_codes[:, start[a]:].bitcast(U32)).indirect(offs_t[:, s0 // LIST:(s0 + n) // LIST]),
+                in_=codes[:, start[a]:start[a] + (T if a == 3 else 2 * T)].bitcast(U32).indirect(offs_t[:, s0 // LIST:(s0 + n) // LIST]),
             )
 
         def gather_scales(s0, n):
@@ -123,12 +124,16 @@ def tile_moe_tk_lin_gelu_kernel(tc, xT, w_words, w_scales, b, gate, offs, pos1, 
             )
 
         def gather_and_move_scales(s0, s1):
-            for lo in range(s0, s1, 768):
-                gather_scales(lo, 768)
+            gather_scales(s0, s1 - s0)
             for a in range(1, PASSES):
                 nc.sync.dma_start(
                     slot_scales[a][0:112, s0:s1].bitcast(I32),
                     slot_scales[0][4 * a:4 * a + 112, s0:s1].bitcast(I32),
+                )
+            for a in range(1, PASSES):
+                nc.sync.dma_start(
+                    slot_scales[a][112:P, s0:s1].bitcast(I32),
+                    slot_scales[0][112:P, s0:s1].bitcast(I32),
                 )
 
         waiting = None
@@ -138,16 +143,14 @@ def tile_moe_tk_lin_gelu_kernel(tc, xT, w_words, w_scales, b, gate, offs, pos1, 
                 waiting()
             waiting = ready
         waiting()
-        for s0 in (0, 768, 1536):
-            gather_codes(0, s0, 768)
+        for s0 in (0, 1536):
+            gather_codes(0, s0, 1536)
         for c0 in (0, 512):
             quantize(1, c0, c0, c0 + 512, False)()
-        gather_codes(0, 2304, 768)
-        for s0 in (0, 768, 1536):
-            gather_codes(1, s0, 768)
+        for s0 in (0, 1536):
+            gather_codes(1, s0, 1536)
         for c0 in (0, 512):
             quantize(2, c0, c0, c0 + 512, False)()
-        gather_codes(1, 2304, 768)
         for c0, width in ((0, 512), (512, 256), (768, 256)):
             quantize(3, c0, c0, c0 + width, False)()
         gather_and_move_scales(0, 1536)
@@ -203,14 +206,28 @@ def tile_moe_tk_lin_gelu_kernel(tc, xT, w_words, w_scales, b, gate, offs, pos1, 
                 prod[r][:, t0:t1], y[:].indirect(pos_t[r][:, t0 // LIST:t1 // LIST]), gate_t[r][:, t0:t1], MULT,
             )
 
-        def add(r, t0, t1):
-            nc.vector.tensor_tensor(prod[0][:, t0:t1], prod[0][:, t0:t1], prod[r][:, t0:t1], ADD)
-
+        blocks = T // P
+        turned = prods.tile([P, T], F32, name="turned")
+        result = prods.tile([P, T], F32, name="result")
         pick(0, 0, T)
-        pick(1, 0, T)
-        pick(2, 0, 576)
-        add(1, 0, T)
-        pick(2, 576, T)
-        for t0, t1 in ((0, 576), (576, 800), (800, T)):
-            add(2, t0, t1)
-            nc.sync.dma_start(out[:, t0:t1], prod[0][:, t0:t1])
+        pick(1, 0, T // 2)
+        pick(1, T // 2, T)
+        sums = []
+        for blk in range(blocks):
+            sums.append(psum.tile([P, P], F32, name="acc"))
+            nc.tensor.matmul(sums[blk][:], lhsT=prod[0][:, blk * P:(blk + 1) * P], rhs=ident[:], is_transpose=True, start=True, stop=False)
+        back = []
+        for half in range(2):
+            mine = range(half * blocks // 2, (half + 1) * blocks // 2)
+            for blk in mine:
+                nc.tensor.matmul(sums[blk][:], lhsT=prod[1][:, blk * P:(blk + 1) * P], rhs=ident[:], is_transpose=True, start=False, stop=True)
+                nc.scalar.copy(out=turned[:, blk * P:(blk + 1) * P], in_=sums[blk][:])
+            back.append(psum.tile([P, T // 2], F32, name="acc"))
+            for i, blk in enumerate(mine):
+                nc.tensor.transpose(back[half][:, i * P:(i + 1) * P], turned[:, blk * P:(blk + 1) * P], ident[:])
+        pick(2, 0, T // 2)
+        pick(2, T // 2, T)
+        for t0, t1 in ((0, 512), (512, 832), (832, T)):
+            half = t0 // (T // 2)
+            nc.vector.tensor_tensor(result[:, t0:t1], back[half][:, t0 - half * T // 2:t1 - half * T // 2], prod[2][:, t0:t1], ADD)
+            nc.sync.dma_start(out[:, t0:t1], result[:, t0:t1])

@@ -26,6 +26,9 @@ ADD = mybir.AluOpType.add
 
 GROUP = 128
 LIST = 16
+CHUNK = 1024
+CHUNKS = S // CHUNK
+WIDE = 1408
 
 
 def tile_moe_tk_lin_gelu_kernel(tc, xT, w_words, w_scales, b, gate, offs, pos1, pos2, pos3, out):
@@ -39,15 +42,14 @@ def tile_moe_tk_lin_gelu_kernel(tc, xT, w_words, w_scales, b, gate, offs, pos1, 
 
         offs_t = keep.tile([P, S // LIST], U16, name="offs_t")
         pos_t = [keep.tile([P, T // LIST], U16, name="pos%d_t" % r) for r in range(TOP)]
-        x_scales = keep.tile([P, 2 * T], U8, name="x_scales", align_bytes=64)
-        codes = keep.tile([P, 5 * T], I32, name="codes", align_bytes=64)
-        start = {2: 0, 3: T, 1: 2 * T, 0: 3 * T}
+        x_scales = keep.tile([P, WIDE], U8, name="x_scales", align_bytes=64)
+        codes = keep.tile([P, 3 * T + WIDE], I32, name="codes", align_bytes=64)
+        start = {2: 0, 1: T, 0: 2 * T, 3: 3 * T}
         slot_codes = [keep.tile([P, S], U32, name="slot_codes%d" % a, align_bytes=64) for a in range(PASSES)]
-        slot_scales = [keep.tile([P, S], U8, name="slot_scales%d" % a, align_bytes=64) for a in range(PASSES)]
+        slot_scales = [[keep.tile([P, CHUNK], U8, name="slot_scales%d_%d" % (a, h), tag="planes%d_%d" % (a, h), align_bytes=64) for h in range(CHUNKS)] for a in range(PASSES)]
         w_codes = keep.tile([P, E * PASSES, 2 * N], U8, name="w_codes", align_bytes=64)
         w_planes = keep.tile([P, E * PASSES, N], U8, name="w_planes", align_bytes=64)
         b_t = keep.tile([P, E], F32, name="b_t")
-        gate_t = [keep.tile([P, T], F32, name="gate%d" % r) for r in range(TOP)]
         y = keep.tile([P, S], F32, name="y")
         warm = keep.tile([P, 1], F32, name="warm")
         warm_out = keep.tile([P, 1], F32, name="warm_out")
@@ -57,7 +59,7 @@ def tile_moe_tk_lin_gelu_kernel(tc, xT, w_words, w_scales, b, gate, offs, pos1, 
         nc.vector.memset(warm[:], 0.0)
         nc.scalar.activation(out=warm_out[:], in_=warm[:], func=AF.Gelu_apprx_tanh)
         nc.vector.memset(x_scales[:].bitcast(I32), 0)
-        nc.vector.memset(codes[:, 4 * T:], 0)
+        nc.vector.memset(codes[:, 3 * T:], 0)
         nc.vector.memset(w_planes[:].rearrange("p g n -> p (g n)").bitcast(I32), 0)
 
         def load_x(a, c0, width):
@@ -82,7 +84,7 @@ def tile_moe_tk_lin_gelu_kernel(tc, xT, w_words, w_scales, b, gate, offs, pos1, 
 
         load_pass(0, (256, 256, 256, 128, 128))
         nc.sync.dma_start(offs_t[:], offs)
-        load_pass(1, (512, 512))
+        load_pass(1, (256, 256, 512))
         load_pass(2, (512, 512))
         load_pass(3, (512, 256, 256))
         for r in range(4):
@@ -90,74 +92,66 @@ def tile_moe_tk_lin_gelu_kernel(tc, xT, w_words, w_scales, b, gate, offs, pos1, 
                 w_planes[r:P:32, :, :].bitcast(I32),
                 w_scales.rearrange("e a (q r) n -> r q (e a) n", r=4)[r].bitcast(I32),
             )
-        for e0 in range(0, E, 3):
-            load_w(e0, e0 + 3)
+        load_w(0, 2)
+        load_w(2, 4)
         nc.sync.dma_start(b_t[:], b)
+        for r, pos in enumerate((pos1, pos2, pos3)):
+            nc.sync.dma_start(pos_t[r][:], pos)
 
-        def quantize(a, key, lo, hi, on_vector):
-            raw = pieces[(a, key)][0]
-            width = hi - lo
-            grouped = stage.tile([P, width, PACK], BF16, name="grouped", align_bytes=64)
-            cut = width // 2 if on_vector else 0
-            for c0, c1, copy in ((0, cut, nc.vector.tensor_copy), (cut, width, nc.scalar.copy)):
-                if c1 > c0:
-                    copy(
-                        out=grouped[:, c0:c1, :].rearrange("p (c i) j -> p c j i", i=4),
-                        in_=raw[:, :, lo - key + c0:lo - key + c1].rearrange("p j (c i) -> p c j i", i=4),
-                    )
+        def lay_out(copy, grouped, raw):
+            copy(out=grouped.rearrange("p (c i) j -> p c j i", i=2), in_=raw.rearrange("p j (c i) -> p c j i", i=2))
+
+        def quantize(a, lo, hi):
+            grouped = stage.tile([P, hi - lo, PACK], BF16, name="grouped", align_bytes=64)
+            for (pa, c0), (raw, width) in pieces.items():
+                if pa == a and lo <= c0 < hi:
+                    cut = width // 2 if a == 0 else 0
+                    if cut:
+                        lay_out(nc.vector.tensor_copy, grouped[:, c0 - lo:c0 - lo + cut, :], raw[:, :, 0:cut])
+                    lay_out(nc.scalar.copy, grouped[:, c0 - lo + cut:c0 - lo + width, :], raw[:, :, cut:width])
             return lambda: nc.vector.quantize_mx(
                 out=codes[:, start[a] + lo:start[a] + hi].bitcast(FP8X4),
                 scales=x_scales[4 * a:P, lo:hi],
                 in_=grouped[:].rearrange("p w j -> p (w j)"),
             )
 
-        def gather_codes(a, s0, n):
+        def gather_codes(a, s0, n, window):
             nc.vector.tensor_copy(
                 out=slot_codes[a][:, s0:s0 + n],
-                in_=codes[:, start[a]:start[a] + (T if a == 3 else 2 * T)].bitcast(U32).indirect(offs_t[:, s0 // LIST:(s0 + n) // LIST]),
+                in_=codes[:, start[a]:start[a] + window].bitcast(U32).indirect(offs_t[:, s0 // LIST:(s0 + n) // LIST]),
             )
 
-        def gather_scales(s0, n):
+        def gather_and_move_scales(h):
             nc.vector.tensor_copy(
-                out=slot_scales[0][:, s0:s0 + n],
-                in_=x_scales[:].indirect(offs_t[:, s0 // LIST:(s0 + n) // LIST]),
+                out=slot_scales[0][h][:],
+                in_=x_scales[:].indirect(offs_t[:, h * CHUNK // LIST:(h + 1) * CHUNK // LIST]),
             )
-
-        def gather_and_move_scales(s0, s1):
-            gather_scales(s0, s1 - s0)
             for a in range(1, PASSES):
-                nc.sync.dma_start(
-                    slot_scales[a][0:112, s0:s1].bitcast(I32),
-                    slot_scales[0][4 * a:4 * a + 112, s0:s1].bitcast(I32),
-                )
-            for a in range(1, PASSES):
-                nc.sync.dma_start(
-                    slot_scales[a][112:P, s0:s1].bitcast(I32),
-                    slot_scales[0][112:P, s0:s1].bitcast(I32),
-                )
+                nc.sync.dma_start(slot_scales[a][h][0:112, :].bitcast(I32), slot_scales[0][h][4 * a:4 * a + 112, :].bitcast(I32))
+                nc.sync.dma_start(slot_scales[a][h][112:P, :].bitcast(I32), slot_scales[0][h][112:P, :].bitcast(I32))
 
         waiting = None
         for c0, width in ((0, 256), (256, 256), (512, 256), (768, 128), (896, 128)):
-            ready = quantize(0, c0, c0, c0 + width, True)
+            ready = quantize(0, c0, c0 + width)
             if waiting:
                 waiting()
             waiting = ready
         waiting()
         for s0 in (0, 1536):
-            gather_codes(0, s0, 1536)
+            gather_codes(0, s0, 1536, 2 * T)
         for c0 in (0, 512):
-            quantize(1, c0, c0, c0 + 512, False)()
+            quantize(1, c0, c0 + 512)()
         for s0 in (0, 1536):
-            gather_codes(1, s0, 1536)
+            gather_codes(1, s0, 1536, 2 * T)
         for c0 in (0, 512):
-            quantize(2, c0, c0, c0 + 512, False)()
+            quantize(2, c0, c0 + 512)()
+        gather_codes(2, 0, CHUNK, 2 * T)
         for c0, width in ((0, 512), (512, 256), (768, 256)):
-            quantize(3, c0, c0, c0 + width, False)()
-        gather_and_move_scales(0, 1536)
-        gather_and_move_scales(1536, S)
-        for r, pos in enumerate((pos1, pos2, pos3)):
-            nc.sync.dma_start(pos_t[r][:], pos)
-            nc.sync.dma_start(gate_t[r][:], gate[r])
+            quantize(3, c0, c0 + width)()
+        for h in range(CHUNKS):
+            gather_and_move_scales(h)
+            if h + 1 < CHUNKS:
+                load_w(4 * (h + 1), 4 * (h + 2))
 
         acc = {}
 
@@ -170,7 +164,7 @@ def tile_moe_tk_lin_gelu_kernel(tc, xT, w_words, w_scales, b, gate, offs, pos1, 
                 lhsT=w_codes[:, e * PASSES + a, :].bitcast(FP4X4),
                 lhsT_scale=w_planes[:, e * PASSES + a, :],
                 rhs=slot_codes[a][:, s0:s0 + GROUP].bitcast(FP8X4),
-                rhs_scale=slot_scales[a][:, s0:s0 + GROUP],
+                rhs_scale=slot_scales[a][s0 // CHUNK][:, s0 % CHUNK:s0 % CHUNK + GROUP],
                 start=(a == 0),
                 stop=(a == PASSES - 1),
             )
@@ -189,21 +183,24 @@ def tile_moe_tk_lin_gelu_kernel(tc, xT, w_words, w_scales, b, gate, offs, pos1, 
                     func=AF.Gelu_apprx_tanh, bias=b_t[:, e:e + 1],
                 )
 
-        for s0 in range(0, S, 768):
-            gather_codes(2, s0, 768)
-            open_groups(s0, s0 + 768)
-            sizes = (768,) if s0 + 768 < S else (384, 256, 128)
+        for s0 in range(0, S, CHUNK):
+            if s0:
+                gather_codes(2, s0, CHUNK, 4 * T)
+            open_groups(s0, s0 + CHUNK)
+            sizes = (CHUNK,) if s0 + CHUNK < S else (512, 256, 128, 128)
             lo = s0
             for n in sizes:
-                gather_codes(3, lo, n)
+                gather_codes(3, lo, n, WIDE if n == CHUNK else T)
                 close_groups(lo, lo + n)
                 lo += n
 
+        gates = keep.tile([P, TOP, T], F32, name="gates", tag="planes0_1", align_bytes=64)
+        nc.sync.dma_start(gates[:], gate.rearrange("r p t -> p r t"))
         prod = [prods.tile([P, T], F32, name="prod%d" % r) for r in range(TOP)]
 
         def pick(r, t0, t1):
             nc.vector.tensor_tensor(
-                prod[r][:, t0:t1], y[:].indirect(pos_t[r][:, t0 // LIST:t1 // LIST]), gate_t[r][:, t0:t1], MULT,
+                prod[r][:, t0:t1], y[:].indirect(pos_t[r][:, t0 // LIST:t1 // LIST]), gates[:, r, t0:t1], MULT,
             )
 
         blocks = T // P

@@ -29,6 +29,9 @@ LIST = 16
 CHUNK = 1024
 CHUNKS = S // CHUNK
 WIDE = 1408
+BLOCKS = T // P
+OWN = 3
+LENT = BLOCKS - OWN
 
 
 def tile_moe_tk_lin_gelu_kernel(tc, xT, w_words, w_scales, b, gate, offs, pos1, pos2, pos3, out):
@@ -97,6 +100,11 @@ def tile_moe_tk_lin_gelu_kernel(tc, xT, w_words, w_scales, b, gate, offs, pos1, 
         nc.sync.dma_start(b_t[:], b)
         for r, pos in enumerate((pos1, pos2, pos3)):
             nc.sync.dma_start(pos_t[r][:], pos)
+        gate_rows = keep.tile([P, P], F32, name="gate_rows")
+        gate_cols = keep.tile([P, 2 * LENT], F32, name="gate_cols")
+        nc.gpsimd.memset(gate_rows[:], 0.0)
+        for r in (1, 2):
+            nc.sync.dma_start(gate_rows[(r - 1) * LENT:r * LENT, :], gate[r, 0, OWN * P:].rearrange("(b p) -> b p", p=P))
 
         def lay_out(copy, grouped, raw):
             copy(out=grouped.rearrange("p (c i) j -> p c j i", i=2), in_=raw.rearrange("p j (c i) -> p c j i", i=2))
@@ -153,6 +161,10 @@ def tile_moe_tk_lin_gelu_kernel(tc, xT, w_words, w_scales, b, gate, offs, pos1, 
             if h + 1 < CHUNKS:
                 load_w(4 * (h + 1), 4 * (h + 2))
 
+        turned_rows = psum.tile([P, P], F32, name="acc")
+        nc.tensor.transpose(turned_rows[:], gate_rows[:], ident[:])
+        nc.scalar.copy(out=gate_cols[:], in_=turned_rows[:, 0:2 * LENT])
+
         acc = {}
 
         def multiply(g, a):
@@ -194,37 +206,72 @@ def tile_moe_tk_lin_gelu_kernel(tc, xT, w_words, w_scales, b, gate, offs, pos1, 
                 close_groups(lo, lo + n)
                 lo += n
 
-        gates = keep.tile([P, TOP, T], F32, name="gates", tag="planes0_1", align_bytes=64)
-        nc.sync.dma_start(gates[:], gate.rearrange("r p t -> p r t"))
-        prod = [prods.tile([P, T], F32, name="prod%d" % r) for r in range(TOP)]
+        own_w, lent_w = OWN * P, LENT * P
+        gates_own = keep.tile([P, 2, own_w], F32, name="gates_own", tag="planes0_0", align_bytes=64)
+        nc.sync.dma_start(gates_own[:], gate[1:3, :, 0:own_w].rearrange("r p t -> p r t"))
+        gate0 = keep.tile([P, T], F32, name="gate0", tag="planes0_1", align_bytes=64)
+        nc.sync.dma_start(gate0[:], gate[0])
 
-        def pick(r, t0, t1):
-            nc.vector.tensor_tensor(
-                prod[r][:, t0:t1], y[:].indirect(pos_t[r][:, t0 // LIST:t1 // LIST]), gates[:, r, t0:t1], MULT,
-            )
+        def picked(r, t0, t1):
+            return y[:].indirect(pos_t[r][:, t0 // LIST:t1 // LIST])
 
-        blocks = T // P
-        turned = prods.tile([P, T], F32, name="turned")
+        def blk(i):
+            return slice(i * P, (i + 1) * P)
+
+        def add_turned(dst, terms):
+            for i, term in enumerate(terms):
+                nc.tensor.matmul(dst, lhsT=term, rhs=ident[:], is_transpose=True, start=(i == 0), stop=(i == len(terms) - 1))
+
+        plain = {r: prods.tile([P, lent_w], F32, name="plain%d" % r) for r in (1, 2)}
+        prod = {r: prods.tile([P, own_w], F32, name="prod%d" % r) for r in (1, 2)}
+        scaled = {r: prods.tile([P, lent_w], F32, name="scaled%d" % r) for r in (1, 2)}
+        prod0 = prods.tile([P, T], F32, name="prod0")
+        turned = prods.tile([P, own_w], F32, name="turned")
         result = prods.tile([P, T], F32, name="result")
-        pick(0, 0, T)
-        pick(1, 0, T // 2)
-        pick(1, T // 2, T)
-        sums = []
-        for blk in range(blocks):
-            sums.append(psum.tile([P, P], F32, name="acc"))
-            nc.tensor.matmul(sums[blk][:], lhsT=prod[0][:, blk * P:(blk + 1) * P], rhs=ident[:], is_transpose=True, start=True, stop=False)
-        back = []
-        for half in range(2):
-            mine = range(half * blocks // 2, (half + 1) * blocks // 2)
-            for blk in mine:
-                nc.tensor.matmul(sums[blk][:], lhsT=prod[1][:, blk * P:(blk + 1) * P], rhs=ident[:], is_transpose=True, start=False, stop=True)
-                nc.scalar.copy(out=turned[:, blk * P:(blk + 1) * P], in_=sums[blk][:])
-            back.append(psum.tile([P, T // 2], F32, name="acc"))
-            for i, blk in enumerate(mine):
-                nc.tensor.transpose(back[half][:, i * P:(i + 1) * P], turned[:, blk * P:(blk + 1) * P], ident[:])
-        pick(2, 0, T // 2)
-        pick(2, T // 2, T)
-        for t0, t1 in ((0, 512), (512, 832), (832, T)):
-            half = t0 // (T // 2)
-            nc.vector.tensor_tensor(result[:, t0:t1], back[half][:, t0 - half * T // 2:t1 - half * T // 2], prod[2][:, t0:t1], ADD)
+        for r in (1, 2):
+            nc.scalar.activation(out=plain[r][:], in_=picked(r, own_w, T), func=AF.Copy)
+            nc.vector.tensor_tensor(prod[r][:], picked(r, 0, own_w), gates_own[:, r - 1, :], MULT)
+        nc.vector.tensor_tensor(prod0[:], picked(0, 0, T), gate0[:], MULT)
+
+        runs = ((0, 1, 2), (3, 4))
+        across = {}
+
+        def turn(r):
+            for run in runs:
+                bank = psum.tile([P, len(run) * P], F32, name="acc")
+                for j, i in enumerate(run):
+                    nc.tensor.transpose(bank[:, blk(j)], plain[r][:, blk(i)], ident[:])
+                    across[(r, i)] = bank[:, blk(j)]
+
+        def add_turned_row(bank, src, n, first, last):
+            for i in range(n):
+                nc.tensor.matmul(bank[:, blk(i)], lhsT=src[:, blk(i)], rhs=ident[:], is_transpose=True, start=(first and i == 0), stop=(last and i == n - 1))
+
+        def scale(r, i):
+            col = (r - 1) * LENT + i
+            nc.scalar.activation(out=scaled[r][:, blk(i)], in_=across[(r, i)], func=AF.Copy, scale=gate_cols[:, col:col + 1])
+
+        sums = psum.tile([P, own_w], F32, name="acc")
+        add_turned_row(sums, prod[1], OWN, True, False)
+        turn(1)
+        add_turned_row(sums, prod[2], OWN, False, True)
+        turn(2)
+        nc.scalar.copy(out=turned[:], in_=sums[:])
+        back = psum.tile([P, own_w], F32, name="acc")
+        for i in range(OWN):
+            nc.tensor.transpose(back[:, blk(i)], turned[:, blk(i)], ident[:])
+        nc.vector.tensor_tensor(result[:, 0:own_w], back[:], prod0[:, 0:own_w], ADD)
+        nc.sync.dma_start(out[:, 0:own_w], result[:, 0:own_w])
+        backs = []
+        for run in ((0, 1), (2, 3), (4,)):
+            for i in run:
+                scale(1, i)
+            backs.append(psum.tile([P, len(run) * P], F32, name="acc"))
+            add_turned_row(backs[-1], scaled[1][:, run[0] * P:], len(run), True, False)
+        for run, back in zip(((0, 1), (2, 3), (4,)), backs):
+            for i in run:
+                scale(2, i)
+            add_turned_row(back, scaled[2][:, run[0] * P:], len(run), False, True)
+            t0, t1 = own_w + run[0] * P, own_w + (run[-1] + 1) * P
+            nc.vector.tensor_tensor(result[:, t0:t1], back[:], prod0[:, t0:t1], ADD)
             nc.sync.dma_start(out[:, t0:t1], result[:, t0:t1])

@@ -101,10 +101,9 @@ def tile_moe_tk_lin_gelu_kernel(tc, xT, w_words, w_scales, b, gate, offs, pos1, 
         for r, pos in enumerate((pos1, pos2, pos3)):
             nc.sync.dma_start(pos_t[r][:], pos)
         gate_rows = keep.tile([P, P], F32, name="gate_rows")
-        gate_cols = keep.tile([P, 2 * LENT], F32, name="gate_cols")
+        gate_cols = keep.tile([P, 2 * BLOCKS], F32, name="gate_cols")
         nc.gpsimd.memset(gate_rows[:], 0.0)
-        for r in (1, 2):
-            nc.sync.dma_start(gate_rows[(r - 1) * LENT:r * LENT, :], gate[r, 0, OWN * P:].rearrange("(b p) -> b p", p=P))
+        nc.scalar.dma_start(gate_rows[0:2 * BLOCKS, :], gate.rearrange("r n (b p) -> (r n b) p", p=P)[(2 * N - 1) * BLOCKS:(2 * N + 1) * BLOCKS, :])
 
         def lay_out(copy, grouped, raw):
             copy(out=grouped.rearrange("p (c i) j -> p c j i", i=2), in_=raw.rearrange("p j (c i) -> p c j i", i=2))
@@ -163,7 +162,7 @@ def tile_moe_tk_lin_gelu_kernel(tc, xT, w_words, w_scales, b, gate, offs, pos1, 
 
         turned_rows = psum.tile([P, P], F32, name="acc")
         nc.tensor.transpose(turned_rows[:], gate_rows[:], ident[:])
-        nc.scalar.copy(out=gate_cols[:], in_=turned_rows[:, 0:2 * LENT])
+        nc.scalar.copy(out=gate_cols[:], in_=turned_rows[:, 0:2 * BLOCKS])
 
         acc = {}
 
@@ -207,10 +206,8 @@ def tile_moe_tk_lin_gelu_kernel(tc, xT, w_words, w_scales, b, gate, offs, pos1, 
                 lo += n
 
         own_w, lent_w = OWN * P, LENT * P
-        gates_own = keep.tile([P, 2, own_w], F32, name="gates_own", tag="planes0_0", align_bytes=64)
-        nc.sync.dma_start(gates_own[:], gate[1:3, :, 0:own_w].rearrange("r p t -> p r t"))
-        gate0 = keep.tile([P, T], F32, name="gate0", tag="planes0_1", align_bytes=64)
-        nc.sync.dma_start(gate0[:], gate[0])
+        gates = keep.tile([P, TOP, T], F32, name="gates", tag="planes0_1", align_bytes=64)
+        nc.sync.dma_start(gates[:], gate.rearrange("r p t -> p r t"))
 
         def picked(r, t0, t1):
             return y[:].indirect(pos_t[r][:, t0 // LIST:t1 // LIST])
@@ -227,11 +224,11 @@ def tile_moe_tk_lin_gelu_kernel(tc, xT, w_words, w_scales, b, gate, offs, pos1, 
         scaled = {r: prods.tile([P, lent_w], F32, name="scaled%d" % r) for r in (1, 2)}
         prod0 = prods.tile([P, T], F32, name="prod0")
         turned = prods.tile([P, own_w], F32, name="turned")
-        result = prods.tile([P, T], F32, name="result")
+        result = raws.tile([P, T], F32, name="result", tag="raw0_0")
         for r in (1, 2):
             nc.scalar.activation(out=plain[r][:], in_=picked(r, own_w, T), func=AF.Copy)
-            nc.vector.tensor_tensor(prod[r][:], picked(r, 0, own_w), gates_own[:, r - 1, :], MULT)
-        nc.vector.tensor_tensor(prod0[:], picked(0, 0, T), gate0[:], MULT)
+            nc.vector.tensor_tensor(prod[r][:], picked(r, 0, own_w), gates[:, r, 0:own_w], MULT)
+        nc.vector.tensor_tensor(prod0[:], picked(0, 0, T), gates[:, 0, :], MULT)
 
         runs = ((0, 1, 2), (3, 4))
         across = {}
@@ -248,7 +245,7 @@ def tile_moe_tk_lin_gelu_kernel(tc, xT, w_words, w_scales, b, gate, offs, pos1, 
                 nc.tensor.matmul(bank[:, blk(i)], lhsT=src[:, blk(i)], rhs=ident[:], is_transpose=True, start=(first and i == 0), stop=(last and i == n - 1))
 
         def scale(r, i):
-            col = (r - 1) * LENT + i
+            col = (r - 1) * BLOCKS + OWN + i
             nc.scalar.activation(out=scaled[r][:, blk(i)], in_=across[(r, i)], func=AF.Copy, scale=gate_cols[:, col:col + 1])
 
         sums = psum.tile([P, own_w], F32, name="acc")

@@ -29,6 +29,7 @@ LIST = 16
 CHUNK = 1024
 CHUNKS = S // CHUNK
 WIDE = 1408
+BANK = 512
 BLOCKS = T // P
 OWN = 3
 LENT = BLOCKS - OWN
@@ -164,53 +165,57 @@ def tile_moe_tk_lin_gelu_kernel(tc, xT, w_words, w_scales, b, gate, offs, pos1, 
         nc.tensor.transpose(turned_rows[:], gate_rows[:], ident[:])
         nc.scalar.copy(out=gate_cols[:], in_=turned_rows[:, 0:2 * BLOCKS])
 
-        acc = {}
+        y2 = raws.tile([P, S], F32, name="y2", tag="raw2_0")
+        spans = [(s0, s0 + BANK) for s0 in range(0, S - BANK, BANK)] + [(S - BANK, S - C), (S - C, S - GROUP), (S - GROUP, S)]
+        acc = {span: psum.tile([P, span[1] - span[0]], F32, name="acc") for span in spans}
 
-        def multiply(g, a):
-            s0, e = g * GROUP, g * GROUP // C
-            if a == 0:
-                acc[g] = psum.tile([P, GROUP], F32, name="acc")
-            nc.tensor.matmul_mx(
-                out=acc[g][:],
-                lhsT=w_codes[:, e * PASSES + a, :].bitcast(FP4X4),
-                lhsT_scale=w_planes[:, e * PASSES + a, :],
-                rhs=slot_codes[a][:, s0:s0 + GROUP].bitcast(FP8X4),
-                rhs_scale=slot_scales[a][s0 // CHUNK][:, s0 % CHUNK:s0 % CHUNK + GROUP],
-                start=(a == 0),
-                stop=(a == PASSES - 1),
-            )
-
-        def open_groups(s0, s1):
-            for a in range(PASSES - 1):
-                for g in range(s0 // GROUP, s1 // GROUP):
-                    multiply(g, a)
-
-        def close_groups(s0, s1):
-            for g in range(s0 // GROUP, s1 // GROUP):
-                multiply(g, PASSES - 1)
-                e = g * GROUP // C
-                nc.scalar.activation(
-                    out=y[:, g * GROUP:(g + 1) * GROUP], in_=acc[g][:],
-                    func=AF.Gelu_apprx_tanh, bias=b_t[:, e:e + 1],
+        def multiply(span, a):
+            lo, hi = span
+            for s0 in range(lo, hi, C):
+                s1, e = min(s0 + C, hi), s0 // C
+                nc.tensor.matmul_mx(
+                    out=acc[span][:, s0 - lo:s1 - lo],
+                    lhsT=w_codes[:, e * PASSES + a, :].bitcast(FP4X4),
+                    lhsT_scale=w_planes[:, e * PASSES + a, :],
+                    rhs=slot_codes[a][:, s0:s1].bitcast(FP8X4),
+                    rhs_scale=slot_scales[a][s0 // CHUNK][:, s0 % CHUNK:s0 % CHUNK + s1 - s0],
+                    start=(a == 0 and s0 == lo),
+                    stop=(a == PASSES - 1 and s1 == hi),
                 )
 
+        def close(span):
+            lo, hi = span
+            multiply(span, PASSES - 1)
+            for s0 in range(lo, hi, C):
+                s1, e = min(s0 + C, hi), s0 // C
+                for dst in ((y, y2) if hi <= S - CHUNK else (y,)):
+                    nc.scalar.activation(
+                        out=dst[:, s0:s1], in_=acc[span][:, s0 - lo:s1 - lo],
+                        func=AF.Gelu_apprx_tanh, bias=b_t[:, e:e + 1],
+                    )
+
         for s0 in range(0, S, CHUNK):
+            mine = [span for span in spans if s0 <= span[0] < s0 + CHUNK]
             if s0:
                 gather_codes(2, s0, CHUNK, 4 * T)
-            open_groups(s0, s0 + CHUNK)
-            sizes = (CHUNK,) if s0 + CHUNK < S else (512, 256, 128, 128)
-            lo = s0
-            for n in sizes:
-                gather_codes(3, lo, n, WIDE if n == CHUNK else T)
-                close_groups(lo, lo + n)
-                lo += n
+            for a in range(PASSES - 1):
+                for span in mine:
+                    multiply(span, a)
+            if s0 + CHUNK < S:
+                gather_codes(3, s0, CHUNK, WIDE)
+            for span in mine:
+                if s0 + CHUNK == S:
+                    gather_codes(3, span[0], span[1] - span[0], T)
+                close(span)
 
         own_w, lent_w = OWN * P, LENT * P
+        for s0, s1 in ((S - CHUNK, S - 2 * GROUP), (S - 2 * GROUP, S)):
+            nc.vector.tensor_copy(out=y2[:, s0:s1], in_=y[:, s0:s1])
         gates = keep.tile([P, TOP, T], F32, name="gates", tag="planes0_1", align_bytes=64)
         nc.sync.dma_start(gates[:], gate.rearrange("r p t -> p r t"))
 
-        def picked(r, t0, t1):
-            return y[:].indirect(pos_t[r][:, t0 // LIST:t1 // LIST])
+        def picked(src, r, t0, t1):
+            return src[:].indirect(pos_t[r][:, t0 // LIST:t1 // LIST])
 
         def blk(i):
             return slice(i * P, (i + 1) * P)
@@ -222,13 +227,13 @@ def tile_moe_tk_lin_gelu_kernel(tc, xT, w_words, w_scales, b, gate, offs, pos1, 
         plain = {r: prods.tile([P, lent_w], F32, name="plain%d" % r) for r in (1, 2)}
         prod = {r: prods.tile([P, own_w], F32, name="prod%d" % r) for r in (1, 2)}
         scaled = {r: prods.tile([P, lent_w], F32, name="scaled%d" % r) for r in (1, 2)}
-        prod0 = prods.tile([P, T], F32, name="prod0")
+        prod0 = raws.tile([P, T], F32, name="prod0", tag="raw0_256")
         turned = prods.tile([P, own_w], F32, name="turned")
         result = raws.tile([P, T], F32, name="result", tag="raw0_0")
         for r in (1, 2):
-            nc.scalar.activation(out=plain[r][:], in_=picked(r, own_w, T), func=AF.Copy)
-            nc.vector.tensor_tensor(prod[r][:], picked(r, 0, own_w), gates[:, r, 0:own_w], MULT)
-        nc.vector.tensor_tensor(prod0[:], picked(0, 0, T), gates[:, 0, :], MULT)
+            nc.scalar.activation(out=plain[r][:], in_=picked(y, r, own_w, T), func=AF.Copy)
+            nc.vector.tensor_tensor(prod[r][:], picked(y2, r, 0, own_w), gates[:, r, 0:own_w], MULT)
+        nc.vector.tensor_tensor(prod0[:], picked(y2, 0, 0, T), gates[:, 0, :], MULT)
 
         runs = ((0, 1, 2), (3, 4))
         across = {}

@@ -31,7 +31,7 @@ CHUNKS = S // CHUNK
 WIDE = 1408
 BANK = 512
 BLOCKS = T // P
-OWN = 3
+OWN = 4
 LENT = BLOCKS - OWN
 
 
@@ -102,9 +102,10 @@ def tile_moe_tk_lin_gelu_kernel(tc, xT, w_words, w_scales, b, gate, offs, pos1, 
         for r, pos in enumerate((pos1, pos2, pos3)):
             nc.sync.dma_start(pos_t[r][:], pos)
         gate_rows = keep.tile([P, P], F32, name="gate_rows")
-        gate_cols = keep.tile([P, 2 * BLOCKS], F32, name="gate_cols")
+        gate_cols = keep.tile([P, 2 * LENT], F32, name="gate_cols")
         nc.gpsimd.memset(gate_rows[:], 0.0)
-        nc.scalar.dma_start(gate_rows[0:2 * BLOCKS, :], gate.rearrange("r n (b p) -> (r n b) p", p=P)[(2 * N - 1) * BLOCKS:(2 * N + 1) * BLOCKS, :])
+        for r in (1, 2):
+            nc.scalar.dma_start(gate_rows[(r - 1) * LENT:r * LENT, :], gate[r, 0, OWN * P:].rearrange("(b p) -> b p", p=P))
 
         def lay_out(copy, grouped, raw):
             copy(out=grouped.rearrange("p (c i) j -> p c j i", i=2), in_=raw.rearrange("p j (c i) -> p c j i", i=2))
@@ -163,9 +164,8 @@ def tile_moe_tk_lin_gelu_kernel(tc, xT, w_words, w_scales, b, gate, offs, pos1, 
 
         turned_rows = psum.tile([P, P], F32, name="acc")
         nc.tensor.transpose(turned_rows[:], gate_rows[:], ident[:])
-        nc.scalar.copy(out=gate_cols[:], in_=turned_rows[:, 0:2 * BLOCKS])
+        nc.scalar.copy(out=gate_cols[:], in_=turned_rows[:, 0:2 * LENT])
 
-        y2 = raws.tile([P, S], F32, name="y2", tag="raw2_0")
         spans = [(s0, s0 + BANK) for s0 in range(0, S - BANK, BANK)] + [(S - BANK, S - C), (S - C, S - GROUP), (S - GROUP, S)]
         acc = {span: psum.tile([P, span[1] - span[0]], F32, name="acc") for span in spans}
 
@@ -188,7 +188,7 @@ def tile_moe_tk_lin_gelu_kernel(tc, xT, w_words, w_scales, b, gate, offs, pos1, 
             multiply(span, PASSES - 1)
             for s0 in range(lo, hi, C):
                 s1, e = min(s0 + C, hi), s0 // C
-                for dst in ((y, y2) if hi <= S - CHUNK else (y,)):
+                for dst in (y,):
                     nc.scalar.activation(
                         out=dst[:, s0:s1], in_=acc[span][:, s0 - lo:s1 - lo],
                         func=AF.Gelu_apprx_tanh, bias=b_t[:, e:e + 1],
@@ -209,10 +209,9 @@ def tile_moe_tk_lin_gelu_kernel(tc, xT, w_words, w_scales, b, gate, offs, pos1, 
                 close(span)
 
         own_w, lent_w = OWN * P, LENT * P
-        for s0, s1 in ((S - CHUNK, S - 2 * GROUP), (S - 2 * GROUP, S)):
-            nc.vector.tensor_copy(out=y2[:, s0:s1], in_=y[:, s0:s1])
-        gates = keep.tile([P, TOP, T], F32, name="gates", tag="planes0_1", align_bytes=64)
-        nc.sync.dma_start(gates[:], gate.rearrange("r p t -> p r t"))
+        gates = keep.tile([P, 2 * own_w + T], F32, name="gates", tag="planes0_1", align_bytes=64)
+        nc.sync.dma_start(gates[:, 0:2 * own_w].rearrange("p (r t) -> p r t", r=2), gate[1:3, :, 0:own_w].rearrange("r p t -> p r t"))
+        nc.sync.dma_start(gates[:, 2 * own_w:], gate[0])
 
         def picked(src, r, t0, t1):
             return src[:].indirect(pos_t[r][:, t0 // LIST:t1 // LIST])
@@ -232,10 +231,10 @@ def tile_moe_tk_lin_gelu_kernel(tc, xT, w_words, w_scales, b, gate, offs, pos1, 
         result = raws.tile([P, T], F32, name="result", tag="raw0_0")
         for r in (1, 2):
             nc.scalar.activation(out=plain[r][:], in_=picked(y, r, own_w, T), func=AF.Copy)
-            nc.vector.tensor_tensor(prod[r][:], picked(y2, r, 0, own_w), gates[:, r, 0:own_w], MULT)
-        nc.vector.tensor_tensor(prod0[:], picked(y2, 0, 0, T), gates[:, 0, :], MULT)
+            nc.vector.tensor_tensor(prod[r][:], picked(y, r, 0, own_w), gates[:, (r - 1) * own_w:r * own_w], MULT)
+        nc.vector.tensor_tensor(prod0[:], picked(y, 0, 0, T), gates[:, 2 * own_w:], MULT)
 
-        runs = ((0, 1, 2), (3, 4))
+        runs = ((0, 1, 2, 3),)
         across = {}
 
         def turn(r):
@@ -250,27 +249,32 @@ def tile_moe_tk_lin_gelu_kernel(tc, xT, w_words, w_scales, b, gate, offs, pos1, 
                 nc.tensor.matmul(bank[:, blk(i)], lhsT=src[:, blk(i)], rhs=ident[:], is_transpose=True, start=(first and i == 0), stop=(last and i == n - 1))
 
         def scale(r, i):
-            col = (r - 1) * BLOCKS + OWN + i
+            col = (r - 1) * LENT + i
             nc.scalar.activation(out=scaled[r][:, blk(i)], in_=across[(r, i)], func=AF.Copy, scale=gate_cols[:, col:col + 1])
 
-        sums = psum.tile([P, own_w], F32, name="acc")
-        add_turned_row(sums, prod[1], OWN, True, False)
+        parts = ((0, 4),)
+        sums = [psum.tile([P, n * P], F32, name="acc") for i0, n in parts]
+        for bank, (i0, n) in zip(sums, parts):
+            add_turned_row(bank, prod[1][:, i0 * P:], n, True, False)
         turn(1)
-        add_turned_row(sums, prod[2], OWN, False, True)
+        for bank, (i0, n) in zip(sums, parts):
+            add_turned_row(bank, prod[2][:, i0 * P:], n, False, True)
         turn(2)
-        nc.scalar.copy(out=turned[:], in_=sums[:])
-        back = psum.tile([P, own_w], F32, name="acc")
-        for i in range(OWN):
-            nc.tensor.transpose(back[:, blk(i)], turned[:, blk(i)], ident[:])
-        nc.vector.tensor_tensor(result[:, 0:own_w], back[:], prod0[:, 0:own_w], ADD)
-        nc.sync.dma_start(out[:, 0:own_w], result[:, 0:own_w])
         backs = []
-        for run in ((0, 1), (2, 3), (4,)):
+        for run in ((0, 1, 2), (3,)):
             for i in run:
                 scale(1, i)
             backs.append(psum.tile([P, len(run) * P], F32, name="acc"))
             add_turned_row(backs[-1], scaled[1][:, run[0] * P:], len(run), True, False)
-        for run, back in zip(((0, 1), (2, 3), (4,)), backs):
+        for bank, (i0, n) in zip(sums, parts):
+            t0, t1 = i0 * P, (i0 + n) * P
+            nc.scalar.copy(out=turned[:, t0:t1], in_=bank[:])
+            back = psum.tile([P, n * P], F32, name="acc")
+            for i in range(n):
+                nc.tensor.transpose(back[:, blk(i)], turned[:, blk(i0 + i)], ident[:])
+            nc.vector.tensor_tensor(result[:, t0:t1], back[:], prod0[:, t0:t1], ADD)
+            nc.sync.dma_start(out[:, t0:t1], result[:, t0:t1])
+        for run, back in zip(((0, 1, 2), (3,)), backs):
             for i in run:
                 scale(2, i)
             add_turned_row(back, scaled[2][:, run[0] * P:], len(run), False, True)

@@ -24,15 +24,15 @@ AF = mybir.ActivationFunctionType
 MULT = mybir.AluOpType.mult
 ADD = mybir.AluOpType.add
 
-GROUP = 128
 LIST = 16
 CHUNK = 1024
 CHUNKS = S // CHUNK
 WIDE = 1408
 BANK = 512
-BLOCKS = T // P
-OWN = 4
-LENT = BLOCKS - OWN
+SHIFTED = 112
+OWN = T // 2
+LENT = T - OWN
+LENT_BLOCKS = LENT // P
 
 
 def tile_moe_tk_lin_gelu_kernel(tc, xT, w_words, w_scales, b, gate, offs, pos1, pos2, pos3, out):
@@ -48,9 +48,12 @@ def tile_moe_tk_lin_gelu_kernel(tc, xT, w_words, w_scales, b, gate, offs, pos1, 
         pos_t = [keep.tile([P, T // LIST], U16, name="pos%d_t" % r) for r in range(TOP)]
         x_scales = keep.tile([P, WIDE], U8, name="x_scales", align_bytes=64)
         codes = keep.tile([P, 3 * T + WIDE], I32, name="codes", align_bytes=64)
-        start = {2: 0, 1: T, 0: 2 * T, 3: 3 * T}
+        first_word = {2: 0, 1: T, 0: 2 * T, 3: 3 * T}
         slot_codes = [keep.tile([P, S], U32, name="slot_codes%d" % a, align_bytes=64) for a in range(PASSES)]
-        slot_scales = [[keep.tile([P, CHUNK], U8, name="slot_scales%d_%d" % (a, h), tag="planes%d_%d" % (a, h), align_bytes=64) for h in range(CHUNKS)] for a in range(PASSES)]
+        slot_scales = [
+            [keep.tile([P, CHUNK], U8, name="slot_scales%d_%d" % (a, h), tag="planes%d_%d" % (a, h), align_bytes=64) for h in range(CHUNKS)]
+            for a in range(PASSES)
+        ]
         w_codes = keep.tile([P, E * PASSES, 2 * N], U8, name="w_codes", align_bytes=64)
         w_planes = keep.tile([P, E * PASSES, N], U8, name="w_planes", align_bytes=64)
         b_t = keep.tile([P, E], F32, name="b_t")
@@ -66,18 +69,15 @@ def tile_moe_tk_lin_gelu_kernel(tc, xT, w_words, w_scales, b, gate, offs, pos1, 
         nc.vector.memset(codes[:, 3 * T:], 0)
         nc.vector.memset(w_planes[:].rearrange("p g n -> p (g n)").bitcast(I32), 0)
 
-        def load_x(a, c0, width):
-            raw = raws.tile([P, PACK, width], F32, name="raw%d_%d" % (a, c0))
-            rows = xT[a * K_PASS:(a + 1) * K_PASS, c0:c0 + width]
-            nc.sync.dma_start(raw[:], rows.rearrange("(p j) w -> p j w", j=PACK))
-            return raw
-
         pieces = {}
 
         def load_pass(a, widths):
             c0 = 0
             for width in widths:
-                pieces[(a, c0)] = (load_x(a, c0, width), width)
+                raw = raws.tile([P, PACK, width], F32, name="raw%d_%d" % (a, c0))
+                rows = xT[a * K_PASS:(a + 1) * K_PASS, c0:c0 + width]
+                nc.sync.dma_start(raw[:], rows.rearrange("(p j) w -> p j w", j=PACK))
+                pieces[(a, c0)] = (raw, width)
                 c0 += width
 
         def load_w(e0, e1):
@@ -86,7 +86,8 @@ def tile_moe_tk_lin_gelu_kernel(tc, xT, w_words, w_scales, b, gate, offs, pos1, 
                 w_words[e0:e1].rearrange("e a p n -> p (e a) n").bitcast(I32),
             )
 
-        load_pass(0, (256, 256, 256, 128, 128))
+        first_widths = (256, 256, 256, 128, 128)
+        load_pass(0, first_widths)
         nc.sync.dma_start(offs_t[:], offs)
         load_pass(1, (256, 256, 512))
         load_pass(2, (512, 512))
@@ -102,15 +103,18 @@ def tile_moe_tk_lin_gelu_kernel(tc, xT, w_words, w_scales, b, gate, offs, pos1, 
         for r, pos in enumerate((pos1, pos2, pos3)):
             nc.sync.dma_start(pos_t[r][:], pos)
         gate_rows = keep.tile([P, P], F32, name="gate_rows")
-        gate_cols = keep.tile([P, 2 * LENT], F32, name="gate_cols")
+        gate_cols = keep.tile([P, 2 * LENT_BLOCKS], F32, name="gate_cols")
         nc.gpsimd.memset(gate_rows[:], 0.0)
         for r in (1, 2):
-            nc.scalar.dma_start(gate_rows[(r - 1) * LENT:r * LENT, :], gate[r, 0, OWN * P:].rearrange("(b p) -> b p", p=P))
+            nc.scalar.dma_start(
+                gate_rows[(r - 1) * LENT_BLOCKS:r * LENT_BLOCKS, :],
+                gate[r, 0, OWN:].rearrange("(b p) -> b p", p=P),
+            )
 
         def lay_out(copy, grouped, raw):
             copy(out=grouped.rearrange("p (c i) j -> p c j i", i=2), in_=raw.rearrange("p j (c i) -> p c j i", i=2))
 
-        def quantize(a, lo, hi):
+        def lay_out_tokens(a, lo, hi):
             grouped = stage.tile([P, hi - lo, PACK], BF16, name="grouped", align_bytes=64)
             for (pa, c0), (raw, width) in pieces.items():
                 if pa == a and lo <= c0 < hi:
@@ -118,16 +122,26 @@ def tile_moe_tk_lin_gelu_kernel(tc, xT, w_words, w_scales, b, gate, offs, pos1, 
                     if cut:
                         lay_out(nc.vector.tensor_copy, grouped[:, c0 - lo:c0 - lo + cut, :], raw[:, :, 0:cut])
                     lay_out(nc.scalar.copy, grouped[:, c0 - lo + cut:c0 - lo + width, :], raw[:, :, cut:width])
-            return lambda: nc.vector.quantize_mx(
-                out=codes[:, start[a] + lo:start[a] + hi].bitcast(FP8X4),
+            return grouped
+
+        def quantize(a, lo, hi, grouped):
+            nc.vector.quantize_mx(
+                out=codes[:, first_word[a] + lo:first_word[a] + hi].bitcast(FP8X4),
                 scales=x_scales[4 * a:P, lo:hi],
                 in_=grouped[:].rearrange("p w j -> p (w j)"),
             )
 
+        def quantize_pass(a, widths):
+            lo = 0
+            for width in widths:
+                quantize(a, lo, lo + width, lay_out_tokens(a, lo, lo + width))
+                lo += width
+
         def gather_codes(a, s0, n, window):
+            words = codes[:, first_word[a]:first_word[a] + window].bitcast(U32)
             nc.vector.tensor_copy(
                 out=slot_codes[a][:, s0:s0 + n],
-                in_=codes[:, start[a]:start[a] + window].bitcast(U32).indirect(offs_t[:, s0 // LIST:(s0 + n) // LIST]),
+                in_=words.indirect(offs_t[:, s0 // LIST:(s0 + n) // LIST]),
             )
 
         def gather_and_move_scales(h):
@@ -136,43 +150,45 @@ def tile_moe_tk_lin_gelu_kernel(tc, xT, w_words, w_scales, b, gate, offs, pos1, 
                 in_=x_scales[:].indirect(offs_t[:, h * CHUNK // LIST:(h + 1) * CHUNK // LIST]),
             )
             for a in range(1, PASSES):
-                nc.sync.dma_start(slot_scales[a][h][0:112, :].bitcast(I32), slot_scales[0][h][4 * a:4 * a + 112, :].bitcast(I32))
-                nc.sync.dma_start(slot_scales[a][h][112:P, :].bitcast(I32), slot_scales[0][h][112:P, :].bitcast(I32))
+                nc.sync.dma_start(slot_scales[a][h][0:SHIFTED, :].bitcast(I32), slot_scales[0][h][4 * a:4 * a + SHIFTED, :].bitcast(I32))
+                nc.sync.dma_start(slot_scales[a][h][SHIFTED:P, :].bitcast(I32), slot_scales[0][h][SHIFTED:P, :].bitcast(I32))
 
         waiting = None
-        for c0, width in ((0, 256), (256, 256), (512, 256), (768, 128), (896, 128)):
-            ready = quantize(0, c0, c0 + width)
+        lo = 0
+        for width in first_widths:
+            grouped = lay_out_tokens(0, lo, lo + width)
             if waiting:
-                waiting()
-            waiting = ready
-        waiting()
-        for s0 in (0, 1536):
-            gather_codes(0, s0, 1536, 2 * T)
-        for c0 in (0, 512):
-            quantize(1, c0, c0 + 512)()
-        for s0 in (0, 1536):
-            gather_codes(1, s0, 1536, 2 * T)
-        for c0 in (0, 512):
-            quantize(2, c0, c0 + 512)()
+                quantize(*waiting)
+            waiting = (0, lo, lo + width, grouped)
+            lo += width
+        quantize(*waiting)
+        for s0 in (0, S // 2):
+            gather_codes(0, s0, S // 2, 2 * T)
+        quantize_pass(1, (512, 512))
+        for s0 in (0, S // 2):
+            gather_codes(1, s0, S // 2, 2 * T)
+        quantize_pass(2, (512, 512))
         gather_codes(2, 0, CHUNK, 2 * T)
-        for c0, width in ((0, 512), (512, 256), (768, 256)):
-            quantize(3, c0, c0 + width)()
+        quantize_pass(3, (512, 256, 256))
+        experts = CHUNK // C
         for h in range(CHUNKS):
             gather_and_move_scales(h)
             if h + 1 < CHUNKS:
-                load_w(4 * (h + 1), 4 * (h + 2))
+                load_w(experts * (h + 1), experts * (h + 2))
 
-        turned_rows = psum.tile([P, P], F32, name="acc")
+        turned_rows = psum.tile([P, P], F32, name="bank")
         nc.tensor.transpose(turned_rows[:], gate_rows[:], ident[:])
-        nc.scalar.copy(out=gate_cols[:], in_=turned_rows[:, 0:2 * LENT])
+        nc.scalar.copy(out=gate_cols[:], in_=turned_rows[:, 0:2 * LENT_BLOCKS])
 
-        spans = [(s0, s0 + BANK) for s0 in range(0, S - BANK, BANK)] + [(S - BANK, S - C), (S - C, S - GROUP), (S - GROUP, S)]
-        acc = {span: psum.tile([P, span[1] - span[0]], F32, name="acc") for span in spans}
+        spans = [(s0, s0 + BANK) for s0 in range(0, S - BANK, BANK)] + [(S - BANK, S - C), (S - C, S - C // 2), (S - C // 2, S)]
+        acc = {span: psum.tile([P, span[1] - span[0]], F32, name="bank") for span in spans}
+
+        def by_expert(span):
+            return [(s0, min(s0 + C, span[1]), s0 // C) for s0 in range(span[0], span[1], C)]
 
         def multiply(span, a):
             lo, hi = span
-            for s0 in range(lo, hi, C):
-                s1, e = min(s0 + C, hi), s0 // C
+            for s0, s1, e in by_expert(span):
                 nc.tensor.matmul_mx(
                     out=acc[span][:, s0 - lo:s1 - lo],
                     lhsT=w_codes[:, e * PASSES + a, :].bitcast(FP4X4),
@@ -184,100 +200,88 @@ def tile_moe_tk_lin_gelu_kernel(tc, xT, w_words, w_scales, b, gate, offs, pos1, 
                 )
 
         def close(span):
-            lo, hi = span
             multiply(span, PASSES - 1)
-            for s0 in range(lo, hi, C):
-                s1, e = min(s0 + C, hi), s0 // C
-                for dst in (y,):
-                    nc.scalar.activation(
-                        out=dst[:, s0:s1], in_=acc[span][:, s0 - lo:s1 - lo],
-                        func=AF.Gelu_apprx_tanh, bias=b_t[:, e:e + 1],
-                    )
+            for s0, s1, e in by_expert(span):
+                nc.scalar.activation(
+                    out=y[:, s0:s1], in_=acc[span][:, s0 - span[0]:s1 - span[0]],
+                    func=AF.Gelu_apprx_tanh, bias=b_t[:, e:e + 1],
+                )
 
         for s0 in range(0, S, CHUNK):
             mine = [span for span in spans if s0 <= span[0] < s0 + CHUNK]
+            last = s0 + CHUNK == S
             if s0:
                 gather_codes(2, s0, CHUNK, 4 * T)
             for a in range(PASSES - 1):
                 for span in mine:
                     multiply(span, a)
-            if s0 + CHUNK < S:
+            if not last:
                 gather_codes(3, s0, CHUNK, WIDE)
             for span in mine:
-                if s0 + CHUNK == S:
+                if last:
                     gather_codes(3, span[0], span[1] - span[0], T)
                 close(span)
 
-        own_w, lent_w = OWN * P, LENT * P
-        gates = keep.tile([P, 2 * own_w + T], F32, name="gates", tag="planes0_1", align_bytes=64)
-        nc.sync.dma_start(gates[:, 0:2 * own_w].rearrange("p (r t) -> p r t", r=2), gate[1:3, :, 0:own_w].rearrange("r p t -> p r t"))
-        nc.sync.dma_start(gates[:, 2 * own_w:], gate[0])
+        gates = keep.tile([P, 2 * OWN + T], F32, name="gates", tag="planes0_1", align_bytes=64)
+        nc.sync.dma_start(gates[:, 0:2 * OWN].rearrange("p (r t) -> p r t", r=2), gate[1:3, :, 0:OWN].rearrange("r p t -> p r t"))
+        nc.sync.dma_start(gates[:, 2 * OWN:], gate[0])
 
-        def picked(src, r, t0, t1):
-            return src[:].indirect(pos_t[r][:, t0 // LIST:t1 // LIST])
+        def picked(r, t0, t1):
+            return y[:].indirect(pos_t[r][:, t0 // LIST:t1 // LIST])
 
         def blk(i):
             return slice(i * P, (i + 1) * P)
 
-        def add_turned(dst, terms):
-            for i, term in enumerate(terms):
-                nc.tensor.matmul(dst, lhsT=term, rhs=ident[:], is_transpose=True, start=(i == 0), stop=(i == len(terms) - 1))
+        def turn(src, width):
+            bank = psum.tile([P, width], F32, name="bank")
+            for i in range(width // P):
+                nc.tensor.transpose(bank[:, blk(i)], src[:, blk(i)], ident[:])
+            return bank
 
-        plain = {r: prods.tile([P, lent_w], F32, name="plain%d" % r) for r in (1, 2)}
-        prod = {r: prods.tile([P, own_w], F32, name="prod%d" % r) for r in (1, 2)}
-        scaled = {r: prods.tile([P, lent_w], F32, name="scaled%d" % r) for r in (1, 2)}
+        def add_turned(bank, src, width, first, last):
+            blocks = width // P
+            for i in range(blocks):
+                nc.tensor.matmul(
+                    bank[:, blk(i)], lhsT=src[:, blk(i)], rhs=ident[:], is_transpose=True,
+                    start=(first and i == 0), stop=(last and i == blocks - 1),
+                )
+
+        plain = {r: prods.tile([P, LENT], F32, name="plain%d" % r) for r in (1, 2)}
+        prod = {r: prods.tile([P, OWN], F32, name="prod%d" % r) for r in (1, 2)}
+        scaled = {r: prods.tile([P, LENT], F32, name="scaled%d" % r) for r in (1, 2)}
         prod0 = raws.tile([P, T], F32, name="prod0", tag="raw0_256")
-        turned = prods.tile([P, own_w], F32, name="turned")
+        own_turned = prods.tile([P, OWN], F32, name="own_turned")
         result = raws.tile([P, T], F32, name="result", tag="raw0_0")
         for r in (1, 2):
-            nc.scalar.activation(out=plain[r][:], in_=picked(y, r, own_w, T), func=AF.Copy)
-            nc.vector.tensor_tensor(prod[r][:], picked(y, r, 0, own_w), gates[:, (r - 1) * own_w:r * own_w], MULT)
-        nc.vector.tensor_tensor(prod0[:], picked(y, 0, 0, T), gates[:, 2 * own_w:], MULT)
+            nc.scalar.activation(out=plain[r][:], in_=picked(r, OWN, T), func=AF.Copy)
+            nc.vector.tensor_tensor(prod[r][:], picked(r, 0, OWN), gates[:, (r - 1) * OWN:r * OWN], MULT)
+        nc.vector.tensor_tensor(prod0[:], picked(0, 0, T), gates[:, 2 * OWN:], MULT)
 
-        runs = ((0, 1, 2, 3),)
-        across = {}
+        own_sum = psum.tile([P, OWN], F32, name="bank")
+        lent_turned = {}
+        for r in (1, 2):
+            add_turned(own_sum, prod[r], OWN, r == 1, r == 2)
+            lent_turned[r] = turn(plain[r], LENT)
 
-        def turn(r):
-            for run in runs:
-                bank = psum.tile([P, len(run) * P], F32, name="acc")
-                for j, i in enumerate(run):
-                    nc.tensor.transpose(bank[:, blk(j)], plain[r][:, blk(i)], ident[:])
-                    across[(r, i)] = bank[:, blk(j)]
+        def scale_and_add(r, bank, t0, t1):
+            for i in range(t0 // P, t1 // P):
+                col = (r - 1) * LENT_BLOCKS + i
+                nc.scalar.activation(out=scaled[r][:, blk(i)], in_=lent_turned[r][:, blk(i)], func=AF.Copy, scale=gate_cols[:, col:col + 1])
+            add_turned(bank, scaled[r][:, t0:], t1 - t0, r == 1, r == 2)
 
-        def add_turned_row(bank, src, n, first, last):
-            for i in range(n):
-                nc.tensor.matmul(bank[:, blk(i)], lhsT=src[:, blk(i)], rhs=ident[:], is_transpose=True, start=(first and i == 0), stop=(last and i == n - 1))
-
-        def scale(r, i):
-            col = (r - 1) * LENT + i
-            nc.scalar.activation(out=scaled[r][:, blk(i)], in_=across[(r, i)], func=AF.Copy, scale=gate_cols[:, col:col + 1])
-
-        parts = ((0, 4),)
-        sums = [psum.tile([P, n * P], F32, name="acc") for i0, n in parts]
-        for bank, (i0, n) in zip(sums, parts):
-            add_turned_row(bank, prod[1][:, i0 * P:], n, True, False)
-        turn(1)
-        for bank, (i0, n) in zip(sums, parts):
-            add_turned_row(bank, prod[2][:, i0 * P:], n, False, True)
-        turn(2)
-        backs = []
-        for run in ((0, 1, 2), (3,)):
-            for i in run:
-                scale(1, i)
-            backs.append(psum.tile([P, len(run) * P], F32, name="acc"))
-            add_turned_row(backs[-1], scaled[1][:, run[0] * P:], len(run), True, False)
-        for bank, (i0, n) in zip(sums, parts):
-            t0, t1 = i0 * P, (i0 + n) * P
-            nc.scalar.copy(out=turned[:, t0:t1], in_=bank[:])
-            back = psum.tile([P, n * P], F32, name="acc")
-            for i in range(n):
-                nc.tensor.transpose(back[:, blk(i)], turned[:, blk(i0 + i)], ident[:])
-            nc.vector.tensor_tensor(result[:, t0:t1], back[:], prod0[:, t0:t1], ADD)
+        def finish(t0, t1, pair):
+            nc.vector.tensor_tensor(result[:, t0:t1], pair, prod0[:, t0:t1], ADD)
             nc.sync.dma_start(out[:, t0:t1], result[:, t0:t1])
-        for run, back in zip(((0, 1, 2), (3,)), backs):
-            for i in run:
-                scale(2, i)
-            add_turned_row(back, scaled[2][:, run[0] * P:], len(run), False, True)
-            t0, t1 = own_w + run[0] * P, own_w + (run[-1] + 1) * P
-            nc.vector.tensor_tensor(result[:, t0:t1], back[:], prod0[:, t0:t1], ADD)
-            nc.sync.dma_start(out[:, t0:t1], result[:, t0:t1])
+
+        lent_cuts = ((0, LENT - P), (LENT - P, LENT))
+        lent_sums = []
+        for t0, t1 in lent_cuts:
+            lent_sums.append(psum.tile([P, t1 - t0], F32, name="bank"))
+            scale_and_add(1, lent_sums[-1], t0, t1)
+        nc.scalar.copy(out=own_turned[:], in_=own_sum[:])
+        own_back = turn(own_turned, OWN)
+        for t0, t1 in ((0, OWN // 2), (OWN // 2, OWN)):
+            finish(t0, t1, own_back[:, t0:t1])
+        for (t0, t1), bank in zip(lent_cuts, lent_sums):
+            scale_and_add(2, bank, t0, t1)
+            finish(OWN + t0, OWN + t1, bank[:])

@@ -30,7 +30,10 @@ CHUNKS = S // CHUNK
 WIDE = 1408
 BANK = 512
 SHIFTED = 112
-OWN = T // 2
+HALF = T // 2
+LATE = 128
+BODY = S - LATE
+OWN = 384
 LENT = T - OWN
 LENT_BLOCKS = LENT // P
 
@@ -38,18 +41,19 @@ LENT_BLOCKS = LENT // P
 def tile_moe_tk_lin_gelu_kernel(tc, xT, w_words, w_scales, b, gate, offs, pos1, pos2, pos3, out):
     nc = tc.nc
     with ExitStack() as ctx:
+        lists = ctx.enter_context(tc.tile_pool(name="lists", bufs=1))
         keep = ctx.enter_context(tc.tile_pool(name="keep", bufs=1))
         raws = ctx.enter_context(tc.tile_pool(name="raws", bufs=1))
-        stage = ctx.enter_context(tc.tile_pool(name="stage", bufs=7))
-        prods = ctx.enter_context(tc.tile_pool(name="prods", bufs=1))
+        stage = ctx.enter_context(tc.tile_pool(name="stage", bufs=1))
         psum = ctx.enter_context(tc.psum_pool(name="psum", bufs=8))
 
-        offs_t = keep.tile([P, S // LIST], U16, name="offs_t")
-        pos_t = [keep.tile([P, T // LIST], U16, name="pos%d_t" % r) for r in range(TOP)]
+        offs_t = lists.tile([P, S // LIST], U16, name="offs_t")
+        pos_t = [lists.tile([P, T // LIST], U16, name="pos%d_t" % r) for r in range(TOP)]
         x_scales = keep.tile([P, WIDE], U8, name="x_scales", align_bytes=64)
         codes = keep.tile([P, 3 * T + WIDE], I32, name="codes", align_bytes=64)
         first_word = {2: 0, 1: T, 0: 2 * T, 3: 3 * T}
-        slot_codes = [keep.tile([P, S], U32, name="slot_codes%d" % a, align_bytes=64) for a in range(PASSES)]
+        slot_codes = [keep.tile([P, BODY], U32, name="slot_codes%d" % a, align_bytes=64) for a in range(PASSES)]
+        late_codes = {}
         slot_scales = [
             [keep.tile([P, CHUNK], U8, name="slot_scales%d_%d" % (a, h), tag="planes%d_%d" % (a, h), align_bytes=64) for h in range(CHUNKS)]
             for a in range(PASSES)
@@ -71,14 +75,12 @@ def tile_moe_tk_lin_gelu_kernel(tc, xT, w_words, w_scales, b, gate, offs, pos1, 
 
         pieces = {}
 
-        def load_pass(a, widths):
-            c0 = 0
-            for width in widths:
-                raw = raws.tile([P, PACK, width], F32, name="raw%d_%d" % (a, c0))
-                rows = xT[a * K_PASS:(a + 1) * K_PASS, c0:c0 + width]
+        def load_pass(a, ranges):
+            for c0, c1 in ranges:
+                raw = raws.tile([P, PACK, c1 - c0], F32, name="raw%d_%d" % (a, c0))
+                rows = xT[a * K_PASS:(a + 1) * K_PASS, c0:c1]
                 nc.sync.dma_start(raw[:], rows.rearrange("(p j) w -> p j w", j=PACK))
-                pieces[(a, c0)] = (raw, width)
-                c0 += width
+                pieces[(a, c0)] = raw
 
         def load_w(e0, e1):
             nc.sync.dma_start(
@@ -86,12 +88,12 @@ def tile_moe_tk_lin_gelu_kernel(tc, xT, w_words, w_scales, b, gate, offs, pos1, 
                 w_words[e0:e1].rearrange("e a p n -> p (e a) n").bitcast(I32),
             )
 
-        first_widths = (256, 256, 256, 128, 128)
-        load_pass(0, first_widths)
+        head = ((0, 256), (256, 512), (512, 768), (768, 896), (896, T))
+        later = ((0, 384), (640, T), (384, 640))
+        load_pass(0, head)
         nc.sync.dma_start(offs_t[:], offs)
-        load_pass(1, (256, 256, 512))
-        load_pass(2, (512, 512))
-        load_pass(3, (512, 256, 256))
+        for a in range(1, PASSES):
+            load_pass(a, later)
         for r in range(4):
             nc.sync.dma_start(
                 w_planes[r:P:32, :, :].bitcast(I32),
@@ -106,23 +108,13 @@ def tile_moe_tk_lin_gelu_kernel(tc, xT, w_words, w_scales, b, gate, offs, pos1, 
         gate_cols = keep.tile([P, 2 * LENT_BLOCKS], F32, name="gate_cols")
         nc.gpsimd.memset(gate_rows[:], 0.0)
         for r in (1, 2):
-            nc.scalar.dma_start(
+            nc.sync.dma_start(
                 gate_rows[(r - 1) * LENT_BLOCKS:r * LENT_BLOCKS, :],
                 gate[r, 0, OWN:].rearrange("(b p) -> b p", p=P),
             )
 
         def lay_out(copy, grouped, raw):
             copy(out=grouped.rearrange("p (c i) j -> p c j i", i=2), in_=raw.rearrange("p j (c i) -> p c j i", i=2))
-
-        def lay_out_tokens(a, lo, hi):
-            grouped = stage.tile([P, hi - lo, PACK], BF16, name="grouped", align_bytes=64)
-            for (pa, c0), (raw, width) in pieces.items():
-                if pa == a and lo <= c0 < hi:
-                    cut = width // 2 if a == 0 else 0
-                    if cut:
-                        lay_out(nc.vector.tensor_copy, grouped[:, c0 - lo:c0 - lo + cut, :], raw[:, :, 0:cut])
-                    lay_out(nc.scalar.copy, grouped[:, c0 - lo + cut:c0 - lo + width, :], raw[:, :, cut:width])
-            return grouped
 
         def quantize(a, lo, hi, grouped):
             nc.vector.quantize_mx(
@@ -131,18 +123,27 @@ def tile_moe_tk_lin_gelu_kernel(tc, xT, w_words, w_scales, b, gate, offs, pos1, 
                 in_=grouped[:].rearrange("p w j -> p (w j)"),
             )
 
-        def quantize_pass(a, widths):
-            lo = 0
-            for width in widths:
-                quantize(a, lo, lo + width, lay_out_tokens(a, lo, lo + width))
-                lo += width
-
-        def gather_codes(a, s0, n, window):
+        def gather_codes(a, dst, s0, n, window):
             words = codes[:, first_word[a]:first_word[a] + window].bitcast(U32)
-            nc.vector.tensor_copy(
-                out=slot_codes[a][:, s0:s0 + n],
-                in_=words.indirect(offs_t[:, s0 // LIST:(s0 + n) // LIST]),
-            )
+            nc.vector.tensor_copy(out=dst, in_=words.indirect(offs_t[:, s0 // LIST:(s0 + n) // LIST]))
+
+        def gather_body(a, s0, s1, window):
+            gather_codes(a, slot_codes[a][:, s0:s1], s0, s1 - s0, window)
+
+        def quantize_pass(a):
+            halves = [stage.tile([P, HALF, PACK], BF16, name="half%d_%d" % (a, h), align_bytes=64) for h in range(2)]
+            (a0, a1), (b0, b1), (c0, c1) = later
+            last = pieces[(a, c0)]
+            mid = (HALF + c1) // 2
+            lay_out(nc.scalar.copy, halves[0][:, a0:a1, :], pieces[(a, a0)][:])
+            lay_out(nc.scalar.copy, halves[1][:, b0 - HALF:b1 - HALF, :], pieces[(a, b0)][:])
+            lay_out(nc.scalar.copy, halves[1][:, 0:mid - HALF, :], last[:, :, HALF - c0:mid - c0])
+            lay_out(nc.scalar.copy, halves[0][:, c0:HALF, :], last[:, :, 0:HALF - c0])
+            lay_out(nc.scalar.copy, halves[1][:, mid - HALF:c1 - HALF, :], last[:, :, mid - c0:c1 - c0])
+            for h in range(2):
+                quantize(a, h * HALF, (h + 1) * HALF, halves[h])
+            late_codes[a - 1] = stage.tile([P, LATE], U32, name="late%d" % (a - 1), tag="half%d_0" % a, align_bytes=64)
+            gather_codes(a - 1, late_codes[a - 1][:], BODY, LATE, T)
 
         def gather_and_move_scales(h):
             nc.vector.tensor_copy(
@@ -154,22 +155,21 @@ def tile_moe_tk_lin_gelu_kernel(tc, xT, w_words, w_scales, b, gate, offs, pos1, 
                 nc.sync.dma_start(slot_scales[a][h][SHIFTED:P, :].bitcast(I32), slot_scales[0][h][SHIFTED:P, :].bitcast(I32))
 
         waiting = None
-        lo = 0
-        for width in first_widths:
-            grouped = lay_out_tokens(0, lo, lo + width)
+        for lo, hi in head:
+            grouped = stage.tile([P, hi - lo, PACK], BF16, name="head%d" % lo, align_bytes=64)
+            cut = (hi - lo) // 2
+            lay_out(nc.vector.tensor_copy, grouped[:, 0:cut, :], pieces[(0, lo)][:, :, 0:cut])
+            lay_out(nc.scalar.copy, grouped[:, cut:, :], pieces[(0, lo)][:, :, cut:])
             if waiting:
                 quantize(*waiting)
-            waiting = (0, lo, lo + width, grouped)
-            lo += width
+            waiting = (0, lo, hi, grouped)
         quantize(*waiting)
-        for s0 in (0, S // 2):
-            gather_codes(0, s0, S // 2, 2 * T)
-        quantize_pass(1, (512, 512))
-        for s0 in (0, S // 2):
-            gather_codes(1, s0, S // 2, 2 * T)
-        quantize_pass(2, (512, 512))
-        gather_codes(2, 0, CHUNK, 2 * T)
-        quantize_pass(3, (512, 256, 256))
+        for a in (0, 1):
+            gather_body(a, 0, S // 2, 2 * T)
+            gather_body(a, S // 2, BODY, 2 * T)
+            quantize_pass(a + 1)
+        gather_body(2, 0, CHUNK, 2 * T)
+        quantize_pass(3)
         experts = CHUNK // C
         for h in range(CHUNKS):
             gather_and_move_scales(h)
@@ -180,7 +180,7 @@ def tile_moe_tk_lin_gelu_kernel(tc, xT, w_words, w_scales, b, gate, offs, pos1, 
         nc.tensor.transpose(turned_rows[:], gate_rows[:], ident[:])
         nc.scalar.copy(out=gate_cols[:], in_=turned_rows[:, 0:2 * LENT_BLOCKS])
 
-        spans = [(s0, s0 + BANK) for s0 in range(0, S - BANK, BANK)] + [(S - BANK, S - C), (S - C, S - C // 2), (S - C // 2, S)]
+        spans = [(s0, s0 + BANK) for s0 in range(0, S - BANK, BANK)] + [(S - BANK, S - C), (S - C, BODY), (BODY, S)]
         acc = {span: psum.tile([P, span[1] - span[0]], F32, name="bank") for span in spans}
 
         def by_expert(span):
@@ -189,11 +189,12 @@ def tile_moe_tk_lin_gelu_kernel(tc, xT, w_words, w_scales, b, gate, offs, pos1, 
         def multiply(span, a):
             lo, hi = span
             for s0, s1, e in by_expert(span):
+                words = late_codes[a][:] if s0 == BODY else slot_codes[a][:, s0:s1]
                 nc.tensor.matmul_mx(
                     out=acc[span][:, s0 - lo:s1 - lo],
                     lhsT=w_codes[:, e * PASSES + a, :].bitcast(FP4X4),
                     lhsT_scale=w_planes[:, e * PASSES + a, :],
-                    rhs=slot_codes[a][:, s0:s1].bitcast(FP8X4),
+                    rhs=words.bitcast(FP8X4),
                     rhs_scale=slot_scales[a][s0 // CHUNK][:, s0 % CHUNK:s0 % CHUNK + s1 - s0],
                     start=(a == 0 and s0 == lo),
                     stop=(a == PASSES - 1 and s1 == hi),
@@ -207,19 +208,22 @@ def tile_moe_tk_lin_gelu_kernel(tc, xT, w_words, w_scales, b, gate, offs, pos1, 
                     func=AF.Gelu_apprx_tanh, bias=b_t[:, e:e + 1],
                 )
 
+        late_codes[PASSES - 1] = keep.tile([P, LATE], U32, name="late3", align_bytes=64)
         for s0 in range(0, S, CHUNK):
             mine = [span for span in spans if s0 <= span[0] < s0 + CHUNK]
             last = s0 + CHUNK == S
             if s0:
-                gather_codes(2, s0, CHUNK, 4 * T)
+                gather_body(2, s0, min(s0 + CHUNK, BODY), 4 * T)
             for a in range(PASSES - 1):
                 for span in mine:
                     multiply(span, a)
             if not last:
-                gather_codes(3, s0, CHUNK, WIDE)
+                gather_body(3, s0, s0 + CHUNK, WIDE)
             for span in mine:
-                if last:
-                    gather_codes(3, span[0], span[1] - span[0], T)
+                if span[0] == BODY:
+                    gather_codes(3, late_codes[3][:], BODY, LATE, T)
+                elif last:
+                    gather_body(3, span[0], span[1], T)
                 close(span)
 
         gates = keep.tile([P, 2 * OWN + T], F32, name="gates", tag="planes0_1", align_bytes=64)
@@ -232,56 +236,47 @@ def tile_moe_tk_lin_gelu_kernel(tc, xT, w_words, w_scales, b, gate, offs, pos1, 
         def blk(i):
             return slice(i * P, (i + 1) * P)
 
-        def turn(src, width):
-            bank = psum.tile([P, width], F32, name="bank")
-            for i in range(width // P):
-                nc.tensor.transpose(bank[:, blk(i)], src[:, blk(i)], ident[:])
-            return bank
-
-        def add_turned(bank, src, width, first, last):
-            blocks = width // P
-            for i in range(blocks):
-                nc.tensor.matmul(
-                    bank[:, blk(i)], lhsT=src[:, blk(i)], rhs=ident[:], is_transpose=True,
-                    start=(first and i == 0), stop=(last and i == blocks - 1),
-                )
-
-        plain = {r: prods.tile([P, LENT], F32, name="plain%d" % r) for r in (1, 2)}
-        prod = {r: prods.tile([P, OWN], F32, name="prod%d" % r) for r in (1, 2)}
-        scaled = {r: prods.tile([P, LENT], F32, name="scaled%d" % r) for r in (1, 2)}
+        plain = {r: keep.tile([P, LENT], F32, name="plain%d" % r) for r in (1, 2)}
+        scaled = {r: keep.tile([P, LENT], F32, name="scaled%d" % r) for r in (1, 2)}
+        prod = {r: keep.tile([P, OWN], F32, name="prod%d" % r) for r in (1, 2)}
+        pair = keep.tile([P, OWN], F32, name="pair")
         prod0 = raws.tile([P, T], F32, name="prod0", tag="raw0_256")
-        own_turned = prods.tile([P, OWN], F32, name="own_turned")
         result = raws.tile([P, T], F32, name="result", tag="raw0_0")
+
+        def product0(t0, t1):
+            nc.vector.tensor_tensor(prod0[:, t0:t1], picked(0, t0, t1), gates[:, 2 * OWN + t0:2 * OWN + t1], MULT)
+
+        def finish(t0, t1, others):
+            nc.vector.tensor_tensor(result[:, t0:t1], others, prod0[:, t0:t1], ADD)
+            nc.sync.dma_start(out[:, t0:t1], result[:, t0:t1])
+
         for r in (1, 2):
             nc.scalar.activation(out=plain[r][:], in_=picked(r, OWN, T), func=AF.Copy)
             nc.vector.tensor_tensor(prod[r][:], picked(r, 0, OWN), gates[:, (r - 1) * OWN:r * OWN], MULT)
-        nc.vector.tensor_tensor(prod0[:], picked(0, 0, T), gates[:, 2 * OWN:], MULT)
+        product0(0, OWN)
+        nc.vector.tensor_tensor(pair[:], prod[1][:], prod[2][:], ADD)
+        product0(OWN, OWN + 2 * P)
+        finish(0, OWN, pair[:])
+        product0(OWN + 2 * P, T)
 
-        own_sum = psum.tile([P, OWN], F32, name="bank")
-        lent_turned = {}
+        groups = ((0, 3), (3, 4), (4, 5))
+        turned = {}
         for r in (1, 2):
-            add_turned(own_sum, prod[r], OWN, r == 1, r == 2)
-            lent_turned[r] = turn(plain[r], LENT)
-
-        def scale_and_add(r, bank, t0, t1):
-            for i in range(t0 // P, t1 // P):
-                col = (r - 1) * LENT_BLOCKS + i
-                nc.scalar.activation(out=scaled[r][:, blk(i)], in_=lent_turned[r][:, blk(i)], func=AF.Copy, scale=gate_cols[:, col:col + 1])
-            add_turned(bank, scaled[r][:, t0:], t1 - t0, r == 1, r == 2)
-
-        def finish(t0, t1, pair):
-            nc.vector.tensor_tensor(result[:, t0:t1], pair, prod0[:, t0:t1], ADD)
-            nc.sync.dma_start(out[:, t0:t1], result[:, t0:t1])
-
-        lent_cuts = ((0, LENT - P), (LENT - P, LENT))
-        lent_sums = []
-        for t0, t1 in lent_cuts:
-            lent_sums.append(psum.tile([P, t1 - t0], F32, name="bank"))
-            scale_and_add(1, lent_sums[-1], t0, t1)
-        nc.scalar.copy(out=own_turned[:], in_=own_sum[:])
-        own_back = turn(own_turned, OWN)
-        for t0, t1 in ((0, OWN // 2), (OWN // 2, OWN)):
-            finish(t0, t1, own_back[:, t0:t1])
-        for (t0, t1), bank in zip(lent_cuts, lent_sums):
-            scale_and_add(2, bank, t0, t1)
-            finish(OWN + t0, OWN + t1, bank[:])
+            for i0, i1 in ((0, 3), (3, 5)):
+                bank = psum.tile([P, (i1 - i0) * P], F32, name="bank")
+                for i in range(i0, i1):
+                    nc.tensor.transpose(bank[:, blk(i - i0)], plain[r][:, blk(i)], ident[:])
+                    turned[(r, i)] = bank[:, blk(i - i0)]
+        sums = {g: psum.tile([P, (g[1] - g[0]) * P], F32, name="bank") for g in groups}
+        for r in (1, 2):
+            for i0, i1 in groups:
+                for i in range(i0, i1):
+                    col = (r - 1) * LENT_BLOCKS + i
+                    nc.scalar.activation(out=scaled[r][:, blk(i)], in_=turned[(r, i)], func=AF.Copy, scale=gate_cols[:, col:col + 1])
+                for i in range(i0, i1):
+                    nc.tensor.matmul(
+                        sums[(i0, i1)][:, blk(i - i0)], lhsT=scaled[r][:, blk(i)], rhs=ident[:], is_transpose=True,
+                        start=(r == 1 and i == i0), stop=(r == 2 and i == i1 - 1),
+                    )
+                if r == 2:
+                    finish(OWN + i0 * P, OWN + i1 * P, sums[(i0, i1)][:])

@@ -25,14 +25,14 @@ MULT = mybir.AluOpType.mult
 ADD = mybir.AluOpType.add
 
 LIST = 16
-CHUNK = 1024
+CHUNK = 1536
 CHUNKS = S // CHUNK
-WIDE = 1408
+WIDE = 2048
 BANK = 512
 SHIFTED = 112
 HALF = T // 2
-LATE = 128
-BODY = S - LATE
+LATE = {0: 128, 1: 1024, 2: 128, 3: 128}
+BODY = {a: S - n for a, n in LATE.items()}
 OWN = 384
 LENT = T - OWN
 LENT_BLOCKS = LENT // P
@@ -52,7 +52,7 @@ def tile_moe_tk_lin_gelu_kernel(tc, xT, w_words, w_scales, b, gate, offs, pos1, 
         x_scales = keep.tile([P, WIDE], U8, name="x_scales", align_bytes=64)
         codes = keep.tile([P, 3 * T + WIDE], I32, name="codes", align_bytes=64)
         first_word = {2: 0, 1: T, 0: 2 * T, 3: 3 * T}
-        slot_codes = [keep.tile([P, BODY], U32, name="slot_codes%d" % a, align_bytes=64) for a in range(PASSES)]
+        slot_codes = [keep.tile([P, BODY[a]], U32, name="slot_codes%d" % a, align_bytes=64) for a in range(PASSES)]
         late_codes = {}
         slot_scales = [
             [keep.tile([P, CHUNK], U8, name="slot_scales%d_%d" % (a, h), tag="planes%d_%d" % (a, h), align_bytes=64) for h in range(CHUNKS)]
@@ -100,7 +100,7 @@ def tile_moe_tk_lin_gelu_kernel(tc, xT, w_words, w_scales, b, gate, offs, pos1, 
                 w_scales.rearrange("e a (q r) n -> r q (e a) n", r=4)[r].bitcast(I32),
             )
         load_w(0, 2)
-        load_w(2, 4)
+        load_w(2, 6)
         nc.sync.dma_start(b_t[:], b)
         for r, pos in enumerate((pos1, pos2, pos3)):
             nc.sync.dma_start(pos_t[r][:], pos)
@@ -142,8 +142,8 @@ def tile_moe_tk_lin_gelu_kernel(tc, xT, w_words, w_scales, b, gate, offs, pos1, 
             lay_out(nc.scalar.copy, halves[1][:, mid - HALF:c1 - HALF, :], last[:, :, mid - c0:c1 - c0])
             for h in range(2):
                 quantize(a, h * HALF, (h + 1) * HALF, halves[h])
-            late_codes[a - 1] = stage.tile([P, LATE], U32, name="late%d" % (a - 1), tag="half%d_0" % a, align_bytes=64)
-            gather_codes(a - 1, late_codes[a - 1][:], BODY, LATE, T)
+            late_codes[a - 1] = stage.tile([P, LATE[a - 1]], U32, name="late%d" % (a - 1), tag="half%d_0" % a, align_bytes=64)
+            gather_codes(a - 1, late_codes[a - 1][:], BODY[a - 1], LATE[a - 1], T if LATE[a - 1] < T else 2 * T)
 
         def gather_and_move_scales(h):
             nc.vector.tensor_copy(
@@ -164,10 +164,11 @@ def tile_moe_tk_lin_gelu_kernel(tc, xT, w_words, w_scales, b, gate, offs, pos1, 
                 quantize(*waiting)
             waiting = (0, lo, hi, grouped)
         quantize(*waiting)
-        for a in (0, 1):
-            gather_body(a, 0, S // 2, 2 * T)
-            gather_body(a, S // 2, BODY, 2 * T)
-            quantize_pass(a + 1)
+        gather_body(0, 0, S // 2, 2 * T)
+        gather_body(0, S // 2, BODY[0], 2 * T)
+        quantize_pass(1)
+        gather_body(1, 0, BODY[1], 4 * T)
+        quantize_pass(2)
         gather_body(2, 0, CHUNK, 2 * T)
         quantize_pass(3)
         experts = CHUNK // C
@@ -180,16 +181,18 @@ def tile_moe_tk_lin_gelu_kernel(tc, xT, w_words, w_scales, b, gate, offs, pos1, 
         nc.tensor.transpose(turned_rows[:], gate_rows[:], ident[:])
         nc.scalar.copy(out=gate_cols[:], in_=turned_rows[:, 0:2 * LENT_BLOCKS])
 
-        spans = [(s0, s0 + BANK) for s0 in range(0, S - BANK, BANK)] + [(S - BANK, S - C), (S - C, BODY), (BODY, S)]
+        cuts = (0, 1536, 2304, 2688, 2944, S)
+        spans = [(s0, min(s0 + BANK, hi)) for lo, hi in zip(cuts, cuts[1:]) for s0 in range(lo, hi, BANK)]
         acc = {span: psum.tile([P, span[1] - span[0]], F32, name="bank") for span in spans}
 
         def by_expert(span):
-            return [(s0, min(s0 + C, span[1]), s0 // C) for s0 in range(span[0], span[1], C)]
+            edges = sorted({span[0], span[1]} | {s0 for s0 in range(0, S, C) if span[0] < s0 < span[1]})
+            return [(s0, s1, s0 // C) for s0, s1 in zip(edges, edges[1:])]
 
         def multiply(span, a):
             lo, hi = span
             for s0, s1, e in by_expert(span):
-                words = late_codes[a][:] if s0 == BODY else slot_codes[a][:, s0:s1]
+                words = late_codes[a][:, s0 - BODY[a]:s1 - BODY[a]] if s0 >= BODY[a] else slot_codes[a][:, s0:s1]
                 nc.tensor.matmul_mx(
                     out=acc[span][:, s0 - lo:s1 - lo],
                     lhsT=w_codes[:, e * PASSES + a, :].bitcast(FP4X4),
@@ -208,25 +211,24 @@ def tile_moe_tk_lin_gelu_kernel(tc, xT, w_words, w_scales, b, gate, offs, pos1, 
                     func=AF.Gelu_apprx_tanh, bias=b_t[:, e:e + 1],
                 )
 
-        late_codes[PASSES - 1] = keep.tile([P, LATE], U32, name="late3", align_bytes=64)
-        for s0 in range(0, S, CHUNK):
-            mine = [span for span in spans if s0 <= span[0] < s0 + CHUNK]
-            last = s0 + CHUNK == S
-            if s0:
-                gather_body(2, s0, min(s0 + CHUNK, BODY), 4 * T)
-            for a in range(PASSES - 1):
-                for span in mine:
-                    multiply(span, a)
-            if not last:
-                gather_body(3, s0, s0 + CHUNK, WIDE)
-            for span in mine:
-                if span[0] == BODY:
-                    gather_codes(3, late_codes[3][:], BODY, LATE, T)
-                elif last:
-                    gather_body(3, span[0], span[1], T)
-                close(span)
+        late_codes[PASSES - 1] = keep.tile([P, LATE[3]], U32, name="late3", align_bytes=64)
+        for lo, hi in zip(cuts, cuts[1:]):
+            if lo == CHUNK:
+                gather_body(2, CHUNK, BODY[2], 4 * T)
+            if lo % CHUNK == 0:
+                for a in range(PASSES - 1):
+                    for span in spans:
+                        if lo <= span[0] < lo + CHUNK:
+                            multiply(span, a)
+            if lo == BODY[3]:
+                gather_codes(3, late_codes[3][:], lo, hi - lo, T)
+            else:
+                gather_body(3, lo, hi, T if hi - lo < T else WIDE)
+            for span in spans:
+                if lo <= span[0] < hi:
+                    close(span)
 
-        gates = keep.tile([P, 2 * OWN + T], F32, name="gates", tag="planes0_1", align_bytes=64)
+        gates = keep.tile([P, 2 * OWN + T], F32, name="gates", tag="planes0_0", align_bytes=64)
         nc.sync.dma_start(gates[:, 0:2 * OWN].rearrange("p (r t) -> p r t", r=2), gate[1:3, :, 0:OWN].rearrange("r p t -> p r t"))
         nc.sync.dma_start(gates[:, 2 * OWN:], gate[0])
 
@@ -255,9 +257,9 @@ def tile_moe_tk_lin_gelu_kernel(tc, xT, w_words, w_scales, b, gate, offs, pos1, 
             nc.vector.tensor_tensor(prod[r][:], picked(r, 0, OWN), gates[:, (r - 1) * OWN:r * OWN], MULT)
         product0(0, OWN)
         nc.vector.tensor_tensor(pair[:], prod[1][:], prod[2][:], ADD)
-        product0(OWN, OWN + 2 * P)
+        product0(OWN, OWN + 3 * P)
         finish(0, OWN, pair[:])
-        product0(OWN + 2 * P, T)
+        product0(OWN + 3 * P, T)
 
         groups = ((0, 3), (3, 4), (4, 5))
         turned = {}

@@ -88,7 +88,7 @@ def tile_moe_tk_lin_gelu_kernel(tc, xT, w_words, w_scales, b, gate, offs, pos1, 
                 w_words[e0:e1].rearrange("e a p n -> p (e a) n").bitcast(I32),
             )
 
-        head = ((0, 256), (256, 512), (512, 768), (768, 896), (896, T))
+        head = ((0, 512), (512, 896), (896, T))
         later = ((0, 384), (640, T), (384, 640))
         load_pass(0, head)
         nc.sync.dma_start(offs_t[:], offs)

@@ -154,16 +154,20 @@ def tile_moe_tk_lin_gelu_kernel(tc, xT, w_words, w_scales, b, gate, offs, pos1, 
                 nc.sync.dma_start(slot_scales[a][h][0:SHIFTED, :].bitcast(I32), slot_scales[0][h][4 * a:4 * a + SHIFTED, :].bitcast(I32))
                 nc.sync.dma_start(slot_scales[a][h][SHIFTED:P, :].bitcast(I32), slot_scales[0][h][SHIFTED:P, :].bitcast(I32))
 
-        waiting = None
-        for lo, hi in head:
-            grouped = stage.tile([P, hi - lo, PACK], BF16, name="head%d" % lo, align_bytes=64)
-            cut = (hi - lo) // 2
-            lay_out(nc.vector.tensor_copy, grouped[:, 0:cut, :], pieces[(0, lo)][:, :, 0:cut])
-            lay_out(nc.scalar.copy, grouped[:, cut:, :], pieces[(0, lo)][:, :, cut:])
-            if waiting:
-                quantize(*waiting)
-            waiting = (0, lo, hi, grouped)
-        quantize(*waiting)
+        def lay_out_head(copy, grouped, lo, c0, t0, t1):
+            lay_out(copy, grouped[:, t0 - lo:t1 - lo, :], pieces[(0, c0)][:, :, t0 - c0:t1 - c0])
+
+        grouped = {lo: stage.tile([P, hi - lo, PACK], BF16, name="head%d" % lo, align_bytes=64) for lo, hi in ((0, 512), (512, 768), (768, 896), (896, T))}
+        lay_out_head(nc.vector.tensor_copy, grouped[0], 0, 0, 0, 256)
+        lay_out_head(nc.scalar.copy, grouped[0], 0, 0, 256, 512)
+        quantize(0, 0, 512, grouped[0])
+        lay_out_head(nc.vector.tensor_copy, grouped[512], 512, 512, 512, 768)
+        lay_out_head(nc.scalar.copy, grouped[768], 768, 512, 768, 896)
+        quantize(0, 768, 896, grouped[768])
+        lay_out_head(nc.vector.tensor_copy, grouped[896], 896, 896, 896, 960)
+        lay_out_head(nc.scalar.copy, grouped[896], 896, 896, 960, T)
+        quantize(0, 512, 768, grouped[512])
+        quantize(0, 896, T, grouped[896])
         gather_body(0, 0, S // 2, 2 * T)
         gather_body(0, S // 2, BODY[0], 2 * T)
         quantize_pass(1)
@@ -261,7 +265,7 @@ def tile_moe_tk_lin_gelu_kernel(tc, xT, w_words, w_scales, b, gate, offs, pos1, 
         finish(0, OWN, pair[:])
         product0(OWN + 3 * P, T)
 
-        groups = ((0, 3), (3, 4), (4, 5))
+        groups = ((0, 2), (2, 4), (4, 5))
         turned = {}
         for r in (1, 2):
             for i0, i1 in ((0, 3), (3, 5)):

@@ -222,8 +222,12 @@ def tile_moe_tk_lin_gelu_kernel(tc, xT, w_words, w_scales, b, gate, offs, pos1, 
             if lo % CHUNK == 0:
                 for a in range(PASSES - 1):
                     for span in spans:
-                        if lo <= span[0] < lo + CHUNK:
+                        if lo <= span[0] < lo + CHUNK and (a == 0 or span not in spans[-2:]):
                             multiply(span, a)
+            if (lo, hi) == spans[-2]:
+                for a in (1, 2):
+                    for span in spans[-2:]:
+                        multiply(span, a)
             if lo == BODY[3]:
                 gather_codes(3, late_codes[3][:], lo, hi - lo, T)
             else:
@@ -242,12 +246,12 @@ def tile_moe_tk_lin_gelu_kernel(tc, xT, w_words, w_scales, b, gate, offs, pos1, 
         def blk(i):
             return slice(i * P, (i + 1) * P)
 
-        plain = {r: keep.tile([P, LENT], F32, name="plain%d" % r) for r in (1, 2)}
         scaled = {r: keep.tile([P, LENT], F32, name="scaled%d" % r) for r in (1, 2)}
         prod = {r: keep.tile([P, OWN], F32, name="prod%d" % r) for r in (1, 2)}
         pair = keep.tile([P, OWN], F32, name="pair")
-        prod0 = raws.tile([P, T], F32, name="prod0", tag="raw0_256")
+        prod0 = keep.tile([P, T], F32, name="prod0")
         result = raws.tile([P, T], F32, name="result", tag="raw0_0")
+        turned = {}
 
         def product0(t0, t1):
             nc.vector.tensor_tensor(prod0[:, t0:t1], picked(0, t0, t1), gates[:, 2 * OWN + t0:2 * OWN + t1], MULT)
@@ -256,33 +260,46 @@ def tile_moe_tk_lin_gelu_kernel(tc, xT, w_words, w_scales, b, gate, offs, pos1, 
             nc.vector.tensor_tensor(result[:, t0:t1], others, prod0[:, t0:t1], ADD)
             nc.sync.dma_start(out[:, t0:t1], result[:, t0:t1])
 
+        def look_up(r, i0, i1, tag):
+            plain = keep.tile([P, (i1 - i0) * P], F32, name="plain", tag=tag)
+            nc.scalar.activation(out=plain[:], in_=picked(r, OWN + i0 * P, OWN + i1 * P), func=AF.Copy)
+            bank = psum.tile([P, (i1 - i0) * P], F32, name="bank")
+            for i in range(i0, i1):
+                nc.tensor.transpose(bank[:, blk(i - i0)], plain[:, blk(i - i0)], ident[:])
+                turned[(r, i)] = bank[:, blk(i - i0)]
+
+        sums = {}
+
+        def scale_and_add(r, i0, i1):
+            if r == 1:
+                sums[i0] = psum.tile([P, (i1 - i0) * P], F32, name="bank")
+            for i in range(i0, i1):
+                col = (r - 1) * LENT_BLOCKS + i
+                nc.scalar.activation(out=scaled[r][:, blk(i)], in_=turned[(r, i)], func=AF.Copy, scale=gate_cols[:, col:col + 1])
+            for i in range(i0, i1):
+                nc.tensor.matmul(
+                    sums[i0][:, blk(i - i0)], lhsT=scaled[r][:, blk(i)], rhs=ident[:], is_transpose=True,
+                    start=(r == 1 and i == i0), stop=(r == 2 and i == i1 - 1),
+                )
+
+        look_up(1, 0, 2, "plain_a")
+        look_up(1, 2, 5, "plain_b")
+        look_up(2, 0, 2, "plain_c")
+        scale_and_add(1, 0, 2)
+        look_up(2, 2, 5, "plain_a")
+        scale_and_add(2, 0, 2)
         for r in (1, 2):
-            nc.scalar.activation(out=plain[r][:], in_=picked(r, OWN, T), func=AF.Copy)
+            for i in (2, 3, 4):
+                scale_and_add(r, i, i + 1)
+
+        for r in (1, 2):
             nc.vector.tensor_tensor(prod[r][:], picked(r, 0, OWN), gates[:, (r - 1) * OWN:r * OWN], MULT)
         product0(0, OWN)
         nc.vector.tensor_tensor(pair[:], prod[1][:], prod[2][:], ADD)
-        product0(OWN, OWN + 3 * P)
+        product0(OWN, OWN + 2 * P)
         finish(0, OWN, pair[:])
+        product0(OWN + 2 * P, OWN + 3 * P)
+        finish(OWN, OWN + 2 * P, sums[0][:])
         product0(OWN + 3 * P, T)
-
-        groups = ((0, 2), (2, 4), (4, 5))
-        turned = {}
-        for r in (1, 2):
-            for i0, i1 in ((0, 3), (3, 5)):
-                bank = psum.tile([P, (i1 - i0) * P], F32, name="bank")
-                for i in range(i0, i1):
-                    nc.tensor.transpose(bank[:, blk(i - i0)], plain[r][:, blk(i)], ident[:])
-                    turned[(r, i)] = bank[:, blk(i - i0)]
-        sums = {g: psum.tile([P, (g[1] - g[0]) * P], F32, name="bank") for g in groups}
-        for r in (1, 2):
-            for i0, i1 in groups:
-                for i in range(i0, i1):
-                    col = (r - 1) * LENT_BLOCKS + i
-                    nc.scalar.activation(out=scaled[r][:, blk(i)], in_=turned[(r, i)], func=AF.Copy, scale=gate_cols[:, col:col + 1])
-                for i in range(i0, i1):
-                    nc.tensor.matmul(
-                        sums[(i0, i1)][:, blk(i - i0)], lhsT=scaled[r][:, blk(i)], rhs=ident[:], is_transpose=True,
-                        start=(r == 1 and i == i0), stop=(r == 2 and i == i1 - 1),
-                    )
-                if r == 2:
-                    finish(OWN + i0 * P, OWN + i1 * P, sums[(i0, i1)][:])
+        for i in (2, 3, 4):
+            finish(OWN + i * P, OWN + (i + 1) * P, sums[i][:])

@@ -157,16 +157,18 @@ def tile_moe_tk_lin_gelu_kernel(tc, xT, w_words, w_scales, b, gate, offs, pos1, 
         def lay_out_head(copy, grouped, lo, c0, t0, t1):
             lay_out(copy, grouped[:, t0 - lo:t1 - lo, :], pieces[(0, c0)][:, :, t0 - c0:t1 - c0])
 
-        grouped = {lo: stage.tile([P, hi - lo, PACK], BF16, name="head%d" % lo, align_bytes=64) for lo, hi in ((0, 512), (512, 768), (768, 896), (896, T))}
+        grouped = {lo: stage.tile([P, hi - lo, PACK], BF16, name="head%d" % lo, align_bytes=64) for lo, hi in ((0, 256), (256, 512), (512, 640), (640, 896), (896, T))}
         lay_out_head(nc.vector.tensor_copy, grouped[0], 0, 0, 0, 256)
-        lay_out_head(nc.scalar.copy, grouped[0], 0, 0, 256, 512)
-        quantize(0, 0, 512, grouped[0])
-        lay_out_head(nc.vector.tensor_copy, grouped[512], 512, 512, 512, 768)
-        lay_out_head(nc.scalar.copy, grouped[768], 768, 512, 768, 896)
-        quantize(0, 768, 896, grouped[768])
+        lay_out_head(nc.scalar.copy, grouped[256], 256, 0, 256, 512)
+        quantize(0, 0, 256, grouped[0])
+        quantize(0, 256, 512, grouped[256])
+        lay_out_head(nc.scalar.copy, grouped[512], 512, 512, 512, 640)
+        lay_out_head(nc.scalar.copy, grouped[640], 640, 512, 640, 704)
+        lay_out_head(nc.vector.tensor_copy, grouped[640], 640, 512, 704, 896)
+        quantize(0, 512, 640, grouped[512])
         lay_out_head(nc.vector.tensor_copy, grouped[896], 896, 896, 896, 960)
         lay_out_head(nc.scalar.copy, grouped[896], 896, 896, 960, T)
-        quantize(0, 512, 768, grouped[512])
+        quantize(0, 640, 896, grouped[640])
         quantize(0, 896, T, grouped[896])
         gather_body(0, 0, S // 2, 2 * T)
         gather_body(0, S // 2, BODY[0], 2 * T)
@@ -185,7 +187,7 @@ def tile_moe_tk_lin_gelu_kernel(tc, xT, w_words, w_scales, b, gate, offs, pos1, 
         nc.tensor.transpose(turned_rows[:], gate_rows[:], ident[:])
         nc.scalar.copy(out=gate_cols[:], in_=turned_rows[:, 0:2 * LENT_BLOCKS])
 
-        cuts = (0, 1536, 2304, 2688, 2944, S)
+        cuts = (0, 1536, 2048, 2560, 2816, 2944, S)
         spans = [(s0, min(s0 + BANK, hi)) for lo, hi in zip(cuts, cuts[1:]) for s0 in range(lo, hi, BANK)]
         acc = {span: psum.tile([P, span[1] - span[0]], F32, name="bank") for span in spans}
 
@@ -222,11 +224,11 @@ def tile_moe_tk_lin_gelu_kernel(tc, xT, w_words, w_scales, b, gate, offs, pos1, 
             if lo % CHUNK == 0:
                 for a in range(PASSES - 1):
                     for span in spans:
-                        if lo <= span[0] < lo + CHUNK and (a == 0 or span not in spans[-2:]):
+                        if lo <= span[0] < lo + CHUNK and (a == 0 or span not in spans[-3:]):
                             multiply(span, a)
-            if (lo, hi) == spans[-2]:
+            if (lo, hi) == spans[-4]:
                 for a in (1, 2):
-                    for span in spans[-2:]:
+                    for span in spans[-3:]:
                         multiply(span, a)
             if lo == BODY[3]:
                 gather_codes(3, late_codes[3][:], lo, hi - lo, T)

@@ -248,10 +248,10 @@ def tile_moe_tk_lin_gelu_kernel(tc, xT, w_words, w_scales, b, gate, offs, pos1, 
         def blk(i):
             return slice(i * P, (i + 1) * P)
 
-        scaled = {r: keep.tile([P, LENT], F32, name="scaled%d" % r) for r in (1, 2)}
+        scaled = {(r, i): keep.tile([P, P], F32, name="scaled%d_%d" % (r, i)) for r in (1, 2) for i in range(LENT_BLOCKS)}
         prod = {r: keep.tile([P, OWN], F32, name="prod%d" % r) for r in (1, 2)}
         pair = keep.tile([P, OWN], F32, name="pair")
-        prod0 = keep.tile([P, T], F32, name="prod0")
+        prod0 = keep.tile([P, T - P], F32, name="prod0")
         result = raws.tile([P, T], F32, name="result", tag="raw0_0")
         turned = {}
 
@@ -277,10 +277,10 @@ def tile_moe_tk_lin_gelu_kernel(tc, xT, w_words, w_scales, b, gate, offs, pos1, 
                 sums[i0] = psum.tile([P, (i1 - i0) * P], F32, name="bank")
             for i in range(i0, i1):
                 col = (r - 1) * LENT_BLOCKS + i
-                nc.scalar.activation(out=scaled[r][:, blk(i)], in_=turned[(r, i)], func=AF.Copy, scale=gate_cols[:, col:col + 1])
+                nc.scalar.activation(out=scaled[(r, i)][:], in_=turned[(r, i)], func=AF.Copy, scale=gate_cols[:, col:col + 1])
             for i in range(i0, i1):
                 nc.tensor.matmul(
-                    sums[i0][:, blk(i - i0)], lhsT=scaled[r][:, blk(i)], rhs=ident[:], is_transpose=True,
+                    sums[i0][:, blk(i - i0)], lhsT=scaled[(r, i)][:], rhs=ident[:], is_transpose=True,
                     start=(r == 1 and i == i0), stop=(r == 2 and i == i1 - 1),
                 )
 
@@ -300,8 +300,11 @@ def tile_moe_tk_lin_gelu_kernel(tc, xT, w_words, w_scales, b, gate, offs, pos1, 
         nc.vector.tensor_tensor(pair[:], prod[1][:], prod[2][:], ADD)
         product0(OWN, OWN + 2 * P)
         finish(0, OWN, pair[:])
-        product0(OWN + 2 * P, OWN + 3 * P)
+        product0(OWN + 2 * P, OWN + 4 * P)
         finish(OWN, OWN + 2 * P, sums[0][:])
-        product0(OWN + 3 * P, T)
-        for i in (2, 3, 4):
+        prod_last = keep.tile([P, P], F32, name="prod_last", tag="scaled2_1")
+        nc.vector.tensor_tensor(prod_last[:], picked(0, T - P, T), gates[:, 2 * OWN + T - P:], MULT)
+        for i in (2, 3):
             finish(OWN + i * P, OWN + (i + 1) * P, sums[i][:])
+        nc.vector.tensor_tensor(result[:, T - P:], sums[4][:], prod_last[:], ADD)
+        nc.sync.dma_start(out[:, T - P:], result[:, T - P:])

@@ -31,8 +31,9 @@ WIDE = 2048
 BANK = 512
 SHIFTED = 112
 HALF = T // 2
-LATE = {0: 128, 1: 1024, 2: 128, 3: 128}
+LATE = {0: 128, 1: 128, 2: 128, 3: 128}
 BODY = {a: S - n for a, n in LATE.items()}
+EARLY1 = 2048
 OWN = 384
 LENT = T - OWN
 LENT_BLOCKS = LENT // P
@@ -54,10 +55,7 @@ def tile_moe_tk_lin_gelu_kernel(tc, xT, w_words, w_scales, b, gate, offs, pos1, 
         first_word = {2: 0, 1: T, 0: 2 * T, 3: 3 * T}
         slot_codes = [keep.tile([P, BODY[a]], U32, name="slot_codes%d" % a, align_bytes=64) for a in range(PASSES)]
         late_codes = {}
-        slot_scales = [
-            [keep.tile([P, CHUNK], U8, name="slot_scales%d_%d" % (a, h), tag="planes%d_%d" % (a, h), align_bytes=64) for h in range(CHUNKS)]
-            for a in range(PASSES)
-        ]
+        packed = [keep.tile([P, CHUNK], U8, name="packed%d" % h, tag="planes0_%d" % h, align_bytes=64) for h in range(CHUNKS)]
         w_codes = keep.tile([P, E * PASSES, 2 * N], U8, name="w_codes", align_bytes=64)
         w_planes = keep.tile([P, E * PASSES, N], U8, name="w_planes", align_bytes=64)
         b_t = keep.tile([P, E], F32, name="b_t")
@@ -99,8 +97,8 @@ def tile_moe_tk_lin_gelu_kernel(tc, xT, w_words, w_scales, b, gate, offs, pos1, 
                 w_planes[r:P:32, :, :].bitcast(I32),
                 w_scales.rearrange("e a (q r) n -> r q (e a) n", r=4)[r].bitcast(I32),
             )
-        load_w(0, 2)
-        load_w(2, 6)
+        load_w(0, E // 2)
+        load_w(E // 2, E)
         nc.sync.dma_start(b_t[:], b)
         for r, pos in enumerate((pos1, pos2, pos3)):
             nc.sync.dma_start(pos_t[r][:], pos)
@@ -147,12 +145,17 @@ def tile_moe_tk_lin_gelu_kernel(tc, xT, w_words, w_scales, b, gate, offs, pos1, 
 
         def gather_and_move_scales(h):
             nc.vector.tensor_copy(
-                out=slot_scales[0][h][:],
+                out=packed[h][:],
                 in_=x_scales[:].indirect(offs_t[:, h * CHUNK // LIST:(h + 1) * CHUNK // LIST]),
             )
             for a in range(1, PASSES):
-                nc.sync.dma_start(slot_scales[a][h][0:SHIFTED, :].bitcast(I32), slot_scales[0][h][4 * a:4 * a + SHIFTED, :].bitcast(I32))
-                nc.sync.dma_start(slot_scales[a][h][SHIFTED:P, :].bitcast(I32), slot_scales[0][h][SHIFTED:P, :].bitcast(I32))
+                c0 = (a - 1) * S + h * CHUNK
+                nc.sync.dma_start(lifted[0:SHIFTED, c0:c0 + CHUNK].bitcast(I32), packed[h][4 * a:4 * a + SHIFTED, :].bitcast(I32))
+
+        def plane(a, s0, s1):
+            if a == 0:
+                return packed[s0 // CHUNK][:, s0 % CHUNK:s0 % CHUNK + s1 - s0]
+            return lifted[:, (a - 1) * S + s0:(a - 1) * S + s1]
 
         def lay_out_head(copy, grouped, lo, c0, t0, t1):
             lay_out(copy, grouped[:, t0 - lo:t1 - lo, :], pieces[(0, c0)][:, :, t0 - c0:t1 - c0])
@@ -170,18 +173,18 @@ def tile_moe_tk_lin_gelu_kernel(tc, xT, w_words, w_scales, b, gate, offs, pos1, 
         lay_out_head(nc.scalar.copy, grouped[896], 896, 896, 960, T)
         quantize(0, 640, 896, grouped[640])
         quantize(0, 896, T, grouped[896])
+        lifted = stage.tile([P, (PASSES - 1) * S], U8, name="lifted", tag="head896", align_bytes=64)
+        nc.gpsimd.memset(lifted[:].bitcast(I32), 0)
         gather_body(0, 0, S // 2, 2 * T)
         gather_body(0, S // 2, BODY[0], 2 * T)
         quantize_pass(1)
-        gather_body(1, 0, BODY[1], 4 * T)
+        gather_body(1, 0, EARLY1, 4 * T)
         quantize_pass(2)
         gather_body(2, 0, CHUNK, 2 * T)
         quantize_pass(3)
-        experts = CHUNK // C
         for h in range(CHUNKS):
             gather_and_move_scales(h)
-            if h + 1 < CHUNKS:
-                load_w(experts * (h + 1), experts * (h + 2))
+        gather_body(1, EARLY1, BODY[1], 4 * T)
 
         turned_rows = psum.tile([P, P], F32, name="bank")
         nc.tensor.transpose(turned_rows[:], gate_rows[:], ident[:])
@@ -204,7 +207,7 @@ def tile_moe_tk_lin_gelu_kernel(tc, xT, w_words, w_scales, b, gate, offs, pos1, 
                     lhsT=w_codes[:, e * PASSES + a, :].bitcast(FP4X4),
                     lhsT_scale=w_planes[:, e * PASSES + a, :],
                     rhs=words.bitcast(FP8X4),
-                    rhs_scale=slot_scales[a][s0 // CHUNK][:, s0 % CHUNK:s0 % CHUNK + s1 - s0],
+                    rhs_scale=plane(a, s0, s1),
                     start=(a == 0 and s0 == lo),
                     stop=(a == PASSES - 1 and s1 == hi),
                 )

@@ -31,9 +31,8 @@ WIDE = 2048
 BANK = 512
 SHIFTED = 112
 HALF = T // 2
-LATE = {0: 128, 1: 128, 2: 128, 3: 128}
+LATE = {0: 128, 1: 1024, 2: 128, 3: 128}
 BODY = {a: S - n for a, n in LATE.items()}
-EARLY1 = 2048
 OWN = 384
 LENT = T - OWN
 LENT_BLOCKS = LENT // P
@@ -46,6 +45,7 @@ def tile_moe_tk_lin_gelu_kernel(tc, xT, w_words, w_scales, b, gate, offs, pos1, 
         keep = ctx.enter_context(tc.tile_pool(name="keep", bufs=1))
         raws = ctx.enter_context(tc.tile_pool(name="raws", bufs=1))
         stage = ctx.enter_context(tc.tile_pool(name="stage", bufs=1))
+        lap = ctx.enter_context(tc.tile_pool(name="lap", bufs=1))
         psum = ctx.enter_context(tc.psum_pool(name="psum", bufs=8))
 
         offs_t = lists.tile([P, S // LIST], U16, name="offs_t")
@@ -57,20 +57,21 @@ def tile_moe_tk_lin_gelu_kernel(tc, xT, w_words, w_scales, b, gate, offs, pos1, 
         late_codes = {}
         packed = [keep.tile([P, CHUNK], U8, name="packed%d" % h, tag="planes0_%d" % h, align_bytes=64) for h in range(CHUNKS)]
         w_codes = keep.tile([P, E * PASSES, 2 * N], U8, name="w_codes", align_bytes=64)
-        w_planes = keep.tile([P, E * PASSES, N], U8, name="w_planes", align_bytes=64)
         b_t = keep.tile([P, E], F32, name="b_t")
         y = keep.tile([P, S], F32, name="y")
         warm = keep.tile([P, 1], F32, name="warm")
         warm_out = keep.tile([P, 1], F32, name="warm_out")
 
+        nc.gpsimd.memset(warm[:], 0.0)
+        nc.scalar.activation(out=warm_out[:], in_=warm[:], func=AF.Gelu_apprx_tanh)
         ident = keep.tile([P, P], F32, name="ident")
         make_identity(nc, ident[:])
-        nc.vector.memset(warm[:], 0.0)
-        nc.scalar.activation(out=warm_out[:], in_=warm[:], func=AF.Gelu_apprx_tanh)
         nc.vector.memset(x_scales[:].bitcast(I32), 0)
         nc.vector.memset(codes[:, 3 * T:], 0)
-        nc.vector.memset(w_planes[:].rearrange("p g n -> p (g n)").bitcast(I32), 0)
 
+        gate_rows = keep.tile([P, P], F32, name="gate_rows")
+        gate_cols = keep.tile([P, 2 * LENT_BLOCKS], F32, name="gate_cols")
+        nc.gpsimd.memset(gate_rows[:], 0.0)
         pieces = {}
 
         def load_pass(a, ranges):
@@ -92,25 +93,6 @@ def tile_moe_tk_lin_gelu_kernel(tc, xT, w_words, w_scales, b, gate, offs, pos1, 
         nc.sync.dma_start(offs_t[:], offs)
         for a in range(1, PASSES):
             load_pass(a, later)
-        for r in range(4):
-            nc.sync.dma_start(
-                w_planes[r:P:32, :, :].bitcast(I32),
-                w_scales.rearrange("e a (q r) n -> r q (e a) n", r=4)[r].bitcast(I32),
-            )
-        load_w(0, E // 2)
-        load_w(E // 2, E)
-        nc.sync.dma_start(b_t[:], b)
-        for r, pos in enumerate((pos1, pos2, pos3)):
-            nc.sync.dma_start(pos_t[r][:], pos)
-        gate_rows = keep.tile([P, P], F32, name="gate_rows")
-        gate_cols = keep.tile([P, 2 * LENT_BLOCKS], F32, name="gate_cols")
-        nc.gpsimd.memset(gate_rows[:], 0.0)
-        for r in (1, 2):
-            nc.sync.dma_start(
-                gate_rows[(r - 1) * LENT_BLOCKS:r * LENT_BLOCKS, :],
-                gate[r, 0, OWN:].rearrange("(b p) -> b p", p=P),
-            )
-
         def lay_out(copy, grouped, raw):
             copy(out=grouped.rearrange("p (c i) j -> p c j i", i=2), in_=raw.rearrange("p j (c i) -> p c j i", i=2))
 
@@ -132,12 +114,10 @@ def tile_moe_tk_lin_gelu_kernel(tc, xT, w_words, w_scales, b, gate, offs, pos1, 
             halves = [stage.tile([P, HALF, PACK], BF16, name="half%d_%d" % (a, h), align_bytes=64) for h in range(2)]
             (a0, a1), (b0, b1), (c0, c1) = later
             last = pieces[(a, c0)]
-            mid = (HALF + c1) // 2
             lay_out(nc.scalar.copy, halves[0][:, a0:a1, :], pieces[(a, a0)][:])
             lay_out(nc.scalar.copy, halves[1][:, b0 - HALF:b1 - HALF, :], pieces[(a, b0)][:])
-            lay_out(nc.scalar.copy, halves[1][:, 0:mid - HALF, :], last[:, :, HALF - c0:mid - c0])
             lay_out(nc.scalar.copy, halves[0][:, c0:HALF, :], last[:, :, 0:HALF - c0])
-            lay_out(nc.scalar.copy, halves[1][:, mid - HALF:c1 - HALF, :], last[:, :, mid - c0:c1 - c0])
+            lay_out(nc.scalar.copy, halves[1][:, 0:c1 - HALF, :], last[:, :, HALF - c0:c1 - c0])
             for h in range(2):
                 quantize(a, h * HALF, (h + 1) * HALF, halves[h])
             late_codes[a - 1] = stage.tile([P, LATE[a - 1]], U32, name="late%d" % (a - 1), tag="half%d_0" % a, align_bytes=64)
@@ -160,7 +140,8 @@ def tile_moe_tk_lin_gelu_kernel(tc, xT, w_words, w_scales, b, gate, offs, pos1, 
         def lay_out_head(copy, grouped, lo, c0, t0, t1):
             lay_out(copy, grouped[:, t0 - lo:t1 - lo, :], pieces[(0, c0)][:, :, t0 - c0:t1 - c0])
 
-        grouped = {lo: stage.tile([P, hi - lo, PACK], BF16, name="head%d" % lo, align_bytes=64) for lo, hi in ((0, 256), (256, 512), (512, 640), (640, 896), (896, T))}
+        grouped = {lo: stage.tile([P, hi - lo, PACK], BF16, name="head%d" % lo, align_bytes=64) for lo, hi in ((0, 256), (256, 512), (512, 640), (640, 896))}
+        grouped[896] = lap.tile([P, T - 896, PACK], BF16, name="head896", align_bytes=64, offset=E * PASSES * N - 512)
         lay_out_head(nc.vector.tensor_copy, grouped[0], 0, 0, 0, 256)
         lay_out_head(nc.scalar.copy, grouped[256], 256, 0, 256, 512)
         quantize(0, 0, 256, grouped[0])
@@ -173,18 +154,34 @@ def tile_moe_tk_lin_gelu_kernel(tc, xT, w_words, w_scales, b, gate, offs, pos1, 
         lay_out_head(nc.scalar.copy, grouped[896], 896, 896, 960, T)
         quantize(0, 640, 896, grouped[640])
         quantize(0, 896, T, grouped[896])
-        lifted = stage.tile([P, (PASSES - 1) * S], U8, name="lifted", tag="head896", align_bytes=64)
+        w_planes = lap.tile([P, E * PASSES, N], U8, name="w_planes", align_bytes=64, offset=0)
+        lifted = lap.tile([P, (PASSES - 1) * S], U8, name="lifted", align_bytes=64, offset=E * PASSES * N)
+        nc.gpsimd.memset(w_planes[:].rearrange("p g n -> p (g n)").bitcast(I32), 0)
         nc.gpsimd.memset(lifted[:].bitcast(I32), 0)
+        for r in range(4):
+            nc.sync.dma_start(
+                w_planes[r:P:32, :, :].bitcast(I32),
+                w_scales.rearrange("e a (q r) n -> r q (e a) n", r=4)[r].bitcast(I32),
+            )
+        load_w(0, E // 2)
+        load_w(E // 2, E)
+        nc.sync.dma_start(b_t[:], b)
+        for r, pos in enumerate((pos1, pos2, pos3)):
+            nc.sync.dma_start(pos_t[r][:], pos)
+        for r in (1, 2):
+            nc.sync.dma_start(
+                gate_rows[(r - 1) * LENT_BLOCKS:r * LENT_BLOCKS, :],
+                gate[r, 0, OWN:].rearrange("(b p) -> b p", p=P),
+            )
         gather_body(0, 0, S // 2, 2 * T)
         gather_body(0, S // 2, BODY[0], 2 * T)
         quantize_pass(1)
-        gather_body(1, 0, EARLY1, 4 * T)
+        gather_body(1, 0, BODY[1], 4 * T)
         quantize_pass(2)
         gather_body(2, 0, CHUNK, 2 * T)
         quantize_pass(3)
         for h in range(CHUNKS):
             gather_and_move_scales(h)
-        gather_body(1, EARLY1, BODY[1], 4 * T)
 
         turned_rows = psum.tile([P, P], F32, name="bank")
         nc.tensor.transpose(turned_rows[:], gate_rows[:], ident[:])
@@ -288,14 +285,18 @@ def tile_moe_tk_lin_gelu_kernel(tc, xT, w_words, w_scales, b, gate, offs, pos1, 
                 )
 
         look_up(1, 0, 2, "plain_a")
-        look_up(1, 2, 5, "plain_b")
-        look_up(2, 0, 2, "plain_c")
-        scale_and_add(1, 0, 2)
-        look_up(2, 2, 5, "plain_a")
-        scale_and_add(2, 0, 2)
+        look_up(2, 0, 2, "plain_b")
+        look_up(1, 2, 4, "plain_c")
         for r in (1, 2):
-            for i in (2, 3, 4):
+            scale_and_add(r, 0, 2)
+        look_up(2, 2, 4, "plain_b")
+        look_up(1, 4, 5, "plain_c")
+        look_up(2, 4, 5, "plain_a")
+        for r in (1, 2):
+            for i in (2, 3):
                 scale_and_add(r, i, i + 1)
+        for r in (1, 2):
+            scale_and_add(r, 4, 5)
 
         for r in (1, 2):
             nc.vector.tensor_tensor(prod[r][:], picked(r, 0, OWN), gates[:, (r - 1) * OWN:r * OWN], MULT)

@@ -10,6 +10,7 @@ P = 128
 PACK = 4
 K_PASS = P * PACK
 PASSES = K // K_PASS
+LAST = PASSES - 1
 FLOPS = 2 * K * N * S
 
 F32 = mybir.dt.float32
@@ -25,14 +26,21 @@ MULT = mybir.AluOpType.mult
 ADD = mybir.AluOpType.add
 
 LIST = 16
-CHUNK = 1536
-CHUNKS = S // CHUNK
-WIDE = 2048
+QUADRANT = 32
+SCALE_ROWS = 4
 BANK = 512
+BANKS = 8
+CHUNK = S // 2
+CHUNKS = S // CHUNK
+WIDE = 2 * T
 SHIFTED = 112
 HALF = T // 2
 LATE = {0: 128, 1: 1024, 2: 128, 3: 128}
 BODY = {a: S - n for a, n in LATE.items()}
+HEAD = ((0, 512), (512, 896), (896, T))
+LATER = ((0, 384), (640, T), (384, 640))
+CUTS = (0, 1536, 2048, 2560, 2816, 2944, S)
+W_EXPERTS = 3
 OWN = 384
 LENT = T - OWN
 LENT_BLOCKS = LENT // P
@@ -46,16 +54,16 @@ def tile_moe_tk_lin_gelu_kernel(tc, xT, w_words, w_scales, b, gate, offs, pos1, 
         raws = ctx.enter_context(tc.tile_pool(name="raws", bufs=1))
         stage = ctx.enter_context(tc.tile_pool(name="stage", bufs=1))
         lap = ctx.enter_context(tc.tile_pool(name="lap", bufs=1))
-        psum = ctx.enter_context(tc.psum_pool(name="psum", bufs=8))
+        psum = ctx.enter_context(tc.psum_pool(name="psum", bufs=BANKS))
 
         offs_t = lists.tile([P, S // LIST], U16, name="offs_t")
         pos_t = [lists.tile([P, T // LIST], U16, name="pos%d_t" % r) for r in range(TOP)]
         x_scales = keep.tile([P, WIDE], U8, name="x_scales", align_bytes=64)
-        codes = keep.tile([P, 3 * T + WIDE], I32, name="codes", align_bytes=64)
+        codes = keep.tile([P, LAST * T + WIDE], I32, name="codes", align_bytes=64)
         first_word = {2: 0, 1: T, 0: 2 * T, 3: 3 * T}
         slot_codes = [keep.tile([P, BODY[a]], U32, name="slot_codes%d" % a, align_bytes=64) for a in range(PASSES)]
         late_codes = {}
-        packed = [keep.tile([P, CHUNK], U8, name="packed%d" % h, tag="planes0_%d" % h, align_bytes=64) for h in range(CHUNKS)]
+        packed = [keep.tile([P, CHUNK], U8, name="packed%d" % h, align_bytes=64) for h in range(CHUNKS)]
         w_codes = keep.tile([P, E * PASSES, 2 * N], U8, name="w_codes", align_bytes=64)
         b_t = keep.tile([P, E], F32, name="b_t")
         y = keep.tile([P, S], F32, name="y")
@@ -67,7 +75,7 @@ def tile_moe_tk_lin_gelu_kernel(tc, xT, w_words, w_scales, b, gate, offs, pos1, 
         ident = keep.tile([P, P], F32, name="ident")
         make_identity(nc, ident[:])
         nc.vector.memset(x_scales[:].bitcast(I32), 0)
-        nc.vector.memset(codes[:, 3 * T:], 0)
+        nc.vector.memset(codes[:, first_word[LAST]:], 0)
 
         gate_rows = keep.tile([P, P], F32, name="gate_rows")
         gate_cols = keep.tile([P, 2 * LENT_BLOCKS], F32, name="gate_cols")
@@ -81,25 +89,18 @@ def tile_moe_tk_lin_gelu_kernel(tc, xT, w_words, w_scales, b, gate, offs, pos1, 
                 nc.sync.dma_start(raw[:], rows.rearrange("(p j) w -> p j w", j=PACK))
                 pieces[(a, c0)] = raw
 
-        def load_w(e0, e1):
-            nc.sync.dma_start(
-                w_codes[:, e0 * PASSES:e1 * PASSES, :].bitcast(I32),
-                w_words[e0:e1].rearrange("e a p n -> p (e a) n").bitcast(I32),
-            )
-
-        head = ((0, 512), (512, 896), (896, T))
-        later = ((0, 384), (640, T), (384, 640))
-        load_pass(0, head)
+        load_pass(0, HEAD)
         nc.sync.dma_start(offs_t[:], offs)
         for a in range(1, PASSES):
-            load_pass(a, later)
+            load_pass(a, LATER)
+
         def lay_out(copy, grouped, raw):
             copy(out=grouped.rearrange("p (c i) j -> p c j i", i=2), in_=raw.rearrange("p j (c i) -> p c j i", i=2))
 
         def quantize(a, lo, hi, grouped):
             nc.vector.quantize_mx(
                 out=codes[:, first_word[a] + lo:first_word[a] + hi].bitcast(FP8X4),
-                scales=x_scales[4 * a:P, lo:hi],
+                scales=x_scales[SCALE_ROWS * a:P, lo:hi],
                 in_=grouped[:].rearrange("p w j -> p (w j)"),
             )
 
@@ -112,16 +113,62 @@ def tile_moe_tk_lin_gelu_kernel(tc, xT, w_words, w_scales, b, gate, offs, pos1, 
 
         def quantize_pass(a):
             halves = [stage.tile([P, HALF, PACK], BF16, name="half%d_%d" % (a, h), align_bytes=64) for h in range(2)]
-            (a0, a1), (b0, b1), (c0, c1) = later
-            last = pieces[(a, c0)]
+            (a0, a1), (b0, b1), (c0, c1) = LATER
+            across = pieces[(a, c0)]
             lay_out(nc.scalar.copy, halves[0][:, a0:a1, :], pieces[(a, a0)][:])
             lay_out(nc.scalar.copy, halves[1][:, b0 - HALF:b1 - HALF, :], pieces[(a, b0)][:])
-            lay_out(nc.scalar.copy, halves[0][:, c0:HALF, :], last[:, :, 0:HALF - c0])
-            lay_out(nc.scalar.copy, halves[1][:, 0:c1 - HALF, :], last[:, :, HALF - c0:c1 - c0])
+            lay_out(nc.scalar.copy, halves[0][:, c0:HALF, :], across[:, :, 0:HALF - c0])
+            lay_out(nc.scalar.copy, halves[1][:, 0:c1 - HALF, :], across[:, :, HALF - c0:c1 - c0])
             for h in range(2):
                 quantize(a, h * HALF, (h + 1) * HALF, halves[h])
             late_codes[a - 1] = stage.tile([P, LATE[a - 1]], U32, name="late%d" % (a - 1), tag="half%d_0" % a, align_bytes=64)
-            gather_codes(a - 1, late_codes[a - 1][:], BODY[a - 1], LATE[a - 1], T if LATE[a - 1] < T else 2 * T)
+            gather_codes(a - 1, late_codes[a - 1][:], BODY[a - 1], LATE[a - 1], T if LATE[a - 1] < T else WIDE)
+
+        groups = {lo: stage.tile([P, hi - lo, PACK], BF16, name="head%d" % lo, align_bytes=64) for lo, hi in ((0, 256), (256, 512), (512, 640), (640, 896))}
+        w_plane_bytes = E * PASSES * N
+        last_lo = HEAD[-1][0]
+        groups[last_lo] = lap.tile([P, T - last_lo, PACK], BF16, name="head_last", align_bytes=64, offset=w_plane_bytes - (T - last_lo) * PACK)
+
+        def lay_out_head(copy, lo, c0, t0, t1):
+            lay_out(copy, groups[lo][:, t0 - lo:t1 - lo, :], pieces[(0, c0)][:, :, t0 - c0:t1 - c0])
+
+        lay_out_head(nc.vector.tensor_copy, 0, 0, 0, 256)
+        lay_out_head(nc.scalar.copy, 256, 0, 256, 512)
+        quantize(0, 0, 256, groups[0])
+        quantize(0, 256, 512, groups[256])
+        lay_out_head(nc.scalar.copy, 512, 512, 512, 640)
+        lay_out_head(nc.scalar.copy, 640, 512, 640, 704)
+        lay_out_head(nc.vector.tensor_copy, 640, 512, 704, 896)
+        quantize(0, 512, 640, groups[512])
+        lay_out_head(nc.vector.tensor_copy, 896, 896, 896, 960)
+        lay_out_head(nc.scalar.copy, 896, 896, 960, T)
+        quantize(0, 640, 896, groups[640])
+        quantize(0, 896, T, groups[896])
+
+        w_planes = lap.tile([P, E * PASSES, N], U8, name="w_planes", align_bytes=64, offset=0)
+        lifted = lap.tile([P, LAST * S], U8, name="lifted", align_bytes=64, offset=w_plane_bytes)
+        nc.gpsimd.memset(w_planes[:].rearrange("p g n -> p (g n)").bitcast(I32), 0)
+        nc.gpsimd.memset(lifted[:].bitcast(I32), 0)
+
+        def load_rest():
+            for r in range(SCALE_ROWS):
+                nc.sync.dma_start(
+                    w_planes[r:P:QUADRANT, :, :].bitcast(I32),
+                    w_scales.rearrange("e a (q r) n -> r q (e a) n", r=SCALE_ROWS)[r].bitcast(I32),
+                )
+            for e0 in range(0, E, W_EXPERTS):
+                nc.sync.dma_start(
+                    w_codes[:, e0 * PASSES:(e0 + W_EXPERTS) * PASSES, :].bitcast(I32),
+                    w_words[e0:e0 + W_EXPERTS].rearrange("e a p n -> p (e a) n").bitcast(I32),
+                )
+            nc.sync.dma_start(b_t[:], b)
+            for r in (1, 2):
+                nc.sync.dma_start(
+                    gate_rows[(r - 1) * LENT_BLOCKS:r * LENT_BLOCKS, :],
+                    gate[r, 0, OWN:].rearrange("(i p) -> i p", p=P),
+                )
+            for r, pos in reversed(list(enumerate((pos1, pos2, pos3)))):
+                nc.sync.dma_start(pos_t[r][:], pos)
 
         def gather_and_move_scales(h):
             nc.vector.tensor_copy(
@@ -130,55 +177,21 @@ def tile_moe_tk_lin_gelu_kernel(tc, xT, w_words, w_scales, b, gate, offs, pos1, 
             )
             for a in range(1, PASSES):
                 c0 = (a - 1) * S + h * CHUNK
-                nc.sync.dma_start(lifted[0:SHIFTED, c0:c0 + CHUNK].bitcast(I32), packed[h][4 * a:4 * a + SHIFTED, :].bitcast(I32))
+                shift = SCALE_ROWS * a
+                nc.sync.dma_start(lifted[0:SHIFTED, c0:c0 + CHUNK].bitcast(I32), packed[h][shift:shift + SHIFTED, :].bitcast(I32))
 
         def plane(a, s0, s1):
             if a == 0:
                 return packed[s0 // CHUNK][:, s0 % CHUNK:s0 % CHUNK + s1 - s0]
             return lifted[:, (a - 1) * S + s0:(a - 1) * S + s1]
 
-        def lay_out_head(copy, grouped, lo, c0, t0, t1):
-            lay_out(copy, grouped[:, t0 - lo:t1 - lo, :], pieces[(0, c0)][:, :, t0 - c0:t1 - c0])
-
-        grouped = {lo: stage.tile([P, hi - lo, PACK], BF16, name="head%d" % lo, align_bytes=64) for lo, hi in ((0, 256), (256, 512), (512, 640), (640, 896))}
-        grouped[896] = lap.tile([P, T - 896, PACK], BF16, name="head896", align_bytes=64, offset=E * PASSES * N - 512)
-        lay_out_head(nc.vector.tensor_copy, grouped[0], 0, 0, 0, 256)
-        lay_out_head(nc.scalar.copy, grouped[256], 256, 0, 256, 512)
-        quantize(0, 0, 256, grouped[0])
-        quantize(0, 256, 512, grouped[256])
-        lay_out_head(nc.scalar.copy, grouped[512], 512, 512, 512, 640)
-        lay_out_head(nc.scalar.copy, grouped[640], 640, 512, 640, 704)
-        lay_out_head(nc.vector.tensor_copy, grouped[640], 640, 512, 704, 896)
-        quantize(0, 512, 640, grouped[512])
-        lay_out_head(nc.vector.tensor_copy, grouped[896], 896, 896, 896, 960)
-        lay_out_head(nc.scalar.copy, grouped[896], 896, 896, 960, T)
-        quantize(0, 640, 896, grouped[640])
-        quantize(0, 896, T, grouped[896])
-        w_planes = lap.tile([P, E * PASSES, N], U8, name="w_planes", align_bytes=64, offset=0)
-        lifted = lap.tile([P, (PASSES - 1) * S], U8, name="lifted", align_bytes=64, offset=E * PASSES * N)
-        nc.gpsimd.memset(w_planes[:].rearrange("p g n -> p (g n)").bitcast(I32), 0)
-        nc.gpsimd.memset(lifted[:].bitcast(I32), 0)
-        for r in range(4):
-            nc.sync.dma_start(
-                w_planes[r:P:32, :, :].bitcast(I32),
-                w_scales.rearrange("e a (q r) n -> r q (e a) n", r=4)[r].bitcast(I32),
-            )
-        load_w(0, E // 2)
-        load_w(E // 2, E)
-        nc.sync.dma_start(b_t[:], b)
-        for r, pos in enumerate((pos1, pos2, pos3)):
-            nc.sync.dma_start(pos_t[r][:], pos)
-        for r in (1, 2):
-            nc.sync.dma_start(
-                gate_rows[(r - 1) * LENT_BLOCKS:r * LENT_BLOCKS, :],
-                gate[r, 0, OWN:].rearrange("(b p) -> b p", p=P),
-            )
-        gather_body(0, 0, S // 2, 2 * T)
-        gather_body(0, S // 2, BODY[0], 2 * T)
+        load_rest()
+        gather_body(0, 0, CHUNK, WIDE)
+        gather_body(0, CHUNK, BODY[0], WIDE)
         quantize_pass(1)
-        gather_body(1, 0, BODY[1], 4 * T)
+        gather_body(1, 0, BODY[1], 2 * WIDE)
         quantize_pass(2)
-        gather_body(2, 0, CHUNK, 2 * T)
+        gather_body(2, 0, CHUNK, WIDE)
         quantize_pass(3)
         for h in range(CHUNKS):
             gather_and_move_scales(h)
@@ -187,9 +200,10 @@ def tile_moe_tk_lin_gelu_kernel(tc, xT, w_words, w_scales, b, gate, offs, pos1, 
         nc.tensor.transpose(turned_rows[:], gate_rows[:], ident[:])
         nc.scalar.copy(out=gate_cols[:], in_=turned_rows[:, 0:2 * LENT_BLOCKS])
 
-        cuts = (0, 1536, 2048, 2560, 2816, 2944, S)
-        spans = [(s0, min(s0 + BANK, hi)) for lo, hi in zip(cuts, cuts[1:]) for s0 in range(lo, hi, BANK)]
+        spans = [(s0, min(s0 + BANK, hi)) for lo, hi in zip(CUTS, CUTS[1:]) for s0 in range(lo, hi, BANK)]
         acc = {span: psum.tile([P, span[1] - span[0]], F32, name="bank") for span in spans}
+        narrow = spans[-3:]
+        before_narrow = spans[-4]
 
         def by_expert(span):
             edges = sorted({span[0], span[1]} | {s0 for s0 in range(0, S, C) if span[0] < s0 < span[1]})
@@ -206,40 +220,40 @@ def tile_moe_tk_lin_gelu_kernel(tc, xT, w_words, w_scales, b, gate, offs, pos1, 
                     rhs=words.bitcast(FP8X4),
                     rhs_scale=plane(a, s0, s1),
                     start=(a == 0 and s0 == lo),
-                    stop=(a == PASSES - 1 and s1 == hi),
+                    stop=(a == LAST and s1 == hi),
                 )
 
         def close(span):
-            multiply(span, PASSES - 1)
+            multiply(span, LAST)
             for s0, s1, e in by_expert(span):
                 nc.scalar.activation(
                     out=y[:, s0:s1], in_=acc[span][:, s0 - span[0]:s1 - span[0]],
                     func=AF.Gelu_apprx_tanh, bias=b_t[:, e:e + 1],
                 )
 
-        late_codes[PASSES - 1] = keep.tile([P, LATE[3]], U32, name="late3", align_bytes=64)
-        for lo, hi in zip(cuts, cuts[1:]):
+        late_codes[LAST] = keep.tile([P, LATE[LAST]], U32, name="late3", align_bytes=64)
+        for lo, hi in zip(CUTS, CUTS[1:]):
             if lo == CHUNK:
-                gather_body(2, CHUNK, BODY[2], 4 * T)
+                gather_body(2, CHUNK, BODY[2], 2 * WIDE)
             if lo % CHUNK == 0:
-                for a in range(PASSES - 1):
+                for a in range(LAST):
                     for span in spans:
-                        if lo <= span[0] < lo + CHUNK and (a == 0 or span not in spans[-3:]):
+                        if lo <= span[0] < lo + CHUNK and (a == 0 or span not in narrow):
                             multiply(span, a)
-            if (lo, hi) == spans[-4]:
-                for a in (1, 2):
-                    for span in spans[-3:]:
+            if (lo, hi) == before_narrow:
+                for a in range(1, LAST):
+                    for span in narrow:
                         multiply(span, a)
-            if lo == BODY[3]:
-                gather_codes(3, late_codes[3][:], lo, hi - lo, T)
+            if lo == BODY[LAST]:
+                gather_codes(LAST, late_codes[LAST][:], lo, hi - lo, T)
             else:
-                gather_body(3, lo, hi, T if hi - lo < T else WIDE)
+                gather_body(LAST, lo, hi, T if hi - lo < T else WIDE)
             for span in spans:
                 if lo <= span[0] < hi:
                     close(span)
 
-        gates = keep.tile([P, 2 * OWN + T], F32, name="gates", tag="planes0_0", align_bytes=64)
-        nc.sync.dma_start(gates[:, 0:2 * OWN].rearrange("p (r t) -> p r t", r=2), gate[1:3, :, 0:OWN].rearrange("r p t -> p r t"))
+        gates = keep.tile([P, 2 * OWN + T], F32, name="gates", tag="packed0", align_bytes=64)
+        nc.sync.dma_start(gates[:, 0:2 * OWN].rearrange("p (r t) -> p r t", r=2), gate[1:TOP, :, 0:OWN].rearrange("r p t -> p r t"))
         nc.sync.dma_start(gates[:, 2 * OWN:], gate[0])
 
         def picked(r, t0, t1):
@@ -248,12 +262,16 @@ def tile_moe_tk_lin_gelu_kernel(tc, xT, w_words, w_scales, b, gate, offs, pos1, 
         def blk(i):
             return slice(i * P, (i + 1) * P)
 
+        def lent(i):
+            return OWN + i * P
+
         scaled = {(r, i): keep.tile([P, P], F32, name="scaled%d_%d" % (r, i)) for r in (1, 2) for i in range(LENT_BLOCKS)}
         prod = {r: keep.tile([P, OWN], F32, name="prod%d" % r) for r in (1, 2)}
         pair = keep.tile([P, OWN], F32, name="pair")
         prod0 = keep.tile([P, T - P], F32, name="prod0")
         result = raws.tile([P, T], F32, name="result", tag="raw0_0")
         turned = {}
+        sums = {}
 
         def product0(t0, t1):
             nc.vector.tensor_tensor(prod0[:, t0:t1], picked(0, t0, t1), gates[:, 2 * OWN + t0:2 * OWN + t1], MULT)
@@ -264,13 +282,11 @@ def tile_moe_tk_lin_gelu_kernel(tc, xT, w_words, w_scales, b, gate, offs, pos1, 
 
         def look_up(r, i0, i1, tag):
             plain = keep.tile([P, (i1 - i0) * P], F32, name="plain", tag=tag)
-            nc.scalar.activation(out=plain[:], in_=picked(r, OWN + i0 * P, OWN + i1 * P), func=AF.Copy)
+            nc.scalar.activation(out=plain[:], in_=picked(r, lent(i0), lent(i1)), func=AF.Copy)
             bank = psum.tile([P, (i1 - i0) * P], F32, name="bank")
             for i in range(i0, i1):
                 nc.tensor.transpose(bank[:, blk(i - i0)], plain[:, blk(i - i0)], ident[:])
                 turned[(r, i)] = bank[:, blk(i - i0)]
-
-        sums = {}
 
         def scale_and_add(r, i0, i1):
             if r == 1:
@@ -284,31 +300,30 @@ def tile_moe_tk_lin_gelu_kernel(tc, xT, w_words, w_scales, b, gate, offs, pos1, 
                     start=(r == 1 and i == i0), stop=(r == 2 and i == i1 - 1),
                 )
 
-        look_up(1, 0, 2, "plain_a")
-        look_up(2, 0, 2, "plain_b")
-        look_up(1, 2, 4, "plain_c")
+        early, final = 2, LENT_BLOCKS - 1
+        look_up(1, 0, early, "plain_a")
+        look_up(2, 0, early, "plain_b")
+        look_up(1, early, LENT_BLOCKS, "plain_c")
         for r in (1, 2):
-            scale_and_add(r, 0, 2)
-        look_up(2, 2, 4, "plain_b")
-        look_up(1, 4, 5, "plain_c")
-        look_up(2, 4, 5, "plain_a")
+            scale_and_add(r, 0, early)
+        look_up(2, early, final, "plain_b")
+        look_up(2, final, LENT_BLOCKS, "plain_c")
         for r in (1, 2):
-            for i in (2, 3):
+            for i in range(early, final):
                 scale_and_add(r, i, i + 1)
         for r in (1, 2):
-            scale_and_add(r, 4, 5)
+            scale_and_add(r, final, LENT_BLOCKS)
 
         for r in (1, 2):
             nc.vector.tensor_tensor(prod[r][:], picked(r, 0, OWN), gates[:, (r - 1) * OWN:r * OWN], MULT)
-        product0(0, OWN)
+        product0(0, lent(early))
         nc.vector.tensor_tensor(pair[:], prod[1][:], prod[2][:], ADD)
-        product0(OWN, OWN + 2 * P)
+        product0(lent(early), lent(final))
         finish(0, OWN, pair[:])
-        product0(OWN + 2 * P, OWN + 4 * P)
-        finish(OWN, OWN + 2 * P, sums[0][:])
-        prod_last = keep.tile([P, P], F32, name="prod_last", tag="scaled2_1")
-        nc.vector.tensor_tensor(prod_last[:], picked(0, T - P, T), gates[:, 2 * OWN + T - P:], MULT)
-        for i in (2, 3):
-            finish(OWN + i * P, OWN + (i + 1) * P, sums[i][:])
-        nc.vector.tensor_tensor(result[:, T - P:], sums[4][:], prod_last[:], ADD)
-        nc.sync.dma_start(out[:, T - P:], result[:, T - P:])
+        finish(OWN, lent(early), sums[0][:])
+        prod_last = keep.tile([P, P], F32, name="prod_last", tag="scaled2_%d" % (early - 1))
+        nc.vector.tensor_tensor(prod_last[:], picked(0, lent(final), T), gates[:, 2 * OWN + lent(final):], MULT)
+        for i in range(early, final):
+            finish(lent(i), lent(i + 1), sums[i][:])
+        nc.vector.tensor_tensor(result[:, lent(final):], sums[final][:], prod_last[:], ADD)
+        nc.sync.dma_start(out[:, lent(final):], result[:, lent(final):])

@@ -40,7 +40,6 @@ BODY = {a: S - n for a, n in LATE.items()}
 HEAD = ((0, 512), (512, 896), (896, T))
 LATER = ((0, 384), (640, T), (384, 640))
 CUTS = (0, 1536, 2048, 2560, 2816, 2944, S)
-W_EXPERTS = 3
 OWN = 384
 LENT = T - OWN
 LENT_BLOCKS = LENT // P
@@ -156,10 +155,10 @@ def tile_moe_tk_lin_gelu_kernel(tc, xT, w_words, w_scales, b, gate, offs, pos1, 
                     w_planes[r:P:QUADRANT, :, :].bitcast(I32),
                     w_scales.rearrange("e a (q r) n -> r q (e a) n", r=SCALE_ROWS)[r].bitcast(I32),
                 )
-            for e0 in range(0, E, W_EXPERTS):
+            for e in range(E):
                 nc.sync.dma_start(
-                    w_codes[:, e0 * PASSES:(e0 + W_EXPERTS) * PASSES, :].bitcast(I32),
-                    w_words[e0:e0 + W_EXPERTS].rearrange("e a p n -> p (e a) n").bitcast(I32),
+                    w_codes[:, e * PASSES:(e + 1) * PASSES, :].bitcast(I32),
+                    w_words[e].rearrange("a p n -> p a n").bitcast(I32),
                 )
             nc.sync.dma_start(b_t[:], b)
             for r in (1, 2):

@@ -69,12 +69,13 @@ def tile_moe_tk_lin_gelu_kernel(tc, xT, w_words, w_scales, b, gate, offs, pos1, 
         warm = keep.tile([P, 1], F32, name="warm")
         warm_out = keep.tile([P, 1], F32, name="warm_out")
 
-        nc.gpsimd.memset(warm[:], 0.0)
+        nc.vector.memset(warm[:], 0.0)
         nc.scalar.activation(out=warm_out[:], in_=warm[:], func=AF.Gelu_apprx_tanh)
         ident = keep.tile([P, P], F32, name="ident")
         make_identity(nc, ident[:])
         nc.vector.memset(x_scales[:].bitcast(I32), 0)
-        nc.vector.memset(codes[:, first_word[LAST]:], 0)
+        nc.vector.memset(codes[:, first_word[LAST]:first_word[LAST] + T], 0)
+        nc.vector.memset(codes[:, first_word[LAST] + T:], 0)
 
         gate_rows = keep.tile([P, P], F32, name="gate_rows")
         gate_cols = keep.tile([P, 2 * LENT_BLOCKS], F32, name="gate_cols")
@@ -116,8 +117,11 @@ def tile_moe_tk_lin_gelu_kernel(tc, xT, w_words, w_scales, b, gate, offs, pos1, 
             across = pieces[(a, c0)]
             lay_out(nc.scalar.copy, halves[0][:, a0:a1, :], pieces[(a, a0)][:])
             lay_out(nc.scalar.copy, halves[1][:, b0 - HALF:b1 - HALF, :], pieces[(a, b0)][:])
+            mid = (HALF + c1) // 2 if a == 1 else HALF
+            if mid > HALF:
+                lay_out(nc.scalar.copy, halves[1][:, 0:mid - HALF, :], across[:, :, HALF - c0:mid - c0])
             lay_out(nc.scalar.copy, halves[0][:, c0:HALF, :], across[:, :, 0:HALF - c0])
-            lay_out(nc.scalar.copy, halves[1][:, 0:c1 - HALF, :], across[:, :, HALF - c0:c1 - c0])
+            lay_out(nc.scalar.copy, halves[1][:, mid - HALF:c1 - HALF, :], across[:, :, mid - c0:c1 - c0])
             for h in range(2):
                 quantize(a, h * HALF, (h + 1) * HALF, halves[h])
             late_codes[a - 1] = stage.tile([P, LATE[a - 1]], U32, name="late%d" % (a - 1), tag="half%d_0" % a, align_bytes=64)
@@ -166,7 +170,7 @@ def tile_moe_tk_lin_gelu_kernel(tc, xT, w_words, w_scales, b, gate, offs, pos1, 
                     gate_rows[(r - 1) * LENT_BLOCKS:r * LENT_BLOCKS, :],
                     gate[r, 0, OWN:].rearrange("(i p) -> i p", p=P),
                 )
-            for r, pos in reversed(list(enumerate((pos1, pos2, pos3)))):
+            for r, pos in enumerate((pos1, pos2, pos3)):
                 nc.sync.dma_start(pos_t[r][:], pos)
 
         def gather_and_move_scales(h):

@@ -69,13 +69,12 @@ def tile_moe_tk_lin_gelu_kernel(tc, xT, w_words, w_scales, b, gate, offs, pos1, 
         warm = keep.tile([P, 1], F32, name="warm")
         warm_out = keep.tile([P, 1], F32, name="warm_out")
 
-        nc.vector.memset(warm[:], 0.0)
+        nc.gpsimd.memset(warm[:], 0.0)
         nc.scalar.activation(out=warm_out[:], in_=warm[:], func=AF.Gelu_apprx_tanh)
         ident = keep.tile([P, P], F32, name="ident")
         make_identity(nc, ident[:])
         nc.vector.memset(x_scales[:].bitcast(I32), 0)
-        nc.vector.memset(codes[:, first_word[LAST]:first_word[LAST] + T], 0)
-        nc.vector.memset(codes[:, first_word[LAST] + T:], 0)
+        nc.vector.memset(codes[:, first_word[LAST]:], 0)
 
         gate_rows = keep.tile([P, P], F32, name="gate_rows")
         gate_cols = keep.tile([P, 2 * LENT_BLOCKS], F32, name="gate_cols")
@@ -319,10 +318,11 @@ def tile_moe_tk_lin_gelu_kernel(tc, xT, w_words, w_scales, b, gate, offs, pos1, 
 
         for r in (1, 2):
             nc.vector.tensor_tensor(prod[r][:], picked(r, 0, OWN), gates[:, (r - 1) * OWN:r * OWN], MULT)
-        product0(0, lent(early))
+        product0(0, OWN)
         nc.vector.tensor_tensor(pair[:], prod[1][:], prod[2][:], ADD)
-        product0(lent(early), lent(final))
+        product0(OWN, lent(early))
         finish(0, OWN, pair[:])
+        product0(lent(early), lent(final))
         finish(OWN, lent(early), sums[0][:])
         prod_last = keep.tile([P, P], F32, name="prod_last", tag="scaled2_%d" % (early - 1))
         nc.vector.tensor_tensor(prod_last[:], picked(0, lent(final), T), gates[:, 2 * OWN + lent(final):], MULT)

@@ -35,11 +35,15 @@ CHUNKS = S // CHUNK
 WIDE = 2 * T
 SHIFTED = 112
 HALF = T // 2
+QUARTER = T // 4
+COPY = {1: QUARTER, 2: 64, 3: 64}
+ZERO = 80
 LATE = {0: 128, 1: 1024, 2: 128, 3: 128}
 BODY = {a: S - n for a, n in LATE.items()}
 HEAD = ((0, 512), (512, 896), (896, T))
-LATER = ((0, 384), (640, T), (384, 640))
+LATER = tuple((c0, c0 + QUARTER) for c0 in range(0, T, QUARTER))
 CUTS = (0, 1536, 2048, 2560, 2816, 2944, S)
+W_LOAD = 6
 OWN = 384
 LENT = T - OWN
 LENT_BLOCKS = LENT // P
@@ -73,8 +77,9 @@ def tile_moe_tk_lin_gelu_kernel(tc, xT, w_words, w_scales, b, gate, offs, pos1, 
         nc.scalar.activation(out=warm_out[:], in_=warm[:], func=AF.Gelu_apprx_tanh)
         ident = keep.tile([P, P], F32, name="ident")
         make_identity(nc, ident[:])
-        nc.vector.memset(x_scales[:].bitcast(I32), 0)
-        nc.vector.memset(codes[:, first_word[LAST]:], 0)
+        for words in (x_scales[:].bitcast(I32), codes[:, first_word[LAST]:]):
+            for c0 in range(0, words.shape[1], ZERO):
+                nc.vector.memset(words[:, c0:min(c0 + ZERO, words.shape[1])], 0)
 
         gate_rows = keep.tile([P, P], F32, name="gate_rows")
         gate_cols = keep.tile([P, 2 * LENT_BLOCKS], F32, name="gate_cols")
@@ -83,7 +88,7 @@ def tile_moe_tk_lin_gelu_kernel(tc, xT, w_words, w_scales, b, gate, offs, pos1, 
 
         def load_pass(a, ranges):
             for c0, c1 in ranges:
-                raw = raws.tile([P, PACK, c1 - c0], F32, name="raw%d_%d" % (a, c0))
+                raw = raws.tile([P, PACK, c1 - c0], F32, name="raw%d_%d" % (a, c0), align_bytes=64)
                 rows = xT[a * K_PASS:(a + 1) * K_PASS, c0:c1]
                 nc.sync.dma_start(raw[:], rows.rearrange("(p j) w -> p j w", j=PACK))
                 pieces[(a, c0)] = raw
@@ -112,18 +117,12 @@ def tile_moe_tk_lin_gelu_kernel(tc, xT, w_words, w_scales, b, gate, offs, pos1, 
 
         def quantize_pass(a):
             halves = [stage.tile([P, HALF, PACK], BF16, name="half%d_%d" % (a, h), align_bytes=64) for h in range(2)]
-            (a0, a1), (b0, b1), (c0, c1) = LATER
-            across = pieces[(a, c0)]
-            lay_out(nc.scalar.copy, halves[0][:, a0:a1, :], pieces[(a, a0)][:])
-            lay_out(nc.scalar.copy, halves[1][:, b0 - HALF:b1 - HALF, :], pieces[(a, b0)][:])
-            mid = (HALF + c1) // 2 if a == 1 else HALF
-            if mid > HALF:
-                lay_out(nc.scalar.copy, halves[1][:, 0:mid - HALF, :], across[:, :, HALF - c0:mid - c0])
-            lay_out(nc.scalar.copy, halves[0][:, c0:HALF, :], across[:, :, 0:HALF - c0])
-            lay_out(nc.scalar.copy, halves[1][:, mid - HALF:c1 - HALF, :], across[:, :, mid - c0:c1 - c0])
+            for t0 in range(0, T, COPY[a]):
+                c0 = t0 - t0 % QUARTER
+                lay_out(nc.scalar.copy, halves[t0 // HALF][:, t0 % HALF:t0 % HALF + COPY[a], :], pieces[(a, c0)][:, :, t0 - c0:t0 - c0 + COPY[a]])
             for h in range(2):
                 quantize(a, h * HALF, (h + 1) * HALF, halves[h])
-            late_codes[a - 1] = stage.tile([P, LATE[a - 1]], U32, name="late%d" % (a - 1), tag="half%d_0" % a, align_bytes=64)
+            late_codes[a - 1] = raws.tile([P, LATE[a - 1]], U32, name="late%d" % (a - 1), tag="raw%d_%d" % (a, T - QUARTER), align_bytes=64)
             gather_codes(a - 1, late_codes[a - 1][:], BODY[a - 1], LATE[a - 1], T if LATE[a - 1] < T else WIDE)
 
         groups = {lo: stage.tile([P, hi - lo, PACK], BF16, name="head%d" % lo, align_bytes=64) for lo, hi in ((0, 256), (256, 512), (512, 640), (640, 896))}
@@ -158,10 +157,10 @@ def tile_moe_tk_lin_gelu_kernel(tc, xT, w_words, w_scales, b, gate, offs, pos1, 
                     w_planes[r:P:QUADRANT, :, :].bitcast(I32),
                     w_scales.rearrange("e a (q r) n -> r q (e a) n", r=SCALE_ROWS)[r].bitcast(I32),
                 )
-            for e in range(E):
+            for g0 in range(0, E * PASSES, W_LOAD):
                 nc.sync.dma_start(
-                    w_codes[:, e * PASSES:(e + 1) * PASSES, :].bitcast(I32),
-                    w_words[e].rearrange("a p n -> p a n").bitcast(I32),
+                    w_codes[:, g0:g0 + W_LOAD, :].bitcast(I32),
+                    w_words.rearrange("e a p n -> p (e a) n")[:, g0:g0 + W_LOAD, :].bitcast(I32),
                 )
             nc.sync.dma_start(b_t[:], b)
             for r in (1, 2):
@@ -200,7 +199,8 @@ def tile_moe_tk_lin_gelu_kernel(tc, xT, w_words, w_scales, b, gate, offs, pos1, 
 
         turned_rows = psum.tile([P, P], F32, name="bank")
         nc.tensor.transpose(turned_rows[:], gate_rows[:], ident[:])
-        nc.scalar.copy(out=gate_cols[:], in_=turned_rows[:, 0:2 * LENT_BLOCKS])
+        for col in range(2 * LENT_BLOCKS):
+            nc.scalar.copy(out=gate_cols[:, col:col + 1], in_=turned_rows[:, col:col + 1])
 
         spans = [(s0, min(s0 + BANK, hi)) for lo, hi in zip(CUTS, CUTS[1:]) for s0 in range(lo, hi, BANK)]
         acc = {span: psum.tile([P, span[1] - span[0]], F32, name="bank") for span in spans}
@@ -255,7 +255,8 @@ def tile_moe_tk_lin_gelu_kernel(tc, xT, w_words, w_scales, b, gate, offs, pos1, 
                     close(span)
 
         gates = keep.tile([P, 2 * OWN + T], F32, name="gates", tag="packed0", align_bytes=64)
-        nc.sync.dma_start(gates[:, 0:2 * OWN].rearrange("p (r t) -> p r t", r=2), gate[1:TOP, :, 0:OWN].rearrange("r p t -> p r t"))
+        for r in (1, 2):
+            nc.sync.dma_start(gates[:, (r - 1) * OWN:r * OWN], gate[r, :, 0:OWN])
         nc.sync.dma_start(gates[:, 2 * OWN:], gate[0])
 
         def picked(r, t0, t1):
@@ -271,7 +272,7 @@ def tile_moe_tk_lin_gelu_kernel(tc, xT, w_words, w_scales, b, gate, offs, pos1, 
         prod = {r: keep.tile([P, OWN], F32, name="prod%d" % r) for r in (1, 2)}
         pair = keep.tile([P, OWN], F32, name="pair")
         prod0 = keep.tile([P, T - P], F32, name="prod0")
-        result = raws.tile([P, T], F32, name="result", tag="raw0_0")
+        result = raws.tile([P, T], F32, name="result", tag="raw0_0", align_bytes=64)
         turned = {}
         sums = {}
 

@@ -137,12 +137,12 @@ def tile_moe_tk_lin_gelu_kernel(tc, xT, w_words, w_scales, b, gate, offs, pos1, 
         lay_out_head(nc.scalar.copy, 256, 0, 256, 512)
         quantize(0, 0, 256, groups[0])
         quantize(0, 256, 512, groups[256])
-        lay_out_head(nc.scalar.copy, 512, 512, 512, 640)
-        lay_out_head(nc.scalar.copy, 640, 512, 640, 704)
-        lay_out_head(nc.vector.tensor_copy, 640, 512, 704, 896)
+        lay_out_head(nc.vector.tensor_copy, 512, 512, 512, 640)
+        lay_out_head(nc.vector.tensor_copy, 640, 512, 640, 768)
+        lay_out_head(nc.scalar.copy, 640, 512, 768, 896)
         quantize(0, 512, 640, groups[512])
-        lay_out_head(nc.vector.tensor_copy, 896, 896, 896, 960)
-        lay_out_head(nc.scalar.copy, 896, 896, 960, T)
+        lay_out_head(nc.vector.tensor_copy, 896, 896, 896, 992)
+        lay_out_head(nc.scalar.copy, 896, 896, 992, T)
         quantize(0, 640, 896, groups[640])
         quantize(0, 896, T, groups[896])
 

@@ -40,7 +40,8 @@ COPY = {1: QUARTER, 2: 64, 3: 64}
 ZERO = 80
 LATE = {0: 128, 1: 1024, 2: 128, 3: 128}
 BODY = {a: S - n for a, n in LATE.items()}
-HEAD = ((0, 512), (512, 896), (896, T))
+HEAD = ((0, 512), (512, 768), (768, T))
+DMA_ALIGN = 256
 LATER = tuple((c0, c0 + QUARTER) for c0 in range(0, T, QUARTER))
 CUTS = (0, 1536, 2048, 2560, 2816, 2944, S)
 W_LOAD = 6
@@ -67,7 +68,7 @@ def tile_moe_tk_lin_gelu_kernel(tc, xT, w_words, w_scales, b, gate, offs, pos1, 
         slot_codes = [keep.tile([P, BODY[a]], U32, name="slot_codes%d" % a, align_bytes=64) for a in range(PASSES)]
         late_codes = {}
         packed = [keep.tile([P, CHUNK], U8, name="packed%d" % h, align_bytes=64) for h in range(CHUNKS)]
-        w_codes = keep.tile([P, E * PASSES, 2 * N], U8, name="w_codes", align_bytes=64)
+        w_codes = keep.tile([P, E * PASSES, 2 * N], U8, name="w_codes", align_bytes=DMA_ALIGN)
         b_t = keep.tile([P, E], F32, name="b_t")
         y = keep.tile([P, S], F32, name="y")
         warm = keep.tile([P, 1], F32, name="warm")
@@ -88,12 +89,18 @@ def tile_moe_tk_lin_gelu_kernel(tc, xT, w_words, w_scales, b, gate, offs, pos1, 
 
         def load_pass(a, ranges):
             for c0, c1 in ranges:
-                raw = raws.tile([P, PACK, c1 - c0], F32, name="raw%d_%d" % (a, c0), align_bytes=64)
+                raw = raws.tile([P, PACK, c1 - c0], F32, name="raw%d_%d" % (a, c0), align_bytes=DMA_ALIGN)
                 rows = xT[a * K_PASS:(a + 1) * K_PASS, c0:c1]
                 nc.sync.dma_start(raw[:], rows.rearrange("(p j) w -> p j w", j=PACK))
                 pieces[(a, c0)] = raw
 
-        load_pass(0, HEAD)
+        rows0 = xT[0:K_PASS, :].rearrange("(p j) w -> p j w", j=PACK)
+        low_rows = raws.tile([P, 2, T], F32, name="raw0_0", align_bytes=DMA_ALIGN)
+        nc.sync.dma_start(low_rows[:], rows0[:, 0:2, :])
+        high_rows = {}
+        for c0, c1 in HEAD:
+            high_rows[c0] = raws.tile([P, 2, c1 - c0], F32, name="high%d" % c0, align_bytes=DMA_ALIGN)
+            nc.sync.dma_start(high_rows[c0][:], rows0[:, 2:PACK, c0:c1])
         nc.sync.dma_start(offs_t[:], offs)
         for a in range(1, PASSES):
             load_pass(a, LATER)
@@ -105,7 +112,7 @@ def tile_moe_tk_lin_gelu_kernel(tc, xT, w_words, w_scales, b, gate, offs, pos1, 
             nc.vector.quantize_mx(
                 out=codes[:, first_word[a] + lo:first_word[a] + hi].bitcast(FP8X4),
                 scales=x_scales[SCALE_ROWS * a:P, lo:hi],
-                in_=grouped[:].rearrange("p w j -> p (w j)"),
+                in_=grouped.rearrange("p w j -> p (w j)"),
             )
 
         def gather_codes(a, dst, s0, n, window):
@@ -121,30 +128,44 @@ def tile_moe_tk_lin_gelu_kernel(tc, xT, w_words, w_scales, b, gate, offs, pos1, 
                 c0 = t0 - t0 % QUARTER
                 lay_out(nc.scalar.copy, halves[t0 // HALF][:, t0 % HALF:t0 % HALF + COPY[a], :], pieces[(a, c0)][:, :, t0 - c0:t0 - c0 + COPY[a]])
             for h in range(2):
-                quantize(a, h * HALF, (h + 1) * HALF, halves[h])
-            late_codes[a - 1] = raws.tile([P, LATE[a - 1]], U32, name="late%d" % (a - 1), tag="raw%d_%d" % (a, T - QUARTER), align_bytes=64)
+                quantize(a, h * HALF, (h + 1) * HALF, halves[h][:])
+            late_codes[a - 1] = raws.tile([P, LATE[a - 1]], U32, name="late%d" % (a - 1), tag="raw%d_%d" % (a, T - QUARTER), align_bytes=DMA_ALIGN)
             gather_codes(a - 1, late_codes[a - 1][:], BODY[a - 1], LATE[a - 1], T if LATE[a - 1] < T else WIDE)
 
-        groups = {lo: stage.tile([P, hi - lo, PACK], BF16, name="head%d" % lo, align_bytes=64) for lo, hi in ((0, 256), (256, 512), (512, 640), (640, 896))}
         w_plane_bytes = E * PASSES * N
         last_lo = HEAD[-1][0]
-        groups[last_lo] = lap.tile([P, T - last_lo, PACK], BF16, name="head_last", align_bytes=64, offset=w_plane_bytes - (T - last_lo) * PACK)
+        early_tokens = stage.tile([P, last_lo, PACK], BF16, name="early_tokens", align_bytes=64)
+        last_tokens = lap.tile([P, T - last_lo, PACK], BF16, name="last_tokens", align_bytes=64, offset=w_plane_bytes - (T - last_lo) * PACK)
 
-        def lay_out_head(copy, lo, c0, t0, t1):
-            lay_out(copy, groups[lo][:, t0 - lo:t1 - lo, :], pieces[(0, c0)][:, :, t0 - c0:t1 - c0])
+        def grouped0(t0, t1):
+            return early_tokens[:, t0:t1, :] if t0 < last_lo else last_tokens[:, t0 - last_lo:t1 - last_lo, :]
 
-        lay_out_head(nc.vector.tensor_copy, 0, 0, 0, 256)
-        lay_out_head(nc.scalar.copy, 256, 0, 256, 512)
-        quantize(0, 0, 256, groups[0])
-        quantize(0, 256, 512, groups[256])
-        lay_out_head(nc.vector.tensor_copy, 512, 512, 512, 640)
-        lay_out_head(nc.vector.tensor_copy, 640, 512, 640, 768)
-        lay_out_head(nc.scalar.copy, 640, 512, 768, 896)
-        quantize(0, 512, 640, groups[512])
-        lay_out_head(nc.vector.tensor_copy, 896, 896, 896, 992)
-        lay_out_head(nc.scalar.copy, 896, 896, 992, T)
-        quantize(0, 640, 896, groups[640])
-        quantize(0, 896, T, groups[896])
+        def low_half(copy, t0, t1):
+            copy(out=grouped0(t0, t1)[:, :, 0:2], in_=low_rows[:, :, t0:t1].rearrange("p j w -> p w j"))
+
+        def high_half(copy, t0, t1):
+            c0 = max(c for c in high_rows if c <= t0)
+            copy(out=grouped0(t0, t1)[:, :, 2:PACK], in_=high_rows[c0][:, :, t0 - c0:t1 - c0].rearrange("p j w -> p w j"))
+
+        def quantize0(t0, t1):
+            quantize(0, t0, t1, grouped0(t0, t1))
+
+        low_half(nc.vector.tensor_copy, 0, 512)
+        low_half(nc.scalar.copy, 512, 768)
+        low_half(nc.scalar.copy, 768, 864)
+        low_half(nc.vector.tensor_copy, 864, T)
+        high_half(nc.vector.tensor_copy, 0, 128)
+        high_half(nc.vector.tensor_copy, 128, 256)
+        high_half(nc.scalar.copy, 256, 512)
+        quantize0(0, 128)
+        high_half(nc.vector.tensor_copy, 512, 640)
+        high_half(nc.scalar.copy, 640, 768)
+        quantize0(128, 256)
+        quantize0(256, 512)
+        high_half(nc.vector.tensor_copy, 768, 896)
+        high_half(nc.scalar.copy, 896, T)
+        quantize0(512, 768)
+        quantize0(768, T)
 
         w_planes = lap.tile([P, E * PASSES, N], U8, name="w_planes", align_bytes=64, offset=0)
         lifted = lap.tile([P, LAST * S], U8, name="lifted", align_bytes=64, offset=w_plane_bytes)
@@ -255,8 +276,7 @@ def tile_moe_tk_lin_gelu_kernel(tc, xT, w_words, w_scales, b, gate, offs, pos1, 
                     close(span)
 
         gates = keep.tile([P, 2 * OWN + T], F32, name="gates", tag="packed0", align_bytes=64)
-        for r in (1, 2):
-            nc.sync.dma_start(gates[:, (r - 1) * OWN:r * OWN], gate[r, :, 0:OWN])
+        nc.sync.dma_start(gates[:, 0:2 * OWN].rearrange("p (r t) -> p r t", r=2), gate[1:TOP, :, 0:OWN].rearrange("r p t -> p r t"))
         nc.sync.dma_start(gates[:, 2 * OWN:], gate[0])
 
         def picked(r, t0, t1):
@@ -272,7 +292,7 @@ def tile_moe_tk_lin_gelu_kernel(tc, xT, w_words, w_scales, b, gate, offs, pos1, 
         prod = {r: keep.tile([P, OWN], F32, name="prod%d" % r) for r in (1, 2)}
         pair = keep.tile([P, OWN], F32, name="pair")
         prod0 = keep.tile([P, T - P], F32, name="prod0")
-        result = raws.tile([P, T], F32, name="result", tag="raw0_0", align_bytes=64)
+        result = raws.tile([P, T], F32, name="result", tag="raw0_0", align_bytes=DMA_ALIGN)
         turned = {}
         sums = {}
 

@@ -40,7 +40,8 @@ COPY = {1: QUARTER, 2: 64, 3: 64}
 ZERO = 80
 LATE = {0: 128, 1: 1024, 2: 128, 3: 128}
 BODY = {a: S - n for a, n in LATE.items()}
-HEAD = ((0, 512), (512, 768), (768, T))
+HEAD = ((0, 384), (384, 640), (640, 896), (896, T))
+HEAD_ON_VECTOR = (256, 160, 144, 72)
 DMA_ALIGN = 256
 LATER = tuple((c0, c0 + QUARTER) for c0 in range(0, T, QUARTER))
 CUTS = (0, 1536, 2048, 2560, 2816, 2944, S)
@@ -94,13 +95,7 @@ def tile_moe_tk_lin_gelu_kernel(tc, xT, w_words, w_scales, b, gate, offs, pos1, 
                 nc.sync.dma_start(raw[:], rows.rearrange("(p j) w -> p j w", j=PACK))
                 pieces[(a, c0)] = raw
 
-        rows0 = xT[0:K_PASS, :].rearrange("(p j) w -> p j w", j=PACK)
-        low_rows = raws.tile([P, 2, T], F32, name="raw0_0", align_bytes=DMA_ALIGN)
-        nc.sync.dma_start(low_rows[:], rows0[:, 0:2, :])
-        high_rows = {}
-        for c0, c1 in HEAD:
-            high_rows[c0] = raws.tile([P, 2, c1 - c0], F32, name="high%d" % c0, align_bytes=DMA_ALIGN)
-            nc.sync.dma_start(high_rows[c0][:], rows0[:, 2:PACK, c0:c1])
+        load_pass(0, HEAD)
         nc.sync.dma_start(offs_t[:], offs)
         for a in range(1, PASSES):
             load_pass(a, LATER)
@@ -132,40 +127,23 @@ def tile_moe_tk_lin_gelu_kernel(tc, xT, w_words, w_scales, b, gate, offs, pos1, 
             late_codes[a - 1] = raws.tile([P, LATE[a - 1]], U32, name="late%d" % (a - 1), tag="raw%d_%d" % (a, T - QUARTER), align_bytes=DMA_ALIGN)
             gather_codes(a - 1, late_codes[a - 1][:], BODY[a - 1], LATE[a - 1], T if LATE[a - 1] < T else WIDE)
 
+        groups = {lo: stage.tile([P, hi - lo, PACK], BF16, name="head%d" % lo, align_bytes=64) for lo, hi in HEAD[:-1]}
         w_plane_bytes = E * PASSES * N
         last_lo = HEAD[-1][0]
-        early_tokens = stage.tile([P, last_lo, PACK], BF16, name="early_tokens", align_bytes=64)
-        last_tokens = lap.tile([P, T - last_lo, PACK], BF16, name="last_tokens", align_bytes=64, offset=w_plane_bytes - (T - last_lo) * PACK)
+        groups[last_lo] = lap.tile([P, T - last_lo, PACK], BF16, name="head_last", align_bytes=64, offset=w_plane_bytes - (T - last_lo) * PACK)
 
-        def grouped0(t0, t1):
-            return early_tokens[:, t0:t1, :] if t0 < last_lo else last_tokens[:, t0 - last_lo:t1 - last_lo, :]
+        def lay_out_piece(i):
+            (lo, hi), n = HEAD[i], HEAD_ON_VECTOR[i]
+            lay_out(nc.vector.tensor_copy, groups[lo][:, 0:n, :], pieces[(0, lo)][:, :, 0:n])
+            lay_out(nc.scalar.copy, groups[lo][:, n:, :], pieces[(0, lo)][:, :, n:])
 
-        def low_half(copy, t0, t1):
-            copy(out=grouped0(t0, t1)[:, :, 0:2], in_=low_rows[:, :, t0:t1].rearrange("p j w -> p w j"))
-
-        def high_half(copy, t0, t1):
-            c0 = max(c for c in high_rows if c <= t0)
-            copy(out=grouped0(t0, t1)[:, :, 2:PACK], in_=high_rows[c0][:, :, t0 - c0:t1 - c0].rearrange("p j w -> p w j"))
-
-        def quantize0(t0, t1):
-            quantize(0, t0, t1, grouped0(t0, t1))
-
-        low_half(nc.vector.tensor_copy, 0, 512)
-        low_half(nc.scalar.copy, 512, 768)
-        low_half(nc.scalar.copy, 768, 864)
-        low_half(nc.vector.tensor_copy, 864, T)
-        high_half(nc.vector.tensor_copy, 0, 128)
-        high_half(nc.vector.tensor_copy, 128, 256)
-        high_half(nc.scalar.copy, 256, 512)
-        quantize0(0, 128)
-        high_half(nc.vector.tensor_copy, 512, 640)
-        high_half(nc.scalar.copy, 640, 768)
-        quantize0(128, 256)
-        quantize0(256, 512)
-        high_half(nc.vector.tensor_copy, 768, 896)
-        high_half(nc.scalar.copy, 896, T)
-        quantize0(512, 768)
-        quantize0(768, T)
+        for i, (lo, hi) in enumerate(HEAD[:-2]):
+            lay_out_piece(i)
+            quantize(0, lo, hi, groups[lo][:])
+        lay_out_piece(len(HEAD) - 2)
+        lay_out_piece(len(HEAD) - 1)
+        for lo, hi in HEAD[-2:]:
+            quantize(0, lo, hi, groups[lo][:])
 
         w_planes = lap.tile([P, E * PASSES, N], U8, name="w_planes", align_bytes=64, offset=0)
         lifted = lap.tile([P, LAST * S], U8, name="lifted", align_bytes=64, offset=w_plane_bytes)

@@ -41,7 +41,8 @@ ZERO = 80
 LATE = {0: 128, 1: 1024, 2: 128, 3: 128}
 BODY = {a: S - n for a, n in LATE.items()}
 HEAD = ((0, 384), (384, 640), (640, 896), (896, T))
-HEAD_ON_VECTOR = (256, 160, 144, 72)
+SHIFT = {0: 4, 1: 8, 2: 12, 3: 0}
+HEAD_ON_VECTOR = (256, 128, 144, 72)
 DMA_ALIGN = 256
 LATER = tuple((c0, c0 + QUARTER) for c0 in range(0, T, QUARTER))
 CUTS = (0, 1536, 2048, 2560, 2816, 2944, S)
@@ -59,6 +60,7 @@ def tile_moe_tk_lin_gelu_kernel(tc, xT, w_words, w_scales, b, gate, offs, pos1, 
         raws = ctx.enter_context(tc.tile_pool(name="raws", bufs=1))
         stage = ctx.enter_context(tc.tile_pool(name="stage", bufs=1))
         lap = ctx.enter_context(tc.tile_pool(name="lap", bufs=1))
+        plains = ctx.enter_context(tc.tile_pool(name="plains", bufs=1))
         psum = ctx.enter_context(tc.psum_pool(name="psum", bufs=BANKS))
 
         offs_t = lists.tile([P, S // LIST], U16, name="offs_t")
@@ -106,7 +108,7 @@ def tile_moe_tk_lin_gelu_kernel(tc, xT, w_words, w_scales, b, gate, offs, pos1, 
         def quantize(a, lo, hi, grouped):
             nc.vector.quantize_mx(
                 out=codes[:, first_word[a] + lo:first_word[a] + hi].bitcast(FP8X4),
-                scales=x_scales[SCALE_ROWS * a:P, lo:hi],
+                scales=x_scales[SHIFT[a]:P, lo:hi],
                 in_=grouped.rearrange("p w j -> p (w j)"),
             )
 
@@ -118,12 +120,13 @@ def tile_moe_tk_lin_gelu_kernel(tc, xT, w_words, w_scales, b, gate, offs, pos1, 
             gather_codes(a, slot_codes[a][:, s0:s1], s0, s1 - s0, window)
 
         def quantize_pass(a):
-            halves = [stage.tile([P, HALF, PACK], BF16, name="half%d_%d" % (a, h), align_bytes=64) for h in range(2)]
+            call = HALF if SHIFT[a] else T
+            parts = [stage.tile([P, call, PACK], BF16, name="part%d_%d" % (a, h), align_bytes=64) for h in range(T // call)]
             for t0 in range(0, T, COPY[a]):
                 c0 = t0 - t0 % QUARTER
-                lay_out(nc.scalar.copy, halves[t0 // HALF][:, t0 % HALF:t0 % HALF + COPY[a], :], pieces[(a, c0)][:, :, t0 - c0:t0 - c0 + COPY[a]])
-            for h in range(2):
-                quantize(a, h * HALF, (h + 1) * HALF, halves[h][:])
+                lay_out(nc.scalar.copy, parts[t0 // call][:, t0 % call:t0 % call + COPY[a], :], pieces[(a, c0)][:, :, t0 - c0:t0 - c0 + COPY[a]])
+            for h, part in enumerate(parts):
+                quantize(a, h * call, (h + 1) * call, part[:])
             late_codes[a - 1] = raws.tile([P, LATE[a - 1]], U32, name="late%d" % (a - 1), tag="raw%d_%d" % (a, T - QUARTER), align_bytes=DMA_ALIGN)
             gather_codes(a - 1, late_codes[a - 1][:], BODY[a - 1], LATE[a - 1], T if LATE[a - 1] < T else WIDE)
 
@@ -139,7 +142,9 @@ def tile_moe_tk_lin_gelu_kernel(tc, xT, w_words, w_scales, b, gate, offs, pos1, 
 
         for i, (lo, hi) in enumerate(HEAD[:-2]):
             lay_out_piece(i)
-            quantize(0, lo, hi, groups[lo][:])
+            n = HEAD_ON_VECTOR[i]
+            quantize(0, lo, lo + n, groups[lo][:, 0:n, :])
+            quantize(0, lo + n, hi, groups[lo][:, n:, :])
         lay_out_piece(len(HEAD) - 2)
         lay_out_piece(len(HEAD) - 1)
         for lo, hi in HEAD[-2:]:
@@ -175,15 +180,14 @@ def tile_moe_tk_lin_gelu_kernel(tc, xT, w_words, w_scales, b, gate, offs, pos1, 
                 out=packed[h][:],
                 in_=x_scales[:].indirect(offs_t[:, h * CHUNK // LIST:(h + 1) * CHUNK // LIST]),
             )
-            for a in range(1, PASSES):
-                c0 = (a - 1) * S + h * CHUNK
-                shift = SCALE_ROWS * a
-                nc.sync.dma_start(lifted[0:SHIFTED, c0:c0 + CHUNK].bitcast(I32), packed[h][shift:shift + SHIFTED, :].bitcast(I32))
+            for a in range(LAST):
+                c0 = a * S + h * CHUNK
+                nc.sync.dma_start(lifted[0:SHIFTED, c0:c0 + CHUNK].bitcast(I32), packed[h][SHIFT[a]:SHIFT[a] + SHIFTED, :].bitcast(I32))
 
         def plane(a, s0, s1):
-            if a == 0:
+            if a == LAST:
                 return packed[s0 // CHUNK][:, s0 % CHUNK:s0 % CHUNK + s1 - s0]
-            return lifted[:, (a - 1) * S + s0:(a - 1) * S + s1]
+            return lifted[:, a * S + s0:a * S + s1]
 
         load_rest()
         gather_body(0, 0, CHUNK, WIDE)
@@ -281,13 +285,14 @@ def tile_moe_tk_lin_gelu_kernel(tc, xT, w_words, w_scales, b, gate, offs, pos1, 
             nc.vector.tensor_tensor(result[:, t0:t1], others, prod0[:, t0:t1], ADD)
             nc.sync.dma_start(out[:, t0:t1], result[:, t0:t1])
 
-        def look_up(r, i0, i1, tag):
-            plain = keep.tile([P, (i1 - i0) * P], F32, name="plain", tag=tag)
+        def look_up(r, i0, i1, column, per_bank):
+            plain = plains.tile([P, (i1 - i0) * P], F32, name="plain%d_%d" % (r, i0), offset=4 * column)
             nc.scalar.activation(out=plain[:], in_=picked(r, lent(i0), lent(i1)), func=AF.Copy)
-            bank = psum.tile([P, (i1 - i0) * P], F32, name="bank")
-            for i in range(i0, i1):
-                nc.tensor.transpose(bank[:, blk(i - i0)], plain[:, blk(i - i0)], ident[:])
-                turned[(r, i)] = bank[:, blk(i - i0)]
+            for j0 in range(i0, i1, per_bank):
+                bank = psum.tile([P, per_bank * P], F32, name="bank")
+                for i in range(j0, j0 + per_bank):
+                    nc.tensor.transpose(bank[:, blk(i - j0)], plain[:, blk(i - i0)], ident[:])
+                    turned[(r, i)] = bank[:, blk(i - j0)]
 
         def scale_and_add(r, i0, i1):
             if r == 1:
@@ -302,13 +307,13 @@ def tile_moe_tk_lin_gelu_kernel(tc, xT, w_words, w_scales, b, gate, offs, pos1, 
                 )
 
         early, final = 2, LENT_BLOCKS - 1
-        look_up(1, 0, early, "plain_a")
-        look_up(2, 0, early, "plain_b")
-        look_up(1, early, LENT_BLOCKS, "plain_c")
+        look_up(1, 0, early, 3 * P, early)
+        look_up(2, 0, early, 0, early)
+        look_up(1, early, LENT_BLOCKS, 5 * P, LENT_BLOCKS - early)
         for r in (1, 2):
             scale_and_add(r, 0, early)
-        look_up(2, early, final, "plain_b")
-        look_up(2, final, LENT_BLOCKS, "plain_c")
+        look_up(2, early, final, P, 1)
+        look_up(2, final, LENT_BLOCKS, 0, 1)
         for r in (1, 2):
             for i in range(early, final):
                 scale_and_add(r, i, i + 1)
@@ -319,9 +324,8 @@ def tile_moe_tk_lin_gelu_kernel(tc, xT, w_words, w_scales, b, gate, offs, pos1, 
             nc.vector.tensor_tensor(prod[r][:], picked(r, 0, OWN), gates[:, (r - 1) * OWN:r * OWN], MULT)
         product0(0, OWN)
         nc.vector.tensor_tensor(pair[:], prod[1][:], prod[2][:], ADD)
-        product0(OWN, lent(early))
+        product0(OWN, lent(final))
         finish(0, OWN, pair[:])
-        product0(lent(early), lent(final))
         finish(OWN, lent(early), sums[0][:])
         prod_last = keep.tile([P, P], F32, name="prod_last", tag="scaled2_%d" % (early - 1))
         nc.vector.tensor_tensor(prod_last[:], picked(0, lent(final), T), gates[:, 2 * OWN + lent(final):], MULT)

@@ -258,7 +258,8 @@ def tile_moe_tk_lin_gelu_kernel(tc, xT, w_words, w_scales, b, gate, offs, pos1, 
                     close(span)
 
         gates = keep.tile([P, 2 * OWN + T], F32, name="gates", tag="packed0", align_bytes=64)
-        nc.sync.dma_start(gates[:, 0:2 * OWN].rearrange("p (r t) -> p r t", r=2), gate[1:TOP, :, 0:OWN].rearrange("r p t -> p r t"))
+        for r in (1, 2):
+            nc.sync.dma_start(gates[:, (r - 1) * OWN:r * OWN], gate[r, :, 0:OWN])
         nc.sync.dma_start(gates[:, 2 * OWN:], gate[0])
 
         def picked(r, t0, t1):
@@ -315,8 +316,7 @@ def tile_moe_tk_lin_gelu_kernel(tc, xT, w_words, w_scales, b, gate, offs, pos1, 
         look_up(2, early, final, P, 1)
         look_up(2, final, LENT_BLOCKS, 0, 1)
         for r in (1, 2):
-            for i in range(early, final):
-                scale_and_add(r, i, i + 1)
+            scale_and_add(r, early, final)
         for r in (1, 2):
             scale_and_add(r, final, LENT_BLOCKS)
 
@@ -329,7 +329,6 @@ def tile_moe_tk_lin_gelu_kernel(tc, xT, w_words, w_scales, b, gate, offs, pos1, 
         finish(OWN, lent(early), sums[0][:])
         prod_last = keep.tile([P, P], F32, name="prod_last", tag="scaled2_%d" % (early - 1))
         nc.vector.tensor_tensor(prod_last[:], picked(0, lent(final), T), gates[:, 2 * OWN + lent(final):], MULT)
-        for i in range(early, final):
-            finish(lent(i), lent(i + 1), sums[i][:])
+        finish(lent(early), lent(final), sums[early][:])
         nc.vector.tensor_tensor(result[:, lent(final):], sums[final][:], prod_last[:], ADD)
         nc.sync.dma_start(out[:, lent(final):], result[:, lent(final):])

@@ -38,13 +38,13 @@ HALF = T // 2
 QUARTER = T // 4
 COPY = {1: QUARTER, 2: 64, 3: 64}
 ZERO = 80
-LATE = {0: 128, 1: 1024, 2: 128, 3: 128}
-BODY = {a: S - n for a, n in LATE.items()}
+BEHIND = {1: (S - P, S), 2: (2048, S), 3: (0, CHUNK)}
 HEAD = ((0, 384), (384, 640), (640, 896), (896, T))
 SHIFT = {0: 4, 1: 8, 2: 12, 3: 0}
 HEAD_ON_VECTOR = (256, 128, 144, 72)
 DMA_ALIGN = 256
-LATER = tuple((c0, c0 + QUARTER) for c0 in range(0, T, QUARTER))
+QUARTERS = tuple((c0, c0 + QUARTER) for c0 in range(0, T, QUARTER))
+LATER = {1: QUARTERS, 2: QUARTERS, 3: QUARTERS[:-1] + ((T - QUARTER, T - P), (T - P, T))}
 CUTS = (0, 1536, 2048, 2560, 2816, 2944, S)
 W_LOAD = 6
 OWN = 384
@@ -68,8 +68,7 @@ def tile_moe_tk_lin_gelu_kernel(tc, xT, w_words, w_scales, b, gate, offs, pos1, 
         x_scales = keep.tile([P, WIDE], U8, name="x_scales", align_bytes=64)
         codes = keep.tile([P, LAST * T + WIDE], I32, name="codes", align_bytes=64)
         first_word = {2: 0, 1: T, 0: 2 * T, 3: 3 * T}
-        slot_codes = [keep.tile([P, BODY[a]], U32, name="slot_codes%d" % a, align_bytes=64) for a in range(PASSES)]
-        late_codes = {}
+        slot_codes = {a: [] for a in range(PASSES)}
         packed = [keep.tile([P, CHUNK], U8, name="packed%d" % h, align_bytes=64) for h in range(CHUNKS)]
         w_codes = keep.tile([P, E * PASSES, 2 * N], U8, name="w_codes", align_bytes=DMA_ALIGN)
         b_t = keep.tile([P, E], F32, name="b_t")
@@ -100,7 +99,7 @@ def tile_moe_tk_lin_gelu_kernel(tc, xT, w_words, w_scales, b, gate, offs, pos1, 
         load_pass(0, HEAD)
         nc.sync.dma_start(offs_t[:], offs)
         for a in range(1, PASSES):
-            load_pass(a, LATER)
+            load_pass(a, LATER[a])
 
         def lay_out(copy, grouped, raw):
             copy(out=grouped.rearrange("p (c i) j -> p c j i", i=2), in_=raw.rearrange("p j (c i) -> p c j i", i=2))
@@ -112,23 +111,25 @@ def tile_moe_tk_lin_gelu_kernel(tc, xT, w_words, w_scales, b, gate, offs, pos1, 
                 in_=grouped.rearrange("p w j -> p (w j)"),
             )
 
-        def gather_codes(a, dst, s0, n, window):
+        def gather_codes(a, s0, s1, window, behind=None):
+            if behind is None:
+                dst = keep.tile([P, s1 - s0], U32, name="slots%d_%d" % (a, s0), align_bytes=64)
+            else:
+                dst = raws.tile([P, s1 - s0], U32, name="slots%d_%d" % (a, s0), tag="raw%d_%d" % behind, align_bytes=DMA_ALIGN)
+            slot_codes[a].append((s0, s1, dst))
             words = codes[:, first_word[a]:first_word[a] + window].bitcast(U32)
-            nc.vector.tensor_copy(out=dst, in_=words.indirect(offs_t[:, s0 // LIST:(s0 + n) // LIST]))
-
-        def gather_body(a, s0, s1, window):
-            gather_codes(a, slot_codes[a][:, s0:s1], s0, s1 - s0, window)
+            nc.vector.tensor_copy(out=dst[:], in_=words.indirect(offs_t[:, s0 // LIST:s1 // LIST]))
 
         def quantize_pass(a):
             call = HALF if SHIFT[a] else T
             parts = [stage.tile([P, call, PACK], BF16, name="part%d_%d" % (a, h), align_bytes=64) for h in range(T // call)]
             for t0 in range(0, T, COPY[a]):
-                c0 = t0 - t0 % QUARTER
+                c0 = max(lo for lo, hi in LATER[a] if lo <= t0)
                 lay_out(nc.scalar.copy, parts[t0 // call][:, t0 % call:t0 % call + COPY[a], :], pieces[(a, c0)][:, :, t0 - c0:t0 - c0 + COPY[a]])
             for h, part in enumerate(parts):
                 quantize(a, h * call, (h + 1) * call, part[:])
-            late_codes[a - 1] = raws.tile([P, LATE[a - 1]], U32, name="late%d" % (a - 1), tag="raw%d_%d" % (a, T - QUARTER), align_bytes=DMA_ALIGN)
-            gather_codes(a - 1, late_codes[a - 1][:], BODY[a - 1], LATE[a - 1], T if LATE[a - 1] < T else WIDE)
+            s0, s1 = BEHIND[a]
+            gather_codes(a - 1, s0, s1, T if s1 - s0 < T else WIDE, behind=(a, LATER[a][-1][0]))
 
         groups = {lo: stage.tile([P, hi - lo, PACK], BF16, name="head%d" % lo, align_bytes=64) for lo, hi in HEAD[:-1]}
         w_plane_bytes = E * PASSES * N
@@ -190,12 +191,11 @@ def tile_moe_tk_lin_gelu_kernel(tc, xT, w_words, w_scales, b, gate, offs, pos1, 
             return lifted[:, a * S + s0:a * S + s1]
 
         load_rest()
-        gather_body(0, 0, CHUNK, WIDE)
-        gather_body(0, CHUNK, BODY[0], WIDE)
+        gather_codes(0, 0, CHUNK, WIDE)
+        gather_codes(0, CHUNK, BEHIND[1][0], WIDE)
         quantize_pass(1)
-        gather_body(1, 0, BODY[1], 2 * WIDE)
+        gather_codes(1, 0, BEHIND[2][0], 2 * WIDE)
         quantize_pass(2)
-        gather_body(2, 0, CHUNK, WIDE)
         quantize_pass(3)
         for h in range(CHUNKS):
             gather_and_move_scales(h)
@@ -217,7 +217,7 @@ def tile_moe_tk_lin_gelu_kernel(tc, xT, w_words, w_scales, b, gate, offs, pos1, 
         def multiply(span, a):
             lo, hi = span
             for s0, s1, e in by_expert(span):
-                words = late_codes[a][:, s0 - BODY[a]:s1 - BODY[a]] if s0 >= BODY[a] else slot_codes[a][:, s0:s1]
+                words = [tile[:, s0 - first:s1 - first] for first, end, tile in slot_codes[a] if first <= s0 < end][0]
                 nc.tensor.matmul_mx(
                     out=acc[span][:, s0 - lo:s1 - lo],
                     lhsT=w_codes[:, e * PASSES + a, :].bitcast(FP4X4),
@@ -236,10 +236,9 @@ def tile_moe_tk_lin_gelu_kernel(tc, xT, w_words, w_scales, b, gate, offs, pos1, 
                     func=AF.Gelu_apprx_tanh, bias=b_t[:, e:e + 1],
                 )
 
-        late_codes[LAST] = keep.tile([P, LATE[LAST]], U32, name="late3", align_bytes=64)
         for lo, hi in zip(CUTS, CUTS[1:]):
             if lo == CHUNK:
-                gather_body(2, CHUNK, BODY[2], 2 * WIDE)
+                gather_codes(2, CHUNK, S, 2 * WIDE)
             if lo % CHUNK == 0:
                 for a in range(LAST):
                     for span in spans:
@@ -249,17 +248,13 @@ def tile_moe_tk_lin_gelu_kernel(tc, xT, w_words, w_scales, b, gate, offs, pos1, 
                 for a in range(1, LAST):
                     for span in narrow:
                         multiply(span, a)
-            if lo == BODY[LAST]:
-                gather_codes(LAST, late_codes[LAST][:], lo, hi - lo, T)
-            else:
-                gather_body(LAST, lo, hi, T if hi - lo < T else WIDE)
+            gather_codes(LAST, lo, hi, T if hi - lo < T else WIDE)
             for span in spans:
                 if lo <= span[0] < hi:
                     close(span)
 
         gates = keep.tile([P, 2 * OWN + T], F32, name="gates", tag="packed0", align_bytes=64)
-        for r in (1, 2):
-            nc.sync.dma_start(gates[:, (r - 1) * OWN:r * OWN], gate[r, :, 0:OWN])
+        nc.sync.dma_start(gates[:, 0:2 * OWN].rearrange("p (r t) -> p r t", r=2), gate[1:TOP, :, 0:OWN].rearrange("r p t -> p r t"))
         nc.sync.dma_start(gates[:, 2 * OWN:], gate[0])
 
         def picked(r, t0, t1):

@@ -39,9 +39,9 @@ QUARTER = T // 4
 COPY = {1: QUARTER, 2: 64, 3: 64}
 ZERO = 80
 BEHIND = {1: (S - P, S), 2: (2048, S), 3: (0, CHUNK)}
-HEAD = ((0, 384), (384, 640), (640, 896), (896, T))
+HEAD = ((0, 512), (512, 640), (640, 896), (896, T))
 SHIFT = {0: 4, 1: 8, 2: 12, 3: 0}
-HEAD_ON_VECTOR = (256, 128, 144, 72)
+HEAD_ON_VECTOR = (256, 64, 144, 72)
 DMA_ALIGN = 256
 QUARTERS = tuple((c0, c0 + QUARTER) for c0 in range(0, T, QUARTER))
 LATER = {1: QUARTERS, 2: QUARTERS, 3: QUARTERS[:-1] + ((T - QUARTER, T - P), (T - P, T))}
@@ -143,9 +143,8 @@ def tile_moe_tk_lin_gelu_kernel(tc, xT, w_words, w_scales, b, gate, offs, pos1, 
 
         for i, (lo, hi) in enumerate(HEAD[:-2]):
             lay_out_piece(i)
-            n = HEAD_ON_VECTOR[i]
-            quantize(0, lo, lo + n, groups[lo][:, 0:n, :])
-            quantize(0, lo + n, hi, groups[lo][:, n:, :])
+            for t0 in range(lo, hi, QUARTER):
+                quantize(0, t0, min(t0 + QUARTER, hi), groups[lo][:, t0 - lo:min(t0 + QUARTER, hi) - lo, :])
         lay_out_piece(len(HEAD) - 2)
         lay_out_piece(len(HEAD) - 1)
         for lo, hi in HEAD[-2:]:

from contextlib import ExitStack

import concourse.mybir as mybir
from concourse.masks import make_identity

K, T, E, C, N = 2048, 1024, 12, 256, 128
TOP = 3
S = E * C
P = 128
PACK = 4
K_PASS = P * PACK
PASSES = K // K_PASS
LAST = PASSES - 1
FLOPS = 2 * K * N * S

F32 = mybir.dt.float32
BF16 = mybir.dt.bfloat16
I32 = mybir.dt.int32
U32 = mybir.dt.uint32
U16 = mybir.dt.uint16
U8 = mybir.dt.uint8
FP8X4 = mybir.dt.float8_e4m3fn_x4
FP4X4 = mybir.dt.float4_e2m1fn_x4
AF = mybir.ActivationFunctionType
MULT = mybir.AluOpType.mult
ADD = mybir.AluOpType.add

LIST = 16
QUADRANT = 32
SCALE_ROWS = 4
BANK = 512
BANKS = 8
CHUNK = S // 2
CHUNKS = S // CHUNK
WIDE = 2 * T
SHIFTED = 112
HALF = T // 2
QUARTER = T // 4
COPY = {1: QUARTER, 2: 64, 3: 64}
ZERO = 80
BEHIND = {1: (S - P, S), 2: (2048, S), 3: (0, CHUNK)}
HEAD = ((0, 512), (512, 640), (640, 896), (896, T))
SHIFT = {0: 4, 1: 8, 2: 12, 3: 0}
HEAD_ON_VECTOR = (256, 64, 144, 72)
DMA_ALIGN = 256
QUARTERS = tuple((c0, c0 + QUARTER) for c0 in range(0, T, QUARTER))
LATER = {1: QUARTERS, 2: QUARTERS, 3: QUARTERS[:-1] + ((T - QUARTER, T - P), (T - P, T))}
CUTS = (0, 1536, 2048, 2560, 2816, 2944, S)
W_LOAD = 6
OWN = 384
LENT = T - OWN
LENT_BLOCKS = LENT // P


def tile_moe_tk_lin_gelu_kernel(tc, xT, w_words, w_scales, b, gate, offs, pos1, pos2, pos3, out):
    nc = tc.nc
    with ExitStack() as ctx:
        lists = ctx.enter_context(tc.tile_pool(name="lists", bufs=1))
        keep = ctx.enter_context(tc.tile_pool(name="keep", bufs=1))
        raws = ctx.enter_context(tc.tile_pool(name="raws", bufs=1))
        stage = ctx.enter_context(tc.tile_pool(name="stage", bufs=1))
        lap = ctx.enter_context(tc.tile_pool(name="lap", bufs=1))
        plains = ctx.enter_context(tc.tile_pool(name="plains", bufs=1))
        psum = ctx.enter_context(tc.psum_pool(name="psum", bufs=BANKS))

        offs_t = lists.tile([P, S // LIST], U16, name="offs_t")
        pos_t = [lists.tile([P, T // LIST], U16, name="pos%d_t" % r) for r in range(TOP)]
        x_scales = keep.tile([P, WIDE], U8, name="x_scales", align_bytes=64)
        codes = keep.tile([P, LAST * T + WIDE], I32, name="codes", align_bytes=64)
        first_word = {2: 0, 1: T, 0: 2 * T, 3: 3 * T}
        slot_codes = {a: [] for a in range(PASSES)}
        packed = [keep.tile([P, CHUNK], U8, name="packed%d" % h, align_bytes=64) for h in range(CHUNKS)]
        w_codes = keep.tile([P, E * PASSES, 2 * N], U8, name="w_codes", align_bytes=DMA_ALIGN)
        b_t = keep.tile([P, E], F32, name="b_t")
        y = keep.tile([P, S], F32, name="y")
        warm = keep.tile([P, 1], F32, name="warm")
        warm_out = keep.tile([P, 1], F32, name="warm_out")

        nc.gpsimd.memset(warm[:], 0.0)
        nc.scalar.activation(out=warm_out[:], in_=warm[:], func=AF.Gelu_apprx_tanh)
        ident = keep.tile([P, P], F32, name="ident")
        make_identity(nc, ident[:])
        for words in (x_scales[:].bitcast(I32), codes[:, first_word[LAST]:]):
            for c0 in range(0, words.shape[1], ZERO):
                nc.vector.memset(words[:, c0:min(c0 + ZERO, words.shape[1])], 0)

        gate_rows = keep.tile([P, P], F32, name="gate_rows")
        gate_cols = keep.tile([P, 2 * LENT_BLOCKS], F32, name="gate_cols")
        nc.gpsimd.memset(gate_rows[:], 0.0)
        pieces = {}

        def load_pass(a, ranges):
            for c0, c1 in ranges:
                raw = raws.tile([P, PACK, c1 - c0], F32, name="raw%d_%d" % (a, c0), align_bytes=DMA_ALIGN)
                rows = xT[a * K_PASS:(a + 1) * K_PASS, c0:c1]
                nc.sync.dma_start(raw[:], rows.rearrange("(p j) w -> p j w", j=PACK))
                pieces[(a, c0)] = raw

        load_pass(0, HEAD)
        nc.sync.dma_start(offs_t[:], offs)
        for a in range(1, PASSES):
            load_pass(a, LATER[a])

        def lay_out(copy, grouped, raw):
            copy(out=grouped.rearrange("p (c i) j -> p c j i", i=2), in_=raw.rearrange("p j (c i) -> p c j i", i=2))

        def quantize(a, lo, hi, grouped):
            nc.vector.quantize_mx(
                out=codes[:, first_word[a] + lo:first_word[a] + hi].bitcast(FP8X4),
                scales=x_scales[SHIFT[a]:P, lo:hi],
                in_=grouped.rearrange("p w j -> p (w j)"),
            )

        def gather_codes(a, s0, s1, window, behind=None):
            if behind is None:
                dst = keep.tile([P, s1 - s0], U32, name="slots%d_%d" % (a, s0), align_bytes=64)
            else:
                dst = raws.tile([P, s1 - s0], U32, name="slots%d_%d" % (a, s0), tag="raw%d_%d" % behind, align_bytes=DMA_ALIGN)
            slot_codes[a].append((s0, s1, dst))
            words = codes[:, first_word[a]:first_word[a] + window].bitcast(U32)
            nc.vector.tensor_copy(out=dst[:], in_=words.indirect(offs_t[:, s0 // LIST:s1 // LIST]))

        def quantize_pass(a):
            call = HALF if SHIFT[a] else T
            parts = [stage.tile([P, call, PACK], BF16, name="part%d_%d" % (a, h), align_bytes=64) for h in range(T // call)]
            for t0 in range(0, T, COPY[a]):
                c0 = max(lo for lo, hi in LATER[a] if lo <= t0)
                lay_out(nc.scalar.copy, parts[t0 // call][:, t0 % call:t0 % call + COPY[a], :], pieces[(a, c0)][:, :, t0 - c0:t0 - c0 + COPY[a]])
            for h, part in enumerate(parts):
                quantize(a, h * call, (h + 1) * call, part[:])
            s0, s1 = BEHIND[a]
            gather_codes(a - 1, s0, s1, T if s1 - s0 < T else WIDE, behind=(a, LATER[a][-1][0]))

        groups = {lo: stage.tile([P, hi - lo, PACK], BF16, name="head%d" % lo, align_bytes=64) for lo, hi in HEAD[:-1]}
        w_plane_bytes = E * PASSES * N
        last_lo = HEAD[-1][0]
        groups[last_lo] = lap.tile([P, T - last_lo, PACK], BF16, name="head_last", align_bytes=64, offset=w_plane_bytes - (T - last_lo) * PACK)

        def lay_out_piece(i):
            (lo, hi), n = HEAD[i], HEAD_ON_VECTOR[i]
            lay_out(nc.vector.tensor_copy, groups[lo][:, 0:n, :], pieces[(0, lo)][:, :, 0:n])
            lay_out(nc.scalar.copy, groups[lo][:, n:, :], pieces[(0, lo)][:, :, n:])

        for i, (lo, hi) in enumerate(HEAD[:-2]):
            lay_out_piece(i)
            for t0 in range(lo, hi, QUARTER):
                quantize(0, t0, min(t0 + QUARTER, hi), groups[lo][:, t0 - lo:min(t0 + QUARTER, hi) - lo, :])
        lay_out_piece(len(HEAD) - 2)
        lay_out_piece(len(HEAD) - 1)
        for lo, hi in HEAD[-2:]:
            quantize(0, lo, hi, groups[lo][:])

        w_planes = lap.tile([P, E * PASSES, N], U8, name="w_planes", align_bytes=64, offset=0)
        lifted = lap.tile([P, LAST * S], U8, name="lifted", align_bytes=64, offset=w_plane_bytes)
        nc.gpsimd.memset(w_planes[:].rearrange("p g n -> p (g n)").bitcast(I32), 0)
        nc.gpsimd.memset(lifted[:].bitcast(I32), 0)

        def load_rest():
            for r in range(SCALE_ROWS):
                nc.sync.dma_start(
                    w_planes[r:P:QUADRANT, :, :].bitcast(I32),
                    w_scales.rearrange("e a (q r) n -> r q (e a) n", r=SCALE_ROWS)[r].bitcast(I32),
                )
            for g0 in range(0, E * PASSES, W_LOAD):
                nc.sync.dma_start(
                    w_codes[:, g0:g0 + W_LOAD, :].bitcast(I32),
                    w_words.rearrange("e a p n -> p (e a) n")[:, g0:g0 + W_LOAD, :].bitcast(I32),
                )
            nc.sync.dma_start(b_t[:], b)
            for r in (1, 2):
                nc.sync.dma_start(
                    gate_rows[(r - 1) * LENT_BLOCKS:r * LENT_BLOCKS, :],
                    gate[r, 0, OWN:].rearrange("(i p) -> i p", p=P),
                )
            for r, pos in enumerate((pos1, pos2, pos3)):
                nc.sync.dma_start(pos_t[r][:], pos)

        def gather_and_move_scales(h):
            nc.vector.tensor_copy(
                out=packed[h][:],
                in_=x_scales[:].indirect(offs_t[:, h * CHUNK // LIST:(h + 1) * CHUNK // LIST]),
            )
            for a in range(LAST):
                c0 = a * S + h * CHUNK
                nc.sync.dma_start(lifted[0:SHIFTED, c0:c0 + CHUNK].bitcast(I32), packed[h][SHIFT[a]:SHIFT[a] + SHIFTED, :].bitcast(I32))

        def plane(a, s0, s1):
            if a == LAST:
                return packed[s0 // CHUNK][:, s0 % CHUNK:s0 % CHUNK + s1 - s0]
            return lifted[:, a * S + s0:a * S + s1]

        load_rest()
        gather_codes(0, 0, CHUNK, WIDE)
        gather_codes(0, CHUNK, BEHIND[1][0], WIDE)
        quantize_pass(1)
        gather_codes(1, 0, BEHIND[2][0], 2 * WIDE)
        quantize_pass(2)
        quantize_pass(3)
        for h in range(CHUNKS):
            gather_and_move_scales(h)

        turned_rows = psum.tile([P, P], F32, name="bank")
        nc.tensor.transpose(turned_rows[:], gate_rows[:], ident[:])
        for col in range(2 * LENT_BLOCKS):
            nc.scalar.copy(out=gate_cols[:, col:col + 1], in_=turned_rows[:, col:col + 1])

        spans = [(s0, min(s0 + BANK, hi)) for lo, hi in zip(CUTS, CUTS[1:]) for s0 in range(lo, hi, BANK)]
        acc = {span: psum.tile([P, span[1] - span[0]], F32, name="bank") for span in spans}
        narrow = spans[-3:]
        before_narrow = spans[-4]

        def by_expert(span):
            edges = sorted({span[0], span[1]} | {s0 for s0 in range(0, S, C) if span[0] < s0 < span[1]})
            return [(s0, s1, s0 // C) for s0, s1 in zip(edges, edges[1:])]

        def multiply(span, a):
            lo, hi = span
            for s0, s1, e in by_expert(span):
                words = [tile[:, s0 - first:s1 - first] for first, end, tile in slot_codes[a] if first <= s0 < end][0]
                nc.tensor.matmul_mx(
                    out=acc[span][:, s0 - lo:s1 - lo],
                    lhsT=w_codes[:, e * PASSES + a, :].bitcast(FP4X4),
                    lhsT_scale=w_planes[:, e * PASSES + a, :],
                    rhs=words.bitcast(FP8X4),
                    rhs_scale=plane(a, s0, s1),
                    start=(a == 0 and s0 == lo),
                    stop=(a == LAST and s1 == hi),
                )

        def close(span):
            multiply(span, LAST)
            for s0, s1, e in by_expert(span):
                nc.scalar.activation(
                    out=y[:, s0:s1], in_=acc[span][:, s0 - span[0]:s1 - span[0]],
                    func=AF.Gelu_apprx_tanh, bias=b_t[:, e:e + 1],
                )

        for lo, hi in zip(CUTS, CUTS[1:]):
            if lo == CHUNK:
                gather_codes(2, CHUNK, S, 2 * WIDE)
            if lo % CHUNK == 0:
                for a in range(LAST):
                    for span in spans:
                        if lo <= span[0] < lo + CHUNK and (a == 0 or span not in narrow):
                            multiply(span, a)
            if (lo, hi) == before_narrow:
                for a in range(1, LAST):
                    for span in narrow:
                        multiply(span, a)
            gather_codes(LAST, lo, hi, T if hi - lo < T else WIDE)
            for span in spans:
                if lo <= span[0] < hi:
                    close(span)

        gates = keep.tile([P, 2 * OWN + T], F32, name="gates", tag="packed0", align_bytes=64)
        nc.sync.dma_start(gates[:, 0:2 * OWN].rearrange("p (r t) -> p r t", r=2), gate[1:TOP, :, 0:OWN].rearrange("r p t -> p r t"))
        nc.sync.dma_start(gates[:, 2 * OWN:], gate[0])

        def picked(r, t0, t1):
            return y[:].indirect(pos_t[r][:, t0 // LIST:t1 // LIST])

        def blk(i):
            return slice(i * P, (i + 1) * P)

        def lent(i):
            return OWN + i * P

        scaled = {(r, i): keep.tile([P, P], F32, name="scaled%d_%d" % (r, i)) for r in (1, 2) for i in range(LENT_BLOCKS)}
        prod = {r: keep.tile([P, OWN], F32, name="prod%d" % r) for r in (1, 2)}
        pair = keep.tile([P, OWN], F32, name="pair")
        prod0 = keep.tile([P, T - P], F32, name="prod0")
        result = raws.tile([P, T], F32, name="result", tag="raw0_0", align_bytes=DMA_ALIGN)
        turned = {}
        sums = {}

        def product0(t0, t1):
            nc.vector.tensor_tensor(prod0[:, t0:t1], picked(0, t0, t1), gates[:, 2 * OWN + t0:2 * OWN + t1], MULT)

        def finish(t0, t1, others):
            nc.vector.tensor_tensor(result[:, t0:t1], others, prod0[:, t0:t1], ADD)
            nc.sync.dma_start(out[:, t0:t1], result[:, t0:t1])

        def look_up(r, i0, i1, column, per_bank):
            plain = plains.tile([P, (i1 - i0) * P], F32, name="plain%d_%d" % (r, i0), offset=4 * column)
            nc.scalar.activation(out=plain[:], in_=picked(r, lent(i0), lent(i1)), func=AF.Copy)
            for j0 in range(i0, i1, per_bank):
                bank = psum.tile([P, per_bank * P], F32, name="bank")
                for i in range(j0, j0 + per_bank):
                    nc.tensor.transpose(bank[:, blk(i - j0)], plain[:, blk(i - i0)], ident[:])
                    turned[(r, i)] = bank[:, blk(i - j0)]

        def scale_and_add(r, i0, i1):
            if r == 1:
                sums[i0] = psum.tile([P, (i1 - i0) * P], F32, name="bank")
            for i in range(i0, i1):
                col = (r - 1) * LENT_BLOCKS + i
                nc.scalar.activation(out=scaled[(r, i)][:], in_=turned[(r, i)], func=AF.Copy, scale=gate_cols[:, col:col + 1])
            for i in range(i0, i1):
                nc.tensor.matmul(
                    sums[i0][:, blk(i - i0)], lhsT=scaled[(r, i)][:], rhs=ident[:], is_transpose=True,
                    start=(r == 1 and i == i0), stop=(r == 2 and i == i1 - 1),
                )

        early, final = 2, LENT_BLOCKS - 1
        look_up(1, 0, early, 3 * P, early)
        look_up(2, 0, early, 0, early)
        look_up(1, early, LENT_BLOCKS, 5 * P, LENT_BLOCKS - early)
        for r in (1, 2):
            scale_and_add(r, 0, early)
        look_up(2, early, final, P, 1)
        look_up(2, final, LENT_BLOCKS, 0, 1)
        for r in (1, 2):
            scale_and_add(r, early, final)
        for r in (1, 2):
            scale_and_add(r, final, LENT_BLOCKS)

        for r in (1, 2):
            nc.vector.tensor_tensor(prod[r][:], picked(r, 0, OWN), gates[:, (r - 1) * OWN:r * OWN], MULT)
        product0(0, OWN)
        nc.vector.tensor_tensor(pair[:], prod[1][:], prod[2][:], ADD)
        product0(OWN, lent(final))
        finish(0, OWN, pair[:])
        finish(OWN, lent(early), sums[0][:])
        prod_last = keep.tile([P, P], F32, name="prod_last", tag="scaled2_%d" % (early - 1))
        nc.vector.tensor_tensor(prod_last[:], picked(0, lent(final), T), gates[:, 2 * OWN + lent(final):], MULT)
        finish(lent(early), lent(final), sums[early][:])
        nc.vector.tensor_tensor(result[:, lent(final):], sums[final][:], prod_last[:], ADD)
        nc.sync.dma_start(out[:, lent(final):], result[:, lent(final):])
